import numpy as np, ml_dtypes
CORES = [10,34,74,98]
N = 4
import mx_ref
BF = ml_dtypes.bfloat16
def pick(q, e):
    c = np.concatenate([q[0].reshape(128, -1, 4), np.zeros((128, 1, 4), np.uint8)], axis=1); s = np.concatenate([q[1], np.ones((16, 1), np.uint8)], axis=1)
    return (np.ascontiguousarray(c[:, e].reshape(128, -1)), np.ascontiguousarray(s[:, e]))
def join(*qs):
    return (np.concatenate([q[0] for q in qs], axis=1), np.concatenate([q[1] for q in qs], axis=1))
def put(q, e, v):
    c, s = q[0].reshape(128, -1, 4).copy(), q[1].copy(); c[:, e] = v[0].reshape(128, -1, 4); s[:, e] = v[1]
    return (c.reshape(128, -1), s)
def pk(c, s):
    return (np.ascontiguousarray(c), mx_ref.live(s))
def emit(q):
    return q[0], q[1]
def cols(t, e):
    v = np.concatenate([t.reshape(128, -1, 4), np.zeros((128, 1, 4), BF)], axis=1)
    return np.ascontiguousarray(v[:, e]).reshape(128, -1)
def tile(rs):
    return np.stack(rs, axis=2).reshape(128, -1).astype(BF)
def cut(t, i, w=512):
    return t[:, w * i:w * i + w]
def f(rng, *shape):
    return mx_ref.flush((rng.standard_normal(shape, dtype=np.float32) * np.exp2(rng.integers(-2, 3, shape[:-1] + (1,)))).astype(BF))
def wide(rng, *shape, cols=0):
    v = rng.standard_normal(shape, dtype=np.float32) * np.exp2(rng.integers(-12, 13, shape)).astype(np.float32)
    if cols: v *= np.repeat(np.exp2(rng.integers(-cols, cols + 1, shape[:-2] + (1, shape[-1] // 4))) * (rng.random(shape[:-2] + (1, shape[-1] // 4)) > 0.0625), 4, axis=-1).astype(np.float32)
    return mx_ref.flush(v.astype(BF))
T, CAPP, CB, DF = 192, 80, 32, 80
LEVELS = np.array([0, 16, 32, 64], np.float32)
def taken(first, a):
    return np.concatenate([s * T + np.flatnonzero(first[s] == a)[:CAPP] for s in range(N)])
def plain(rng):
    rt, r2 = np.array(f(rng, 128, 512)), np.zeros((128, 512), BF)
    rt[:, 4 * N:] = 0
    v = f(rng, 128, 4 * N + 4).astype(np.float32).reshape(128, N + 1, 4)
    v = v - np.mean(v, axis=(0, 2), keepdims=True)
    r2[:, :4 * N + 4] = mx_ref.flush(v.reshape(128, -1).astype(BF))
    return {"x": np.array(f(rng, N, 128, 4 * T)), "rt": np.stack([rt] * N), "w": np.array(f(rng, N, 128, 2048)), "r2": np.stack([r2] * N), "vx": f(rng, N, 128, 512), "vh": f(rng, N, 128, 512)}
def planned(rng, A, B, V, dead=None, same=False):
    d = plain(rng)
    rt, r2, wt = d["rt"], d["r2"], d["w"].reshape(N, 128, 4, 128, 4)
    rt[:, 120:] = 0
    r2[:, :4 * N + 4] = 0
    wt[:, 120:] = 0
    for k in range(N + 1):
        r2[:, 4 * k:4 * k + 4, 4 * k:4 * k + 4] = 32
        wt[:, 120 + k // 4, :, 4 * k:4 * k + 4, k % 4] = 64
    k = N + 1
    wt[:, 120 + k // 4, :, :, k % 4] = -64
    if same:
        p = f(rng, 128, 4 * N)
        x = np.stack([cols(p, A[s]) for s in range(N)])
    else: x = f(rng, N, 128, 4 * T)
    x = np.array(x, np.float32).reshape(N, 128, T, 4)
    g = rt[0].astype(np.float32).reshape(128, 128, 4)
    for s in range(N): x[s] = x[s] + g[:, A[s]]
    x[:, 120:] = 0
    s, j = np.nonzero(B >= 0)
    b = B[s, j]
    x[s, 120 + b // 4, j, b % 4] = 64
    x[:, 120 + N // 4, :, N % 4] = LEVELS[V]
    if dead is not None: x[:, 120 + k // 4, :, k % 4] = np.where(dead, 256, 0)
    d["x"] = np.array(mx_ref.flush(x.reshape(N, 128, 4 * T).astype(BF)))
    return d
def choose(rng, A):
    B, V = (A + 1 + rng.integers(0, N - 1, A.shape)) % N, np.zeros((N, T), int)
    for a in range(N):
        k = taken(A, a)
        V.flat[k] = 3
        k = rng.permutation(k)[:DF]
        V.flat[k] = 0
        B.flat[k] = np.resize(rng.permutation([b for b in range(N) if b != a]), len(k))
    return B, V
def setup_inputs(rng):
    return plain(rng)
def setup_inputs_crowd(rng):
    h, A = int(rng.integers(1, N - 1)), []
    o = (int(rng.choice([i for i in range(1, N) if i not in (h, h + 1)])), h)
    for s in range(N):
        one, two, e = (s + o[0]) % N, (s + o[1]) % N, int(rng.integers(1, 9))
        rest = [a for a in range(N) if a not in (one, two, (two + 1) % N)]
        A.append(rng.permutation(np.concatenate([np.full(CAPP, one), np.full(CAPP + e, two), np.resize(rng.permutation(rest), T - 2 * CAPP - e)])))
    A = np.stack(A)
    B, V = choose(rng, A)
    for a in range(N):
        one, two, e = (a + o[0]) % N, (a + o[1]) % N, int(rng.integers(1, CB // 4 + 1))
        rest = [b for b in range(N) if b not in (a, one, two)]
        k = taken(A, a)
        k = rng.permutation(k[V.reshape(-1)[k] == 0])
        B.flat[k] = np.concatenate([np.full(CB, one), np.full(CB + e, two), np.resize(rng.permutation(rest), len(k) - 2 * CB - e)])
    return planned(rng, A, B, V)
def setup_inputs_few(rng):
    none, less, even, full = rng.permutation(N)[:4]
    act, n = [a for a in range(N) if a not in (none, less, even, full)] or [full], DF // (2 * N)
    fix = np.concatenate([np.full(n, less), np.full(2 * n, even), np.full(CAPP + 4, full)])
    A = np.stack([rng.permutation(np.concatenate([fix, np.resize(rng.permutation(act), T - len(fix))])) for s in range(N)])
    B, V = choose(rng, A)
    m = (A == less) | (A == even)
    V[m] = rng.integers(0, 4, int(np.count_nonzero(m)))
    k = taken(A, full)
    V.flat[k] = 3
    k = np.concatenate([k[-16::5], rng.permutation(k[:-16])[:DF - 4]])
    V.flat[k] = 0
    B.flat[k] = np.resize(rng.permutation([b for b in range(N) if b != full]), DF)
    d = planned(rng, A, B, V)
    p, t = 120 + (N + 2) // 4, (N + 2) % 4
    d["x"][:, p, t::4] = 64
    d["w"].reshape(N, 128, 4, 128, 4)[:, p, :, 4 * N + 4:4 * N + 8, t] = 64
    d["r2"][:, 4 * N + 4:4 * N + 8] = 0
    d["r2"][:, 4 * N + 4:4 * N + 8, :4 * N] = -64
    d["x"] = (d["x"].astype(np.float32) * np.float32(2.0 ** 21)).astype(BF)
    d["r2"] = (d["r2"].astype(np.float32) * np.float32(2.0 ** 24)).astype(BF)
    return d
def setup_inputs_ties(rng):
    lo, hi = np.sort(rng.permutation(N)[:2])
    k = int(rng.choice([i for i in range(N - 1) if i != hi]))
    act = [a for a in range(N) if a != hi]
    A = np.stack([rng.permutation(np.resize(rng.permutation(act), T)) for s in range(N)])
    B, V, c = np.zeros((N, T), int), np.full((N, T), 3), 3 * (DF // 6)
    for a in act:
        g = rng.permutation(taken(A, a))
        n = (len(g) - 2 * c) // 3
        B.flat[g] = (a + 1) % N
        V.flat[g[:c]] = 0
        B.flat[g[c:2 * c]] = (a + 2) % N
        V.flat[g[c:2 * c]] = 1
        B.flat[g[2 * c:2 * c + 3 * n]] = (a + 3 + np.repeat(np.arange(n), 3) % (N - 3)) % N
        V.flat[g[2 * c:2 * c + 3 * n]] = 2
    d = planned(rng, A, B, V, same=True)
    d["rt"][:, :, 4 * hi:4 * hi + 4] = d["rt"][:, :, 4 * lo:4 * lo + 4]
    d["r2"][:, 4 * k + 4:4 * k + 8, 4 * k:4 * k + 4] = 32
    d["r2"][:, :, 4 * k + 4:4 * k + 8] = d["r2"][:, :, 4 * k:4 * k + 4]
    return d
def setup_inputs_zero(rng):
    A = np.stack([rng.permutation(np.resize(np.arange(N), T)) for s in range(N)])
    B, V, dead = (A + 1 + rng.integers(0, N - 1, A.shape)) % N, np.full((N, T), 3), np.zeros((N, T), bool)
    for a in range(N):
        k = rng.permutation(taken(A, a))
        z = DF // 2 if a % 2 else DF + DF // 8
        dead.flat[k[:z]] = True
        B.flat[k[:z]] = -1
        V.flat[k[:z]] = 0
        g = k[z:DF]
        if len(g):
            V.flat[g] = 1
            B.flat[g] = np.resize(rng.permutation([b for b in range(N) if b != a]), len(g))
        if a == 0: blank = k[:z:2]
    d = planned(rng, A, B, V, dead=dead)
    nil = np.where(d["rt"][0, :, :4].astype(np.float32) < 0, np.float32(0.0), np.float32(-0.0)).astype(BF)
    for i in blank: d["x"][i // T, :, 4 * (i % T):4 * (i % T) + 4] = nil
    return d
def setup_inputs_spread(rng):
    return {**plain(rng), "x": wide(rng, N, 128, 4 * T, cols=4)}
def check_inputs(d):
    b = []
    for k in ("x", "rt", "w", "r2", "vx", "vh"):
        v = np.abs(d[k].astype(np.float32))
        if not (np.isfinite(v).all() and ((v == 0) | (v >= 2.0 ** -30) & (v <= 2.0 ** 30)).all()): b.append("a value of " + k)
    for k, n in (("rt", N), ("r2", N + 1)):
        v = d[k].astype(np.float32)
        if (v[:, :, 4 * n:] != 0).any(): b.append(k + " has numbers behind its first columns")
        if (v != v[:1]).any(): b.append(k + " differs between ranks")
    return b
def reference(x, rt, w, r2, vx, vh):
    q = [mx_ref.quantize(np.ascontiguousarray(x[s])) for s in range(N)]
    every = join(*q)
    first = np.stack([np.argmax(mx_ref.matmul(mx_ref.quantize(np.ascontiguousarray(rt[s])), q[s])[:N] + np.float32(0.0), axis=0) for s in range(N)])
    who, at, made = np.full((N, N * CB), -1), np.full((N, N * CB), -1), []
    for a in range(N):
        k = taken(first, a)
        t = pick(every, np.concatenate([k, np.full(N * CAPP - len(k), -1)]))
        z = [mx_ref.matmul(mx_ref.quantize(np.ascontiguousarray(cut(w[a], i))), t) for i in range(4)]
        h = mx_ref.quantize(np.ascontiguousarray(tile([np.maximum(v, np.float32(0.0)) * np.float32(0.0625) for v in z])))
        made.append(h)
        e = mx_ref.matmul(mx_ref.quantize(np.ascontiguousarray(r2[a])), h)[:N + 1, :len(k)] + np.float32(0.0)
        late = np.sort(np.argsort(e[N], kind="stable")[:DF])
        e[a] = -np.inf
        second = np.argmax(e[:N], axis=0)
        for b in range(N):
            m = late[second[late] == b][:CB]
            who[b, a * CB:a * CB + len(m)] = k[m]
            at[b, a * CB:a * CB + len(m)] = a * N * CAPP + m
    made = join(*made)
    y, oc, osc = np.zeros((N, 128, N * CB), np.float32), np.zeros((N, 128, 4 * N * CB), np.uint8), np.zeros((N, 16, N * CB), np.uint8)
    for b in range(N):
        t, h = pick(every, who[b]), pick(made, at[b])
        v = mx_ref.matmul(mx_ref.quantize(np.ascontiguousarray(vx[b])), t) + mx_ref.matmul(mx_ref.quantize(np.ascontiguousarray(vh[b])), h)
        y[b] = np.where(who[b] >= 0, v, np.float32(0.0))
        oc[b], osc[b] = emit(h)
    return {"y": y, "who": who.astype(np.float32).reshape(N, 1, N * CB), "oc": oc, "osc": osc}

@@ -1,0 +1,336 @@
+from concourse.bass import DstId, RemoteDMATransfer
+from concourse.mybir import dt, AluOpType as OP, AxisListType, ActivationFunctionType as AF
+
+N, TOK, CAP, CB, DF = 4, 192, 80, 32, 80
+NX = N * CAP
+NH = NX // 2
+XC = 336
+HB = 352
+EPS, BIG, LOW = 1e-30, 1e29, -9e29
+STEP = 2.0 ** -10
+RTB = [0, 1, 2, 3, 5, 4, 7, 6, 5, 4, 6, 7, 4, 5]
+RTS = [4, 6, 10]
+
+SCRATCH = {
+    "rtt": ("sbuf", [128, 512], "bfloat16"), "rtq": ("sbuf", [128, 128], "float8_e4m3fn_x4"), "rts": ("sbuf", [128, 128], "uint8"),
+    "rpq": ("sbuf", [128, 448], "float8_e4m3fn_x4"), "rps": ("sbuf", [128, 448], "uint8"), "rto": ("sbuf", [128, 28], "uint16"),
+    "xt": ("sbuf", [128, 776], "bfloat16"), "xq": ("sbuf", [128, 194], "float8_e4m3fn_x4"), "xs": ("sbuf", [128, 194], "uint8"),
+    "wt": ("sbuf", [128, 2048], "bfloat16"), "wq": ("sbuf", [128, 512], "float8_e4m3fn_x4"), "wsc": ("sbuf", [128, 512], "uint8"),
+    "r2t": ("sbuf", [128, 512], "bfloat16"), "r2q": ("sbuf", [128, 128], "float8_e4m3fn_x4"), "r2s": ("sbuf", [128, 128], "uint8"),
+    "r2p": ("sbuf", [128, 512], "float8_e4m3fn_x4"), "r2ps": ("sbuf", [128, 512], "uint8"), "r2o": ("sbuf", [128, 32], "uint16"),
+    "vxt": ("sbuf", [128, 512], "bfloat16"), "vxq": ("sbuf", [128, 128], "float8_e4m3fn_x4"), "vxs": ("sbuf", [128, 128], "uint8"),
+    "vht": ("sbuf", [128, 512], "bfloat16"), "vhq": ("sbuf", [128, 128], "float8_e4m3fn_x4"), "vhs": ("sbuf", [128, 128], "uint8"),
+    "hb": ("sbuf", [128, 4 * (NX + 2)], "bfloat16"),
+    "sl1": ("sbuf", [128, 240], "float8_e4m3fn_x4"), "ss1": ("sbuf", [128, 240], "uint8"),
+    "land1": ("sbuf", [128, XC], "float8_e4m3fn_x4"), "lans1": ("sbuf", [128, XC], "uint8"),
+    "msgo": ("sbuf", [128, 32], "bfloat16"), "msgi": ("sbuf", [128, 32], "bfloat16"),
+    "xw": ("sbuf", [128, 704], "float8_e4m3fn_x4"), "xws": ("sbuf", [128, 704], "uint8"),
+    "sl2": ("sbuf", [128, 192], "float8_e4m3fn_x4"), "ss2": ("sbuf", [128, 192], "uint8"),
+    "land2": ("sbuf", [128, 256], "float8_e4m3fn_x4"), "lans2": ("sbuf", [128, 256], "uint8"),
+    "fin": ("sbuf", [128, 128], "float8_e4m3fn_x4"), "fins": ("sbuf", [128, 128], "uint8"),
+    "lwho": ("sbuf", [128, 32], "float32"), "whot": ("sbuf", [128, 32], "float32"),
+    "z1": ("sbuf", [128, 192], "float32"), "z2": ("sbuf", [128, 192], "float32"), "z3": ("sbuf", [128, 192], "float32"),
+    "mk": ("sbuf", [128, 192], "bfloat16"), "cum": ("sbuf", [128, 192], "bfloat16"), "zb": ("sbuf", [128, 320], "bfloat16"), "zf": ("sbuf", [128, 32], "float32"),
+    "jka": ("sbuf", [128, 1152], "bfloat16"), "jkd": ("sbuf", [128, 512], "bfloat16"),
+    "cnt1": ("sbuf", [128, 8], "float32"), "cntm": ("sbuf", [128, 4], "float32"), "off1": ("sbuf", [128, 24], "uint16"), "ozero": ("sbuf", [128, 4], "uint16"),
+    "inv": ("sbuf", [128, 320], "float32"), "em": ("sbuf", [128, 320], "float32"), "emb": ("sbuf", [128, 320], "float32"),
+    "y1": ("sbuf", [128, 320], "float32"), "y2": ("sbuf", [128, 320], "float32"), "sn": ("sbuf", [128, 320], "float32"), "ns": ("sbuf", [128, 320], "float32"),
+    "gd": ("sbuf", [128, 320], "bfloat16"), "nq": ("sbuf", [128, 320], "bfloat16"), "sg": ("sbuf", [128, 320], "bfloat16"), "cap": ("sbuf", [128, 320], "bfloat16"),
+    "mk2": ("sbuf", [128, 320], "bfloat16"), "cum2": ("sbuf", [128, 320], "bfloat16"),
+    "jk2": ("sbuf", [128, 960], "bfloat16"), "jkb": ("sbuf", [128, 960], "bfloat16"), "jke": ("sbuf", [128, 336], "bfloat16"),
+    "en": ("sbuf", [128, 4], "float32"), "lt": ("sbuf", [128, 4], "float32"), "pen": ("sbuf", [128, 4], "float32"),
+    "bc": ("sbuf", [128, 192], "float32"), "bt": ("sbuf", [128, 192], "float32"), "qm": ("sbuf", [128, 2], "float32"),
+    "g4": ("sbuf", [128, 2], "float32"), "tl": ("sbuf", [128, 2], "float32"), "ini": ("sbuf", [128, 1], "float32"),
+    "cnt2": ("sbuf", [128, 4], "float32"), "off2": ("sbuf", [128, 12], "uint16"),
+    "nb": ("sbuf", [128, 320], "bfloat16"), "num": ("sbuf", [128, XC], "float32"), "wg": ("sbuf", [128, 96], "float32"), "wtr": ("sbuf", [128, 96], "float32"),
+    "ys": ("sbuf", [128, 128], "float32"),
+    "th1": ("sbuf", [128, 1], "float32"), "eb1": ("sbuf", [128, 1], "float32"), "th2": ("sbuf", [128, 1], "float32"), "eb2": ("sbuf", [128, 1], "float32"),
+    "pI": ("sbuf", [128, 16], "int32"), "rI": ("sbuf", [128, 16], "int32"), "qI": ("sbuf", [128, 16], "int32"),
+    "b16": ("sbuf", [128, 8], "int32"), "b32": ("sbuf", [128, 8], "int32"), "bfin": ("sbuf", [128, 8], "int32"), "ofi": ("sbuf", [128, 8], "int32"),
+    "cs": ("sbuf", [128, 8], "float32"), "csp": ("sbuf", [128, 8], "float32"), "csn": ("sbuf", [128, 8], "float32"), "cm": ("sbuf", [128, 8], "float32"), "cmn": ("sbuf", [128, 8], "float32"),
+    "i80": ("sbuf", [128, 80], "float32"), "ofin": ("sbuf", [128, 8], "uint16"),
+    "ps": ("psum", [128, 4096], "float32"),
+}
+SEMAPHORES = ["v", "a", "t", "gq", "dx", "drt", "dw", "dr2", "dvx", "dvh", "dxw", "dnb", "dout", "ls",
+              "arr0", "arr1", "arr2", "arr3", "am", "arrb", "aw"]
+
+
+def rank_program(g, core, T, topo):
+    rank = T.rank_of(core)
+    if rank is None:
+        return
+    cores = list(T.cores)
+    me_chip = topo.chip(core)
+    others = [(rank + 1 + k) % N for k in range(N - 1)]
+    order = [b for b in others if not topo.same_plane(topo.chip(cores[b]), me_chip)] + \
+            [b for b in others if topo.same_plane(topo.chip(cores[b]), me_chip)]
+    eng = {"v": g.vector, "a": g.scalar, "t": g.tensor, "s": g.sync, "g": g}
+    semof = {"v": "v", "a": "a", "t": "t", "g": "gq"}
+    tot, seen = {}, {q: {} for q in eng}
+
+    def wait(q, deps):
+        for s, n in deps:
+            if seen[q].get(s, 0) < n:
+                eng[q].wait_ge(T.sem[s], n)
+                seen[q][s] = n
+
+    def op(q, fn, *deps):
+        wait(q, deps)
+        s = semof[q]
+        fn(eng[q]).then_inc(T.sem[s], 1)
+        tot[s] = tot.get(s, 0) + 1
+        return (s, tot[s])
+
+    def dma(q, s, out, src, *deps):
+        wait(q, deps)
+        eng[q].dma_start(out, src).then_inc(T.sem[s], 16)
+        tot[s] = tot.get(s, 0) + 16
+        return (s, tot[s])
+
+    def send(b, out, src, sem, *deps):
+        wait("g", deps)
+        rid, pid, _ = topo.addr(cores[b])
+        g.remote_dma(out, src, T.sem[sem], T.sem.ls, pid, rid, topo.mask(core, cores[b]))
+        tot["ls"] = tot.get("ls", 0) + len(topo.engines(core, cores[b]))
+
+    def arrivals(srcs, per):
+        return per * sum(len(topo.engines(cores[s], core)) for s in srcs)
+
+    u8, u32 = dt.uint8, dt.uint32
+    c8 = lambda v: v.bitcast(u8)
+    ms = lambda ap, val, *d: op("v", lambda e: e.memset(ap, val), *d)
+    ts = lambda out, x, s1, s2, o0, o1, *d: op("v", lambda e: e.tensor_scalar(out, x, s1, s2, o0) if o1 is None else e.tensor_scalar(out, x, s1, s2, o0, o1), *d)
+    tt = lambda out, x, y, o, *d: op("v", lambda e: e.tensor_tensor(out, x, y, o), *d)
+    cp = lambda out, x, *d: op("v", lambda e: e.tensor_copy(out, x), *d)
+    red = lambda out, x, o, *d: op("v", lambda e: e.tensor_reduce(out, x, AxisListType.X, o), *d)
+    scan = lambda out, x, y, i, o, *d: op("v", lambda e: e.tensor_tensor_scan(out, x, y, i, OP.add, o), *d)
+    quant = lambda q, s, x, *d: op("v", lambda e: e.quantize_mx(q, s, x), *d)
+    act = lambda out, x, f, b, s, *d: op("a", lambda e: e.activation(out, x, f, bias=b, scale=s), *d)
+    acc = lambda out, x, f, b, o, *d: op("a", lambda e: e.activation(out, x, f, bias=b, scale=1.0, accum_out=o), *d)
+    pickq = lambda out, win, off, *d: op("v", lambda e: e.tensor_copy(out.bitcast(u32), win.bitcast(u32).indirect(off)), *d)
+    picks = lambda out, win, off, *d: op("a", lambda e: e.activation(out, win.indirect(off), AF.Copy), *d)
+    quad = lambda q: slice(32 * q, 32 * q + 32)
+    bank = lambda k, n: T.ps[:, 512 * k:512 * k + n]
+
+    def mm(out, w, ws, x, xs, start, stop, *d):
+        return op("t", lambda e: e.matmul_mx(out, w, ws, x, xs, start, stop), *d)
+
+    d_rt = dma("a", "drt", T.rtt[:, 0:16], T.rt[:, 0:16])
+    d_x = dma("s", "dx", T.xt[:, 0:768], T.x[:])
+    d_w = dma("s", "dw", T.wt[:], T.w[:], d_x)
+    d_r2 = dma("s", "dr2", T.r2t[:, 0:20], T.r2[:, 0:20])
+    d_vx = dma("s", "dvx", T.vxt[:], T.vx[:])
+    d_vh = dma("s", "dvh", T.vht[:], T.vh[:])
+
+    gi = lambda out, pat, cmul: op("g", lambda e: e.iota(out, pat, 0, cmul))
+    gi(T.pI[:], [[0, 16]], 1)
+    gi(T.b16[:], [[16, 8]], 0)
+    k_g = gi(T.b32[:], [[32, 8]], 0)
+    k_fin = gi(T.bfin[:], [[64, 4], [16, 2]], 0)
+    k_80 = op("g", lambda e: e.iota(T.i80[:], [[1, 80]], 0, 0, allow_small_or_imprecise_dtypes=True))
+    ms(T.rtt[:, 32:512], 0.0)
+    for c in range(len(RTB)):
+        k_rto = ms(T.rto[:, 2 * c:2 * c + 2], RTB[c])
+    k_x0 = ms(T.xt[:, 768:776], 0.0)
+    ms(T.th1[0:64, :], -EPS / 2)
+    ms(T.th1[64:128, :], EPS / 2)
+    ms(T.eb1[0:32, :], 0.0)
+    ms(T.eb1[32:64, :], -EPS)
+    ms(T.eb1[64:96, :], EPS)
+    k_th = ms(T.eb1[96:128, :], 0.0)
+    ms(T.zb[:], 0.0)
+    k_jk = ms(T.jkd[:, 192:193], -192.0)
+    k_jk = ms(T.jkd[:, 448:449], -192.0)
+    kr = ts(T.rI[:], T.pI[:], 15, None, OP.bitwise_and, None, k_g)
+    kq = ts(T.qI[:], T.pI[:], 31, None, OP.bitwise_and, None)
+    k1 = tt(T.cs[:], T.rI[:, 0:8], T.b16[:], OP.add, kr)
+    ts(T.csp[:], T.cs[:], 0.5, None, OP.add, None, k1)
+    k_cs = ts(T.csn[:], T.cs[:], -1.0, -0.5, OP.mult, OP.add)
+    k_lw = ms(T.lwho[:], -1.0)
+    k_mi = ms(T.msgi[:, 8 * rank:8 * rank + 8], 0.0)
+    k_mo = ms(T.msgo[:], 0.0)
+
+    k = ts(T.rtt[:, 16:32], T.rtt[:, 0:16], -1.0, None, OP.mult, None, d_rt)
+    k_rq = quant(T.rtq[:], T.rts[:], T.rtt[:], k)
+    kp1 = pickq(T.rpq[:, 0:256], T.rtq[:], T.rto[:, 0:16], k_rq)
+    ks1 = picks(T.rps[:, 0:256], T.rts[:], T.rto[:, 0:16], k_rq, k_rto)
+    k_xq = quant(T.xq[:], T.xs[:], T.xt[:], d_x, k_x0)
+    kp2 = pickq(T.rpq[:, 256:448], T.rtq[:], T.rto[:, 16:28])
+    ks2 = picks(T.rps[:, 256:448], T.rts[:], T.rto[:, 16:28])
+    dm = []
+    for j in range(3):
+        mm(bank(j, 192), T.rpq[:, 0:128], T.rps[:, 0:128], T.xq[:, 0:192], T.xs[:, 0:192], True, False, kp1, ks1, k_xq)
+        a = 32 * RTS[j]
+        dj = (kp2, ks2) if j else ()
+        dm.append(mm(bank(j, 192), T.rpq[:, a:a + 128], T.rps[:, a:a + 128], T.xq[:, 0:192], T.xs[:, 0:192], False, True, *dj))
+    k_z1 = act(T.z1[:], bank(0, 192), AF.Identity, T.eb1[:], 1.0, dm[0], k_th)
+    k2 = tt(T.cm[:], T.qI[:, 0:8], T.b32[:], OP.add, kq)
+    k_cm = ts(T.cmn[:], T.cm[:], -1.0, -0.5, OP.mult, OP.add, k2)
+    k = tt(T.z2[:], bank(1, 192), T.z1[:], OP.min, dm[1], k_z1)
+    k_d1 = tt(T.z3[:], bank(2, 192), T.z2[:], OP.min, dm[2], k)
+    k = ts(T.mk[:], T.z3[:], T.th1[:], None, OP.is_gt, None, k_d1)
+    k_cum = scan(T.cum[:], T.mk[:], T.zb[:, 0:192], 0.0, OP.add, k)
+    k_a = [acc(T.jka[:, 192 * c:192 * c + 192], T.cum[:], AF.Sign, T.csn[:, c:c + 1], T.cnt1[:, c:c + 1], k_cum, k_cs) for c in range(3)]
+    k3 = ts(T.jkd[:, 0:192], T.cum[:], T.csp[:, 3:4], 2.0, OP.is_gt, OP.mult, k_cum)
+    k4 = ts(T.jkd[:, 256:448], T.cum[:], T.csp[:, 4:5], 2.0, OP.is_gt, OP.mult)
+    ts(T.cnt1[:, 5:6], T.cum[:, 191:192], -2.0, 192.0, OP.mult, OP.add)
+    red(T.cnt1[:, 3:4], T.jkd[:, 0:193], OP.add, k3, k_jk)
+    k_c = red(T.cnt1[:, 4:5], T.jkd[:, 256:449], OP.add, k4)
+    pk, psc, k_off = {}, {}, {}
+    for i, b in enumerate(order + [rank]):
+        for q in range(N):
+            k_off[b] = ts(T.off1[quad(q), 6 * b:6 * b + 6], T.cnt1[quad(b), 0:6], -0.5, 96.0, OP.mult, OP.add, k_c, k_a[-1])
+        o, so = (T.sl1[:, 80 * i:80 * i + 80], T.ss1[:, 80 * i:80 * i + 80]) if b != rank else \
+                (T.land1[:, 80 * b:80 * b + 80], T.lans1[:, 80 * b:80 * b + 80])
+        pk[b] = pickq(o, T.xq[:, 0:194], T.off1[:, 6 * b:6 * b + 5], k_off[b])
+        psc[b] = picks(so, T.xs[:, 0:194], T.off1[:, 6 * b:6 * b + 5], k_off[b])
+        if b != rank:
+            send(b, c8(T.land1[:, 80 * rank:80 * rank + 80]), c8(T.sl1[:, 80 * i:80 * i + 80]), "arr%d" % rank, pk[b], k_lw)
+            send(b, T.lans1[:, 80 * rank:80 * rank + 80], T.ss1[:, 80 * i:80 * i + 80], "arr%d" % rank, psc[b])
+    k_m = [acc(T.jka[:, 576 + 192 * c:768 + 192 * c], T.cum[:], AF.Sign, T.cmn[:, c:c + 1], T.cntm[:, c:c + 1], k_cm) for c in range(3)]
+    m_v, m_a = {}, {}
+    for b in order + [rank]:
+        m, o = (T.msgo, 8 * b) if b != rank else (T.msgi, 8 * rank)
+        m_v[b] = cp(m[:, o + 1:o + 2], T.off1[:, 6 * b + 5:6 * b + 6], k_off[b], k_mo)
+        for c in range(3):
+            m_a[b] = act(m[quad(c), o:o + 1], T.cntm[quad(b), c:c + 1], AF.Copy, 96.0, -0.5, k_m[2], k_mo)
+        if b != rank:
+            send(b, T.msgi[:, 8 * rank:8 * rank + 2], T.msgo[:, o:o + 2], "am", m_v[b], m_a[b])
+
+    k_oz = ms(T.ozero[:], TOK)
+    k_z = pickq(T.land1[:, NX:XC], T.xq[:, 0:194], T.ozero[:, 0:1], k_xq, k_oz)
+    k_zs = picks(T.lans1[:, NX:XC], T.xs[:, 0:194], T.ozero[:, 0:1], k_z)
+    k_wq = quant(T.wq[:], T.wsc[:], T.wt[:], d_w)
+    ms(T.r2t[:, 40:512], 0.0)
+    k = ts(T.r2t[:, 20:40], T.r2t[:, 0:20], -1.0, None, OP.mult, None, d_r2)
+    k_r2q = quant(T.r2q[:], T.r2s[:], T.r2t[:], k)
+    srt = sorted(others)
+    one = {srt[0]: srt[1], srt[1]: srt[0], srt[2]: srt[0], rank: 0}
+    two = {srt[0]: srt[2], srt[1]: srt[2], srt[2]: srt[1], rank: 0}
+    blocks = [0, 1, 2, 3] + [5 + one[q] for q in range(N)] + [5 + two[q] for q in range(N)] + [4] * 4
+    for c in range(16):
+        k_o = ms(T.r2o[:, 2 * c:2 * c + 2], blocks[c])
+    k_r2p = pickq(T.r2p[:], T.r2q[:], T.r2o[:], k_o, k_r2q)
+    k_r2s = picks(T.r2ps[:], T.r2s[:], T.r2o[:], k_o, k_r2q)
+    k_z2 = pickq(T.land2[:, 64 * rank:64 * rank + 64], T.xq[:, 0:194], T.ozero[:], k_xq)
+    k_z2s = picks(T.lans2[:, 64 * rank:64 * rank + 64], T.xs[:, 0:194], T.ozero[:], k_z2)
+    k_vx = quant(T.vxq[:], T.vxs[:], T.vxt[:], d_vx)
+    k_vh = quant(T.vhq[:], T.vhs[:], T.vht[:], d_vh)
+    for q in range(N):
+        ms(T.th2[quad(q), :], -EPS / 2 if q == srt[2] else EPS / 2)
+        k_t2 = ms(T.eb2[quad(q), :], -EPS if q == srt[1] else 0.0)
+    ms(T.zf[:], 0.0)
+    ms(T.cap[:], 64 * STEP)
+    k_je = ms(T.jke[:, 320:321], -320.0)
+    k_num = ms(T.num[:], -1.0)
+    k = ts(T.ofi[:], T.bfin[:], 32.0, None, OP.add, None, k_fin)
+    k = tt(T.ofi[:], T.rI[:, 0:8], T.ofi[:], OP.add, k)
+    k_ofin = cp(T.ofin[:], T.ofi[:], k)
+
+    arr = lambda s: ("arr%d" % s, arrivals([s], 2))
+    home = (pk[rank], psc[rank])
+    halves = [(0, NH, [0, 1]), (NH, NX + 2, [2, 3])]
+    W = []
+    for h, (c0, c1, who) in enumerate(halves):
+        deps = [arr(s) for s in who if s != rank] + list(home) + [k_z, k_zs, k_wq, k_d1, k_z1]
+        W.append([mm(bank(4 * h + i, c1 - c0), T.wq[:, 128 * i:128 * i + 128], T.wsc[:, 128 * i:128 * i + 128], T.land1[:, c0:c1], T.lans1[:, c0:c1], True, True, *deps) for i in range(4)])
+    kq_h = []
+    for h, (c0, c1, who) in enumerate(halves):
+        hv = lambda i: T.hb[:, 4 * c0 + i:4 * c1:4]
+        k0 = act(hv(0), bank(4 * h, c1 - c0), AF.Relu, 0.0, 0.0625, W[h][0])
+        k1 = ts(hv(1), bank(4 * h + 1, c1 - c0), 0.0, 0.0625, OP.max, OP.mult, W[h][1])
+        k2 = act(hv(2), bank(4 * h + 2, c1 - c0), AF.Relu, 0.0, 0.0625, W[h][2])
+        k3 = ts(hv(3), bank(4 * h + 3, c1 - c0), 0.0, 0.0625, OP.max, OP.mult, W[h][3])
+        kq_h.append(quant(T.xw[:, HB + c0:HB + c1], T.xws[:, HB + c0:HB + c1], T.hb[:, 4 * c0:4 * c1], k0, k1, k2, k3))
+    alla = [arr(s) for s in range(N) if s != rank]
+    dma("s", "dxw", c8(T.xw[:, 0:XC]), c8(T.land1[:]), *alla, *home, k_z, k_zs)
+    d_xw = dma("s", "dxw", T.xws[:, 0:XC], T.lans1[:])
+    am = ("am", arrivals(others, 1))
+    for s in range(N):
+        d_nb = dma("s", "dnb", T.nb[0:1, 80 * s:80 * s + 80], T.msgi[0:80, 8 * s:8 * s + 1], am, m_v[rank], m_a[rank])
+
+    H = lambda a, b: (T.xw[:, HB + a:HB + b], T.xws[:, HB + a:HB + b])
+    P = lambda k: (T.r2p[:, 128 * k:128 * k + 128], T.r2ps[:, 128 * k:128 * k + 128])
+    ea = mm(bank(0, NH), *P(3), *H(0, NH), True, True, kq_h[0], k_r2p, k_r2s, k_r2q)
+    e0 = mm(bank(1, 128), *H(0, 128), T.r2q[:], T.r2s[:], True, True)
+    mm(bank(2, NH), *P(0), *H(0, NH), True, False)
+    fa = mm(bank(2, NH), *P(1), *H(0, NH), False, True)
+    eb = mm(bank(4, NH), *P(3), *H(NH, NX), True, True, kq_h[1])
+    e1 = mm(bank(5, 128), *H(128, 256), T.r2q[:], T.r2s[:], True, True)
+    e2 = mm(bank(6, 128), *H(192, 320), T.r2q[:], T.r2s[:], True, True)
+    mm(bank(7, NH), *P(0), *H(NH, NX), True, False)
+    fb = mm(bank(7, NH), *P(1), *H(NH, NX), False, True)
+    mm(bank(3, NX), *P(0), *H(0, NX), True, False)
+    f2 = mm(bank(3, NX), *P(2), *H(0, NX), False, True)
+    e4 = lambda k: T.ps[:, 512 * k + 4:512 * k + 5]
+    ken0 = act(T.en[:, 0:1], e4(1), AF.Copy, 0.0, 1.0, e0)
+    act(T.y1[:, 0:NH], bank(2, NH), AF.Identity, T.eb2[:], 1.0, fa, k_t2)
+    ken1 = act(T.en[:, 1:2], e4(5), AF.Copy, 0.0, 1.0, e1)
+    ken2 = act(T.en[:, 2:3], e4(6), AF.Copy, 0.0, 1.0, e2)
+    k_y1 = act(T.y1[:, NH:NX], bank(7, NH), AF.Identity, T.eb2[:], 1.0, fb)
+    for s in range(N):
+        ki = ts(T.inv[:, 80 * s:80 * s + 80], T.i80[:], T.msgi[:, 8 * s + 1:8 * s + 2], BIG, OP.is_ge, OP.mult, k_80, am, m_v[rank])
+    tt(T.em[:, 0:NH], bank(0, NH), T.inv[:, 0:NH], OP.add, ea, ki)
+    k_em = tt(T.em[:, NH:NX], bank(4, NH), T.inv[:, NH:NX], OP.add, eb)
+    kc0 = ts(T.jk2[:, 0:320], T.em[:], T.en[:, 0:1], None, OP.is_lt, None, k_em, ken0)
+    kc1 = ts(T.jk2[:, 320:640], T.em[:], T.en[:, 1:2], None, OP.is_lt, None, ken1)
+    k = act(T.jk2[:, 640:960], T.em[:], AF.Sign, T.en[:, 2:3], -1.0, k_em, ken2)
+    kl0 = acc(T.jkb[:, 0:320], T.jk2[:, 0:320], AF.Copy, 0.0, T.lt[:, 0:1], kc0)
+    kl2 = acc(T.jkb[:, 320:640], T.jk2[:, 640:960], AF.Relu, 0.0, T.lt[:, 2:3], k)
+    kl1 = red(T.lt[:, 1:2], T.jk2[:, 320:640], OP.add, kc1)
+    k_y2 = tt(T.y2[:], bank(3, NX), T.y1[:], OP.min, f2, k_y1)
+    k = act(T.sn[:], T.y2[:], AF.Sign, T.th2[:], 1.0, k_y2)
+    k_ns = act(T.ns[:], T.sn[:], AF.Relu, 0.0, -BIG, k)
+    for s in range(N):
+        k_n = act(T.num[0:1, 80 * s:80 * s + 80], T.nb[0:1, 80 * s:80 * s + 80], AF.Copy, float(TOK * s), 1.0, d_nb, k_num)
+    kp = ts(T.pen[:, 0:3], T.lt[:, 0:3], DF - 0.5, LOW, OP.is_ge, OP.mult, kl0, kl1, kl2)
+    for k in range(3):
+        ts(T.bc[:, 32 * k:32 * k + 32], T.zf[:], T.en[:, k:k + 1], T.pen[:, k:k + 1], OP.add, OP.add, kp)
+        kc = ts(T.bc[:, 96 + 32 * k:128 + 32 * k], T.zf[:], T.lt[:, k:k + 1], T.pen[:, k:k + 1], OP.add, OP.add)
+    kc = op("v", lambda e: e.transpose(T.bt[:], T.bc[:]), kc)
+    k_eb = tt(T.emb[:], T.em[:], T.ns[:], OP.add, k_ns)
+    red(T.qm[:, 0:1], T.bt[:, 0:96], OP.max, kc)
+    kc = red(T.qm[:, 1:2], T.bt[:, 96:192], OP.max)
+    tt(T.g4[0:64, :], T.qm[0:64, :], T.qm[64:128, :], OP.max, kc)
+    kc = tt(T.g4[64:128, :], T.qm[64:128, :], T.qm[0:64, :], OP.max)
+    for q in range(N):
+        k = tt(T.tl[quad(q), :], T.g4[quad(q), :], T.g4[quad(q ^ 1), :], OP.max, kc)
+    k_sg = act(T.sg[:], T.emb[:], AF.Sign, T.tl[:, 0:1], -1.0, k, k_eb)
+    k_gd = ts(T.gd[:], T.em[:], T.tl[:, 0:1], STEP, OP.is_equal, OP.mult, k)
+    k_i = ts(T.ini[:], T.tl[:, 1:2], DF + 0.5, STEP, OP.subtract, OP.mult)
+    k = scan(T.nq[:], T.gd[:], T.cap[:], T.ini[:], OP.min, k_i)
+    k = tt(T.mk2[:], T.sg[:], T.nq[:], OP.is_gt, k, k_sg)
+    k_c2 = scan(T.cum2[:], T.mk2[:], T.zb[:], 0.0, OP.add, k)
+    ka = acc(T.jkb[:, 640:960], T.cum2[:], AF.Sign, T.csn[:, 0:1], T.cnt2[:, 0:1], k_c2)
+    k = ts(T.jke[:, 0:320], T.cum2[:], T.csp[:, 1:2], 2.0, OP.is_gt, OP.mult, k_c2)
+    k = red(T.cnt2[:, 1:2], T.jke[:, 0:321], OP.add, k)
+    kc = ts(T.cnt2[:, 2:4], T.cnt2[:, 0:2], -2.0 * HB, None, OP.add, None, k, ka)
+    for i, b in enumerate(order):
+        for q in range(N):
+            ko = ts(T.off2[quad(q), 4 * i:4 * i + 4], T.cnt2[quad(b), 0:4], -0.5, NX / 2.0, OP.mult, OP.add, kc)
+        o = slice(64 * i, 64 * i + 64)
+        kk = pickq(T.sl2[:, o], T.xw[:], T.off2[:, 4 * i:4 * i + 4], ko, d_xw)
+        ks = picks(T.ss2[:, o], T.xws[:], T.off2[:, 4 * i:4 * i + 4], ko, d_xw)
+        d = slice(64 * rank, 64 * rank + 64)
+        send(b, c8(T.land2[:, d]), c8(T.sl2[:, o]), "arrb", kk)
+        send(b, T.lans2[:, d], T.ss2[:, o], "arrb", ks)
+    for i in range(3):
+        kw = op("a", lambda e: e.activation(T.wg[:, 32 * i:32 * i + 32], T.num[:].indirect(T.off2[:, 4 * i:4 * i + 2]), AF.Copy), k_n)
+    kw = op("v", lambda e: e.transpose(T.wtr[:], T.wg[:]), kw)
+    for i, b in enumerate(order):
+        send(b, T.lwho[:, rank:rank + 1], T.wtr[:, 32 * i:32 * i + 1], "aw", kw)
+
+    ab = ("arrb", arrivals(others, 2))
+    mm(bank(5, 224), T.vxq[:], T.vxs[:], T.land2[:, 0:224], T.lans2[:, 0:224], True, False, ab, k_z2, k_z2s, k_vx, k_vh, ken1)
+    ty = mm(bank(5, 224), T.vhq[:], T.vhs[:], T.land2[:, 32:256], T.lans2[:, 32:256], False, True)
+    kf = pickq(T.fin[:], T.land2[:], T.ofin[:], ab, k_ofin)
+    kfs = picks(T.fins[:], T.lans2[:], T.ofin[:], ab, k_ofin)
+    for a in range(N):
+        ky = cp(T.ys[:, CB * a:CB * a + CB], T.ps[:, 2560 + 64 * a:2560 + 64 * a + CB], ty)
+    dma("s", "dout", T.oc[:], c8(T.fin[:]), kf)
+    for k in range(4):
+        dma("s" if k < 2 else "a", "dout", T.osc[4 * k:4 * k + 4, :], T.fins[32 * k:32 * k + 4, :], kfs)
+    dma("a", "dout", T.y[:], T.ys[:], ky)
+    kw = op("v", lambda e: e.transpose(T.whot[:], T.lwho[:]), ("aw", arrivals(others, 1)), k_lw)
+    dma("s", "dout", T.who[:], T.whot[0:4, :], kw)
+    wait("g", [(s, n) for s, n in tot.items()])

@@ -1,4 +1,3 @@
-from concourse.bass import DstId, RemoteDMATransfer
 from concourse.mybir import dt, AluOpType as OP, AxisListType, ActivationFunctionType as AF
 
 N, TOK, CAP, CB, DF = 4, 192, 80, 32, 80
@@ -7,7 +6,6 @@ NH = NX // 2
 XC = 336
 HB = 352
 EPS, BIG, LOW = 1e-30, 1e29, -9e29
-STEP = 2.0 ** -10
 RTB = [0, 1, 2, 3, 5, 4, 7, 6, 5, 4, 6, 7, 4, 5]
 RTS = [4, 6, 10]
 
@@ -24,35 +22,38 @@ SCRATCH = {
     "sl1": ("sbuf", [128, 240], "float8_e4m3fn_x4"), "ss1": ("sbuf", [128, 240], "uint8"),
     "land1": ("sbuf", [128, XC], "float8_e4m3fn_x4"), "lans1": ("sbuf", [128, XC], "uint8"),
     "msgo": ("sbuf", [128, 32], "bfloat16"), "msgi": ("sbuf", [128, 32], "bfloat16"),
+    "cnte": ("sbuf", [128, 8], "bfloat16"), "cntq": ("sbuf", [128, 8], "bfloat16"),
     "xw": ("sbuf", [128, 704], "float8_e4m3fn_x4"), "xws": ("sbuf", [128, 704], "uint8"),
     "sl2": ("sbuf", [128, 192], "float8_e4m3fn_x4"), "ss2": ("sbuf", [128, 192], "uint8"),
-    "land2": ("sbuf", [128, 256], "float8_e4m3fn_x4"), "lans2": ("sbuf", [128, 256], "uint8"),
+    "land2": ("sbuf", [128, 208], "float8_e4m3fn_x4"), "lans2": ("sbuf", [128, 208], "uint8"),
     "fin": ("sbuf", [128, 128], "float8_e4m3fn_x4"), "fins": ("sbuf", [128, 128], "uint8"),
     "lwho": ("sbuf", [128, 32], "float32"), "whot": ("sbuf", [128, 32], "float32"),
     "z1": ("sbuf", [128, 192], "float32"), "z2": ("sbuf", [128, 192], "float32"), "z3": ("sbuf", [128, 192], "float32"),
     "mk": ("sbuf", [128, 192], "bfloat16"), "cum": ("sbuf", [128, 192], "bfloat16"), "zb": ("sbuf", [128, 320], "bfloat16"), "zf": ("sbuf", [128, 32], "float32"),
     "jka": ("sbuf", [128, 1152], "bfloat16"), "jkd": ("sbuf", [128, 512], "bfloat16"),
     "cnt1": ("sbuf", [128, 8], "float32"), "cntm": ("sbuf", [128, 4], "float32"), "off1": ("sbuf", [128, 24], "uint16"), "ozero": ("sbuf", [128, 4], "uint16"),
-    "inv": ("sbuf", [128, 320], "float32"), "em": ("sbuf", [128, 320], "float32"), "emb": ("sbuf", [128, 320], "float32"),
-    "y1": ("sbuf", [128, 320], "float32"), "y2": ("sbuf", [128, 320], "float32"), "sn": ("sbuf", [128, 320], "float32"), "ns": ("sbuf", [128, 320], "float32"),
-    "gd": ("sbuf", [128, 320], "bfloat16"), "nq": ("sbuf", [128, 320], "bfloat16"), "sg": ("sbuf", [128, 320], "bfloat16"), "cap": ("sbuf", [128, 320], "bfloat16"),
+    "inv": ("sbuf", [128, 320], "float32"), "em": ("sbuf", [128, 320], "float32"),
+    "s1": ("sbuf", [128, 320], "bfloat16"), "s2": ("sbuf", [128, 320], "bfloat16"), "c2": ("sbuf", [128, 320], "bfloat16"), "uw": ("sbuf", [128, 320], "bfloat16"),
+    "gd": ("sbuf", [128, 320], "bfloat16"), "nq": ("sbuf", [128, 320], "bfloat16"), "sg": ("sbuf", [128, 320], "bfloat16"),
+    "nf": ("sbuf", [128, 320], "bfloat16"), "t1": ("sbuf", [128, 320], "bfloat16"), "t2": ("sbuf", [128, 320], "bfloat16"),
     "mk2": ("sbuf", [128, 320], "bfloat16"), "cum2": ("sbuf", [128, 320], "bfloat16"),
-    "jk2": ("sbuf", [128, 960], "bfloat16"), "jkb": ("sbuf", [128, 960], "bfloat16"), "jke": ("sbuf", [128, 336], "bfloat16"),
+    "jk2": ("sbuf", [128, 960], "bfloat16"), "jkb": ("sbuf", [128, 960], "bfloat16"), "jke": ("sbuf", [128, 640], "bfloat16"), "jkc": ("sbuf", [128, 640], "bfloat16"),
     "en": ("sbuf", [128, 4], "float32"), "lt": ("sbuf", [128, 4], "float32"), "pen": ("sbuf", [128, 4], "float32"),
     "bc": ("sbuf", [128, 192], "float32"), "bt": ("sbuf", [128, 192], "float32"), "qm": ("sbuf", [128, 2], "float32"),
-    "g4": ("sbuf", [128, 2], "float32"), "tl": ("sbuf", [128, 2], "float32"), "ini": ("sbuf", [128, 1], "float32"),
+    "g4": ("sbuf", [128, 2], "float32"), "tl": ("sbuf", [128, 2], "float32"), "khb": ("sbuf", [128, 2], "float32"), "ac": ("sbuf", [128, 2], "float32"),
     "cnt2": ("sbuf", [128, 4], "float32"), "off2": ("sbuf", [128, 12], "uint16"),
     "nb": ("sbuf", [128, 320], "bfloat16"), "num": ("sbuf", [128, XC], "float32"), "wg": ("sbuf", [128, 96], "float32"), "wtr": ("sbuf", [128, 96], "float32"),
     "ys": ("sbuf", [128, 128], "float32"),
     "th1": ("sbuf", [128, 1], "float32"), "eb1": ("sbuf", [128, 1], "float32"), "th2": ("sbuf", [128, 1], "float32"), "eb2": ("sbuf", [128, 1], "float32"),
     "pI": ("sbuf", [128, 16], "int32"), "rI": ("sbuf", [128, 16], "int32"), "qI": ("sbuf", [128, 16], "int32"),
-    "b16": ("sbuf", [128, 8], "int32"), "b32": ("sbuf", [128, 8], "int32"), "bfin": ("sbuf", [128, 8], "int32"), "ofi": ("sbuf", [128, 8], "int32"),
+    "b16": ("sbuf", [128, 8], "int32"), "b32": ("sbuf", [128, 8], "int32"),
     "cs": ("sbuf", [128, 8], "float32"), "csp": ("sbuf", [128, 8], "float32"), "csn": ("sbuf", [128, 8], "float32"), "cm": ("sbuf", [128, 8], "float32"), "cmn": ("sbuf", [128, 8], "float32"),
     "i80": ("sbuf", [128, 80], "float32"), "ofin": ("sbuf", [128, 8], "uint16"),
     "ps": ("psum", [128, 4096], "float32"),
 }
 SEMAPHORES = ["v", "a", "t", "gq", "dx", "drt", "dw", "dr2", "dvx", "dvh", "dxw", "dnb", "dout", "ls",
-              "arr0", "arr1", "arr2", "arr3", "am", "arrb", "aw"]
+              "arr0", "arr1", "arr2", "arr3", "am", "ae", "arrb", "aw"]
+EARLY = 2
 
 
 def rank_program(g, core, T, topo):
@@ -62,8 +63,9 @@ def rank_program(g, core, T, topo):
     cores = list(T.cores)
     me_chip = topo.chip(core)
     others = [(rank + 1 + k) % N for k in range(N - 1)]
-    order = [b for b in others if not topo.same_plane(topo.chip(cores[b]), me_chip)] + \
-            [b for b in others if topo.same_plane(topo.chip(cores[b]), me_chip)]
+    near = rank ^ 1
+    order = sorted(others, key=lambda b: (b != near, topo.same_plane(topo.chip(cores[b]), me_chip)))
+    slot = lambda a, b: sorted(r for r in range(N) if r != b).index(a)
     eng = {"v": g.vector, "a": g.scalar, "t": g.tensor, "s": g.sync, "g": g}
     semof = {"v": "v", "a": "a", "t": "t", "g": "gq"}
     tot, seen = {}, {q: {} for q in eng}
@@ -104,6 +106,7 @@ def rank_program(g, core, T, topo):
     cp = lambda out, x, *d: op("v", lambda e: e.tensor_copy(out, x), *d)
     red = lambda out, x, o, *d: op("v", lambda e: e.tensor_reduce(out, x, AxisListType.X, o), *d)
     scan = lambda out, x, y, i, o, *d: op("v", lambda e: e.tensor_tensor_scan(out, x, y, i, OP.add, o), *d)
+    elem = lambda out, x, y, o, *d: op("v", lambda e: e.tensor_tensor_scan(out, x, y, -64.0, OP.max, o), *d)
     quant = lambda q, s, x, *d: op("v", lambda e: e.quantize_mx(q, s, x), *d)
     act = lambda out, x, f, b, s, *d: op("a", lambda e: e.activation(out, x, f, bias=b, scale=s), *d)
     acc = lambda out, x, f, b, o, *d: op("a", lambda e: e.activation(out, x, f, bias=b, scale=1.0, accum_out=o), *d)
@@ -126,29 +129,13 @@ def rank_program(g, core, T, topo):
     gi(T.pI[:], [[0, 16]], 1)
     gi(T.b16[:], [[16, 8]], 0)
     k_g = gi(T.b32[:], [[32, 8]], 0)
-    k_fin = gi(T.bfin[:], [[64, 4], [16, 2]], 0)
     k_80 = op("g", lambda e: e.iota(T.i80[:], [[1, 80]], 0, 0, allow_small_or_imprecise_dtypes=True))
     ms(T.rtt[:, 32:512], 0.0)
-    for c in range(len(RTB)):
+    c = 0
+    while c < len(RTB):
         k_rto = ms(T.rto[:, 2 * c:2 * c + 2], RTB[c])
+        c += 1
     k_x0 = ms(T.xt[:, 768:776], 0.0)
-    ms(T.th1[0:64, :], -EPS / 2)
-    ms(T.th1[64:128, :], EPS / 2)
-    ms(T.eb1[0:32, :], 0.0)
-    ms(T.eb1[32:64, :], -EPS)
-    ms(T.eb1[64:96, :], EPS)
-    k_th = ms(T.eb1[96:128, :], 0.0)
-    ms(T.zb[:], 0.0)
-    k_jk = ms(T.jkd[:, 192:193], -192.0)
-    k_jk = ms(T.jkd[:, 448:449], -192.0)
-    kr = ts(T.rI[:], T.pI[:], 15, None, OP.bitwise_and, None, k_g)
-    kq = ts(T.qI[:], T.pI[:], 31, None, OP.bitwise_and, None)
-    k1 = tt(T.cs[:], T.rI[:, 0:8], T.b16[:], OP.add, kr)
-    ts(T.csp[:], T.cs[:], 0.5, None, OP.add, None, k1)
-    k_cs = ts(T.csn[:], T.cs[:], -1.0, -0.5, OP.mult, OP.add)
-    k_lw = ms(T.lwho[:], -1.0)
-    k_mi = ms(T.msgi[:, 8 * rank:8 * rank + 8], 0.0)
-    k_mo = ms(T.msgo[:], 0.0)
 
     k = ts(T.rtt[:, 16:32], T.rtt[:, 0:16], -1.0, None, OP.mult, None, d_rt)
     k_rq = quant(T.rtq[:], T.rts[:], T.rtt[:], k)
@@ -157,6 +144,10 @@ def rank_program(g, core, T, topo):
     k_xq = quant(T.xq[:], T.xs[:], T.xt[:], d_x, k_x0)
     kp2 = pickq(T.rpq[:, 256:448], T.rtq[:], T.rto[:, 16:28])
     ks2 = picks(T.rps[:, 256:448], T.rts[:], T.rto[:, 16:28])
+    ms(T.eb1[0:32, :], 0.0)
+    ms(T.eb1[32:64, :], -EPS)
+    ms(T.eb1[64:96, :], EPS)
+    k_th = ms(T.eb1[96:128, :], 0.0)
     dm = []
     for j in range(3):
         mm(bank(j, 192), T.rpq[:, 0:128], T.rps[:, 0:128], T.xq[:, 0:192], T.xs[:, 0:192], True, False, kp1, ks1, k_xq)
@@ -164,22 +155,41 @@ def rank_program(g, core, T, topo):
         dj = (kp2, ks2) if j else ()
         dm.append(mm(bank(j, 192), T.rpq[:, a:a + 128], T.rps[:, a:a + 128], T.xq[:, 0:192], T.xs[:, 0:192], False, True, *dj))
     k_z1 = act(T.z1[:], bank(0, 192), AF.Identity, T.eb1[:], 1.0, dm[0], k_th)
-    k2 = tt(T.cm[:], T.qI[:, 0:8], T.b32[:], OP.add, kq)
-    k_cm = ts(T.cmn[:], T.cm[:], -1.0, -0.5, OP.mult, OP.add, k2)
+    ms(T.th1[0:64, :], -EPS / 2)
+    ms(T.th1[64:128, :], EPS / 2)
+    kr = ts(T.rI[:], T.pI[:], 15, None, OP.bitwise_and, None, k_g)
+    kq = ts(T.qI[:], T.pI[:], 31, None, OP.bitwise_and, None)
+    ms(T.zb[:], 0.0)
+    k1 = tt(T.cs[:], T.rI[:, 0:8], T.b16[:], OP.add, kr)
+    k_jk = ms(T.jkd[:, 192:193], -192.0)
+    k_jk = ms(T.jkd[:, 448:449], -192.0)
+    ts(T.csp[:], T.cs[:], 0.5, None, OP.add, None, k1)
+    k_cs = ts(T.csn[:], T.cs[:], -1.0, -0.5, OP.mult, OP.add)
     k = tt(T.z2[:], bank(1, 192), T.z1[:], OP.min, dm[1], k_z1)
+    k_lw = ms(T.lwho[:], -1.0)
     k_d1 = tt(T.z3[:], bank(2, 192), T.z2[:], OP.min, dm[2], k)
+    k2 = tt(T.cm[:], T.qI[:, 0:8], T.b32[:], OP.add, kq)
     k = ts(T.mk[:], T.z3[:], T.th1[:], None, OP.is_gt, None, k_d1)
+    k_mo = ms(T.msgo[:], 0.0)
     k_cum = scan(T.cum[:], T.mk[:], T.zb[:, 0:192], 0.0, OP.add, k)
+    send(near, T.cnte[:, 0:1], T.cum[:, 191:192], "ae", k_cum)
+    k_cm = ts(T.cmn[:], T.cm[:], -1.0, -0.5, OP.mult, OP.add, k2)
     k_a = [acc(T.jka[:, 192 * c:192 * c + 192], T.cum[:], AF.Sign, T.csn[:, c:c + 1], T.cnt1[:, c:c + 1], k_cum, k_cs) for c in range(3)]
     k3 = ts(T.jkd[:, 0:192], T.cum[:], T.csp[:, 3:4], 2.0, OP.is_gt, OP.mult, k_cum)
     k4 = ts(T.jkd[:, 256:448], T.cum[:], T.csp[:, 4:5], 2.0, OP.is_gt, OP.mult)
     ts(T.cnt1[:, 5:6], T.cum[:, 191:192], -2.0, 192.0, OP.mult, OP.add)
     red(T.cnt1[:, 3:4], T.jkd[:, 0:193], OP.add, k3, k_jk)
     k_c = red(T.cnt1[:, 4:5], T.jkd[:, 256:449], OP.add, k4)
+    k_mi = ms(T.msgi[:, 8 * rank:8 * rank + 8], 0.0)
     pk, psc, k_off = {}, {}, {}
-    for i, b in enumerate(order + [rank]):
+    seq = order + [rank]
+
+    def offs1(b):
         for q in range(N):
             k_off[b] = ts(T.off1[quad(q), 6 * b:6 * b + 6], T.cnt1[quad(b), 0:6], -0.5, 96.0, OP.mult, OP.add, k_c, k_a[-1])
+
+    offs1(seq[0])
+    for i, b in enumerate(seq):
         o, so = (T.sl1[:, 80 * i:80 * i + 80], T.ss1[:, 80 * i:80 * i + 80]) if b != rank else \
                 (T.land1[:, 80 * b:80 * b + 80], T.lans1[:, 80 * b:80 * b + 80])
         pk[b] = pickq(o, T.xq[:, 0:194], T.off1[:, 6 * b:6 * b + 5], k_off[b])
@@ -187,146 +197,181 @@ def rank_program(g, core, T, topo):
         if b != rank:
             send(b, c8(T.land1[:, 80 * rank:80 * rank + 80]), c8(T.sl1[:, 80 * i:80 * i + 80]), "arr%d" % rank, pk[b], k_lw)
             send(b, T.lans1[:, 80 * rank:80 * rank + 80], T.ss1[:, 80 * i:80 * i + 80], "arr%d" % rank, psc[b])
+            offs1(seq[i + 1])
     k_m = [acc(T.jka[:, 576 + 192 * c:768 + 192 * c], T.cum[:], AF.Sign, T.cmn[:, c:c + 1], T.cntm[:, c:c + 1], k_cm) for c in range(3)]
     m_v, m_a = {}, {}
-    for b in order + [rank]:
+    for b in seq:
         m, o = (T.msgo, 8 * b) if b != rank else (T.msgi, 8 * rank)
-        m_v[b] = cp(m[:, o + 1:o + 2], T.off1[:, 6 * b + 5:6 * b + 6], k_off[b], k_mo)
+        m_v[b] = cp(m[:, o + 1:o + 2], T.off1[:, 6 * b + 5:6 * b + 6], k_off[b], k_mo) if b != near else k_mo
         for c in range(3):
-            m_a[b] = act(m[quad(c), o:o + 1], T.cntm[quad(b), c:c + 1], AF.Copy, 96.0, -0.5, k_m[2], k_mo)
+            m_a[b] = act(m[quad(c), o:o + 1], T.cntm[quad(b), c:c + 1], AF.Copy, 96.0, -0.5, k_m[2], k_mo, k_mi)
         if b != rank:
-            send(b, T.msgi[:, 8 * rank:8 * rank + 2], T.msgo[:, o:o + 2], "am", m_v[b], m_a[b])
+            wd = 1 if b == near else 2
+            send(b, T.msgi[:, 8 * rank:8 * rank + wd], T.msgo[:, o:o + wd], "am", m_v[b], m_a[b])
 
     k_oz = ms(T.ozero[:], TOK)
+    k_wq = quant(T.wq[:], T.wsc[:], T.wt[:], d_w)
     k_z = pickq(T.land1[:, NX:XC], T.xq[:, 0:194], T.ozero[:, 0:1], k_xq, k_oz)
     k_zs = picks(T.lans1[:, NX:XC], T.xs[:, 0:194], T.ozero[:, 0:1], k_z)
-    k_wq = quant(T.wq[:], T.wsc[:], T.wt[:], d_w)
     ms(T.r2t[:, 40:512], 0.0)
     k = ts(T.r2t[:, 20:40], T.r2t[:, 0:20], -1.0, None, OP.mult, None, d_r2)
-    k_r2q = quant(T.r2q[:], T.r2s[:], T.r2t[:], k)
     srt = sorted(others)
     one = {srt[0]: srt[1], srt[1]: srt[0], srt[2]: srt[0], rank: 0}
     two = {srt[0]: srt[2], srt[1]: srt[2], srt[2]: srt[1], rank: 0}
-    blocks = [0, 1, 2, 3] + [5 + one[q] for q in range(N)] + [5 + two[q] for q in range(N)] + [4] * 4
-    for c in range(16):
-        k_o = ms(T.r2o[:, 2 * c:2 * c + 2], blocks[c])
+    blocks = [0, 1, 2, 3] + [5 + one[q] for q in range(N)] + [5 + two[q] for q in range(N)]
+    for c in range(12):
+        ms(T.r2o[:, 2 * c:2 * c + 2], blocks[c])
+    k_o = ms(T.r2o[:, 24:32], 4)
+    k_r2q = quant(T.r2q[:], T.r2s[:], T.r2t[:], k)
+    k_z2 = pickq(T.land2[:, 192:208], T.xq[:, 0:194], T.ozero[:, 0:1], k_xq)
+    k_z2s = picks(T.lans2[:, 192:208], T.xs[:, 0:194], T.ozero[:, 0:1], k_z2)
     k_r2p = pickq(T.r2p[:], T.r2q[:], T.r2o[:], k_o, k_r2q)
     k_r2s = picks(T.r2ps[:], T.r2s[:], T.r2o[:], k_o, k_r2q)
-    k_z2 = pickq(T.land2[:, 64 * rank:64 * rank + 64], T.xq[:, 0:194], T.ozero[:], k_xq)
-    k_z2s = picks(T.lans2[:, 64 * rank:64 * rank + 64], T.xs[:, 0:194], T.ozero[:], k_z2)
-    k_vx = quant(T.vxq[:], T.vxs[:], T.vxt[:], d_vx)
-    k_vh = quant(T.vhq[:], T.vhs[:], T.vht[:], d_vh)
     for q in range(N):
-        ms(T.th2[quad(q), :], -EPS / 2 if q == srt[2] else EPS / 2)
-        k_t2 = ms(T.eb2[quad(q), :], -EPS if q == srt[1] else 0.0)
-    ms(T.zf[:], 0.0)
-    ms(T.cap[:], 64 * STEP)
-    k_je = ms(T.jke[:, 320:321], -320.0)
+        ms(T.eb2[quad(q), :], EPS / 2 if one[q] > q else -EPS / 2)
+        k_t2 = ms(T.th2[quad(q), :], EPS / 2 if two[q] > q else -EPS / 2)
     k_num = ms(T.num[:], -1.0)
-    k = ts(T.ofi[:], T.bfin[:], 32.0, None, OP.add, None, k_fin)
-    k = tt(T.ofi[:], T.rI[:, 0:8], T.ofi[:], OP.add, k)
-    k_ofin = cp(T.ofin[:], T.ofi[:], k)
+    for q in range(N):
+        k_cq = cp(T.cntq[quad(q), 0:1], T.cnte[quad(rank), 0:1], ("ae", arrivals([near], 1)))
+    am = ("am", arrivals(others, 1))
+
+    def absent(s, cn, *dep):
+        return ts(T.inv[:, 80 * s:80 * s + 80], T.i80[:], cn, BIG, OP.is_ge, OP.mult, k_80, *dep)
+
+    absent(rank, T.msgi[:, 8 * rank + 1:8 * rank + 2], m_v[rank])
+    ki0 = absent(near, T.cntq[:, 0:1], k_cq)
 
     arr = lambda s: ("arr%d" % s, arrivals([s], 2))
     home = (pk[rank], psc[rank])
     halves = [(0, NH, [0, 1]), (NH, NX + 2, [2, 3])]
-    W = []
-    for h, (c0, c1, who) in enumerate(halves):
+    if rank >= 2:
+        halves.reverse()
+    H = lambda a, b: (T.xw[:, HB + a:HB + b], T.xws[:, HB + a:HB + b])
+    P = lambda k: (T.r2p[:, 128 * k:128 * k + 128], T.r2ps[:, 128 * k:128 * k + 128])
+    f0, g0 = halves[0][0], halves[1][0]
+    F, G = slice(f0, f0 + NH), slice(g0, g0 + NH)
+    blk = [0, 128, 192] if f0 == 0 else [192, 0, 64]
+
+    def products(h):
+        c0, c1, who = halves[h]
         deps = [arr(s) for s in who if s != rank] + list(home) + [k_z, k_zs, k_wq, k_d1, k_z1]
-        W.append([mm(bank(4 * h + i, c1 - c0), T.wq[:, 128 * i:128 * i + 128], T.wsc[:, 128 * i:128 * i + 128], T.land1[:, c0:c1], T.lans1[:, c0:c1], True, True, *deps) for i in range(4)])
-    kq_h = []
-    for h, (c0, c1, who) in enumerate(halves):
+        return [mm(bank(4 * h + i, c1 - c0), T.wq[:, 128 * i:128 * i + 128], T.wsc[:, 128 * i:128 * i + 128], T.land1[:, c0:c1], T.lans1[:, c0:c1], True, True, *deps) for i in range(4)]
+
+    def tile(h, W):
+        c0, c1, who = halves[h]
         hv = lambda i: T.hb[:, 4 * c0 + i:4 * c1:4]
-        k0 = act(hv(0), bank(4 * h, c1 - c0), AF.Relu, 0.0, 0.0625, W[h][0])
-        k1 = ts(hv(1), bank(4 * h + 1, c1 - c0), 0.0, 0.0625, OP.max, OP.mult, W[h][1])
-        k2 = act(hv(2), bank(4 * h + 2, c1 - c0), AF.Relu, 0.0, 0.0625, W[h][2])
-        k3 = ts(hv(3), bank(4 * h + 3, c1 - c0), 0.0, 0.0625, OP.max, OP.mult, W[h][3])
-        kq_h.append(quant(T.xw[:, HB + c0:HB + c1], T.xws[:, HB + c0:HB + c1], T.hb[:, 4 * c0:4 * c1], k0, k1, k2, k3))
+        k0 = act(hv(0), bank(4 * h, c1 - c0), AF.Relu, 0.0, 0.0625, W[0])
+        k1 = ts(hv(1), bank(4 * h + 1, c1 - c0), 0.0, 0.0625, OP.max, OP.mult, W[1])
+        k2 = act(hv(2), bank(4 * h + 2, c1 - c0), AF.Relu, 0.0, 0.0625, W[2])
+        k3 = ts(hv(3), bank(4 * h + 3, c1 - c0), 0.0, 0.0625, OP.max, OP.mult, W[3])
+        return quant(T.xw[:, HB + c0:HB + c1], T.xws[:, HB + c0:HB + c1], T.hb[:, 4 * c0:4 * c1], k0, k1, k2, k3)
+
+    def diff(k, j, c0, *d):
+        mm(bank(k, NH), *P(0), *H(c0, c0 + NH), True, False, *d)
+        return mm(bank(k, NH), *P(j), *H(c0, c0 + NH), False, True)
+
+    W0 = products(0)
+    kq0 = tile(0, W0)
+    W1 = products(1)
+    k_vx = quant(T.vxq[:], T.vxs[:], T.vxt[:], d_vx)
+    k_vh = quant(T.vhq[:], T.vhs[:], T.vht[:], d_vh)
+    kq1 = tile(1, W1)
     alla = [arr(s) for s in range(N) if s != rank]
     dma("s", "dxw", c8(T.xw[:, 0:XC]), c8(T.land1[:]), *alla, *home, k_z, k_zs)
     d_xw = dma("s", "dxw", T.xws[:, 0:XC], T.lans1[:])
-    am = ("am", arrivals(others, 1))
     for s in range(N):
         d_nb = dma("s", "dnb", T.nb[0:1, 80 * s:80 * s + 80], T.msgi[0:80, 8 * s:8 * s + 1], am, m_v[rank], m_a[rank])
 
-    H = lambda a, b: (T.xw[:, HB + a:HB + b], T.xws[:, HB + a:HB + b])
-    P = lambda k: (T.r2p[:, 128 * k:128 * k + 128], T.r2ps[:, 128 * k:128 * k + 128])
-    ea = mm(bank(0, NH), *P(3), *H(0, NH), True, True, kq_h[0], k_r2p, k_r2s, k_r2q)
-    e0 = mm(bank(1, 128), *H(0, 128), T.r2q[:], T.r2s[:], True, True)
-    mm(bank(2, NH), *P(0), *H(0, NH), True, False)
-    fa = mm(bank(2, NH), *P(1), *H(0, NH), False, True)
-    eb = mm(bank(4, NH), *P(3), *H(NH, NX), True, True, kq_h[1])
-    e1 = mm(bank(5, 128), *H(128, 256), T.r2q[:], T.r2s[:], True, True)
-    e2 = mm(bank(6, 128), *H(192, 320), T.r2q[:], T.r2s[:], True, True)
-    mm(bank(7, NH), *P(0), *H(NH, NX), True, False)
-    fb = mm(bank(7, NH), *P(1), *H(NH, NX), False, True)
-    mm(bank(3, NX), *P(0), *H(0, NX), True, False)
-    f2 = mm(bank(3, NX), *P(2), *H(0, NX), False, True)
     e4 = lambda k: T.ps[:, 512 * k + 4:512 * k + 5]
+    ea = mm(bank(0, NH), *P(3), *H(f0, f0 + NH), True, True, kq0, k_r2p, k_r2s, k_r2q)
+    e0 = mm(bank(1, 128), *H(blk[0], blk[0] + 128), T.r2q[:], T.r2s[:], True, True)
     ken0 = act(T.en[:, 0:1], e4(1), AF.Copy, 0.0, 1.0, e0)
-    act(T.y1[:, 0:NH], bank(2, NH), AF.Identity, T.eb2[:], 1.0, fa, k_t2)
-    ken1 = act(T.en[:, 1:2], e4(5), AF.Copy, 0.0, 1.0, e1)
+    if EARLY > 1:
+        f1a = diff(2, 1, f0)
+    eb = mm(bank(4, NH), *P(3), *H(g0, g0 + NH), True, True, kq1)
+    e2 = mm(bank(6, 128), *H(blk[2], blk[2] + 128), T.r2q[:], T.r2s[:], True, True)
+    e1 = mm(bank(5, 128), *H(blk[1], blk[1] + 128), T.r2q[:], T.r2s[:], True, True)
+    if EARLY <= 1:
+        f1a = diff(2, 1, f0)
+    f2a = diff(3, 2, f0)
+    f1b = diff(7, 1, g0)
+    f2b = diff(1, 2, g0, ken0)
     ken2 = act(T.en[:, 2:3], e4(6), AF.Copy, 0.0, 1.0, e2)
-    k_y1 = act(T.y1[:, NH:NX], bank(7, NH), AF.Identity, T.eb2[:], 1.0, fb)
-    for s in range(N):
-        ki = ts(T.inv[:, 80 * s:80 * s + 80], T.i80[:], T.msgi[:, 8 * s + 1:8 * s + 2], BIG, OP.is_ge, OP.mult, k_80, am, m_v[rank])
-    tt(T.em[:, 0:NH], bank(0, NH), T.inv[:, 0:NH], OP.add, ea, ki)
-    k_em = tt(T.em[:, NH:NX], bank(4, NH), T.inv[:, NH:NX], OP.add, eb)
+    ken1 = act(T.en[:, 1:2], e4(5), AF.Copy, 0.0, 1.0, e1)
+    tt(T.em[:, F], bank(0, NH), T.inv[:, F], OP.add, ea, ki0)
+    for s in others:
+        if s != near:
+            ki = absent(s, T.msgi[:, 8 * s + 1:8 * s + 2], am)
+    k_em = tt(T.em[:, G], bank(4, NH), T.inv[:, G], OP.add, eb, ki)
+    ms(T.zf[:], 0.0)
     kc0 = ts(T.jk2[:, 0:320], T.em[:], T.en[:, 0:1], None, OP.is_lt, None, k_em, ken0)
     kc1 = ts(T.jk2[:, 320:640], T.em[:], T.en[:, 1:2], None, OP.is_lt, None, ken1)
     k = act(T.jk2[:, 640:960], T.em[:], AF.Sign, T.en[:, 2:3], -1.0, k_em, ken2)
-    kl0 = acc(T.jkb[:, 0:320], T.jk2[:, 0:320], AF.Copy, 0.0, T.lt[:, 0:1], kc0)
     kl2 = acc(T.jkb[:, 320:640], T.jk2[:, 640:960], AF.Relu, 0.0, T.lt[:, 2:3], k)
-    kl1 = red(T.lt[:, 1:2], T.jk2[:, 320:640], OP.add, kc1)
-    k_y2 = tt(T.y2[:], bank(3, NX), T.y1[:], OP.min, f2, k_y1)
-    k = act(T.sn[:], T.y2[:], AF.Sign, T.th2[:], 1.0, k_y2)
-    k_ns = act(T.ns[:], T.sn[:], AF.Relu, 0.0, -BIG, k)
-    for s in range(N):
-        k_n = act(T.num[0:1, 80 * s:80 * s + 80], T.nb[0:1, 80 * s:80 * s + 80], AF.Copy, float(TOK * s), 1.0, d_nb, k_num)
-    kp = ts(T.pen[:, 0:3], T.lt[:, 0:3], DF - 0.5, LOW, OP.is_ge, OP.mult, kl0, kl1, kl2)
+    scan(T.jkc[:, 0:320], T.jk2[:, 0:320], T.zb[:], 0.0, OP.add, kc0)
+    k = scan(T.jkc[:, 320:640], T.jk2[:, 320:640], T.zb[:], 0.0, OP.add, kc1)
+    ms(T.khb[:, 0:1], 0.0)
+    cp(T.lt[:, 0:2], T.jkc[:, 319:640:320], k)
+    ts(T.pen[:, 0:2], T.jkc[:, 319:640:320], DF - 0.5, LOW, OP.is_ge, OP.mult)
+    kp = ts(T.pen[:, 2:3], T.lt[:, 2:3], DF - 0.5, LOW, OP.is_ge, OP.mult, kl2)
+    ms(T.khb[:, 1:2], -2.0 * HB)
+    act(T.s1[:, F], bank(2, NH), AF.Sign, T.eb2[:], 1.0, f1a, k_t2)
+    act(T.s2[:, F], bank(3, NH), AF.Sign, T.th2[:], 1.0, f2a)
+    act(T.s1[:, G], bank(7, NH), AF.Sign, T.eb2[:], 1.0, f1b)
+    k = act(T.s2[:, G], bank(1, NH), AF.Sign, T.th2[:], 1.0, f2b)
+    k_cc = act(T.c2[:], T.s2[:], AF.Copy, 4.0, -1.0, k)
     for k in range(3):
         ts(T.bc[:, 32 * k:32 * k + 32], T.zf[:], T.en[:, k:k + 1], T.pen[:, k:k + 1], OP.add, OP.add, kp)
         kc = ts(T.bc[:, 96 + 32 * k:128 + 32 * k], T.zf[:], T.lt[:, k:k + 1], T.pen[:, k:k + 1], OP.add, OP.add)
     kc = op("v", lambda e: e.transpose(T.bt[:], T.bc[:]), kc)
-    k_eb = tt(T.emb[:], T.em[:], T.ns[:], OP.add, k_ns)
+    ms(T.ys[:, CB * rank:CB * rank + CB], 0.0)
     red(T.qm[:, 0:1], T.bt[:, 0:96], OP.max, kc)
     kc = red(T.qm[:, 1:2], T.bt[:, 96:192], OP.max)
+    ms(T.ofin[:, 2 * rank:2 * rank + 2], 192)
     tt(T.g4[0:64, :], T.qm[0:64, :], T.qm[64:128, :], OP.max, kc)
     kc = tt(T.g4[64:128, :], T.qm[64:128, :], T.qm[0:64, :], OP.max)
     for q in range(N):
         k = tt(T.tl[quad(q), :], T.g4[quad(q), :], T.g4[quad(q ^ 1), :], OP.max, kc)
-    k_sg = act(T.sg[:], T.emb[:], AF.Sign, T.tl[:, 0:1], -1.0, k, k_eb)
-    k_gd = ts(T.gd[:], T.em[:], T.tl[:, 0:1], STEP, OP.is_equal, OP.mult, k)
-    k_i = ts(T.ini[:], T.tl[:, 1:2], DF + 0.5, STEP, OP.subtract, OP.mult)
-    k = scan(T.nq[:], T.gd[:], T.cap[:], T.ini[:], OP.min, k_i)
-    k = tt(T.mk2[:], T.sg[:], T.nq[:], OP.is_gt, k, k_sg)
+    k_uw = elem(T.uw[:], T.s1[:], T.c2[:], OP.subtract, k_cc)
+    k_sg = act(T.sg[:], T.em[:], AF.Sign, T.tl[:, 0:1], -1.0, k)
+    for s in range(N):
+        k_n = act(T.num[0:1, 80 * s:80 * s + 80], T.nb[0:1, 80 * s:80 * s + 80], AF.Copy, float(TOK * s), 1.0, d_nb, k_num)
+    k_gd = ts(T.gd[:], T.em[:], T.tl[:, 0:1], None, OP.is_equal, None, k)
+    k_t1 = elem(T.t1[:], T.sg[:], T.uw[:], OP.add, k_sg, k_uw)
+    k_nq = scan(T.nq[:], T.gd[:], T.zb[:], T.tl[:, 1:2], OP.add, k_gd)
+    k = ts(T.nf[:], T.nq[:], DF + 0.5, 6.0, OP.is_gt, OP.add, k_nq)
+    k = elem(T.t2[:], T.t1[:], T.nf[:], OP.subtract, k, k_t1)
+    k = ts(T.mk2[:], T.t2[:], -8.5, None, OP.is_gt, None, k)
     k_c2 = scan(T.cum2[:], T.mk2[:], T.zb[:], 0.0, OP.add, k)
-    ka = acc(T.jkb[:, 640:960], T.cum2[:], AF.Sign, T.csn[:, 0:1], T.cnt2[:, 0:1], k_c2)
+    ka = acc(T.jkb[:, 640:960], T.cum2[:], AF.Sign, T.csn[:, 0:1], T.ac[:, 0:1], k_c2)
     k = ts(T.jke[:, 0:320], T.cum2[:], T.csp[:, 1:2], 2.0, OP.is_gt, OP.mult, k_c2)
-    k = red(T.cnt2[:, 1:2], T.jke[:, 0:321], OP.add, k)
-    kc = ts(T.cnt2[:, 2:4], T.cnt2[:, 0:2], -2.0 * HB, None, OP.add, None, k, ka)
+    k = scan(T.jke[:, 320:640], T.jke[:, 0:320], T.zb[:], -320.0, OP.add, k)
+    ts(T.cnt2[:, 0:4:2], T.khb[:], T.ac[:, 0:1], None, OP.add, None, ka)
+    kc = ts(T.cnt2[:, 1:4:2], T.khb[:], T.jke[:, 639:640], None, OP.add, None, k)
     for i, b in enumerate(order):
         for q in range(N):
             ko = ts(T.off2[quad(q), 4 * i:4 * i + 4], T.cnt2[quad(b), 0:4], -0.5, NX / 2.0, OP.mult, OP.add, kc)
         o = slice(64 * i, 64 * i + 64)
         kk = pickq(T.sl2[:, o], T.xw[:], T.off2[:, 4 * i:4 * i + 4], ko, d_xw)
         ks = picks(T.ss2[:, o], T.xws[:], T.off2[:, 4 * i:4 * i + 4], ko, d_xw)
-        d = slice(64 * rank, 64 * rank + 64)
+        kw = op("a", lambda e: e.activation(T.wg[:, 32 * i:32 * i + 32], T.num[:].indirect(T.off2[:, 4 * i:4 * i + 2]), AF.Copy), k_n)
+        d = slice(64 * slot(rank, b), 64 * slot(rank, b) + 64)
         send(b, c8(T.land2[:, d]), c8(T.sl2[:, o]), "arrb", kk)
         send(b, T.lans2[:, d], T.ss2[:, o], "arrb", ks)
-    for i in range(3):
-        kw = op("a", lambda e: e.activation(T.wg[:, 32 * i:32 * i + 32], T.num[:].indirect(T.off2[:, 4 * i:4 * i + 2]), AF.Copy), k_n)
     kw = op("v", lambda e: e.transpose(T.wtr[:], T.wg[:]), kw)
     for i, b in enumerate(order):
         send(b, T.lwho[:, rank:rank + 1], T.wtr[:, 32 * i:32 * i + 1], "aw", kw)
+    for a in others:
+        k_ofin = ts(T.ofin[:, 2 * a:2 * a + 2], T.cs[:, 0:2], 64.0 * slot(a, rank) + CB, None, OP.add, None)
 
     ab = ("arrb", arrivals(others, 2))
-    mm(bank(5, 224), T.vxq[:], T.vxs[:], T.land2[:, 0:224], T.lans2[:, 0:224], True, False, ab, k_z2, k_z2s, k_vx, k_vh, ken1)
-    ty = mm(bank(5, 224), T.vhq[:], T.vhs[:], T.land2[:, 32:256], T.lans2[:, 32:256], False, True)
-    kf = pickq(T.fin[:], T.land2[:], T.ofin[:], ab, k_ofin)
-    kfs = picks(T.fins[:], T.lans2[:], T.ofin[:], ab, k_ofin)
-    for a in range(N):
-        ky = cp(T.ys[:, CB * a:CB * a + CB], T.ps[:, 2560 + 64 * a:2560 + 64 * a + CB], ty)
+    mm(bank(5, 160), T.vxq[:], T.vxs[:], T.land2[:, 0:160], T.lans2[:, 0:160], True, False, ab, k_vx, k_vh, ken1)
+    ty = mm(bank(5, 160), T.vhq[:], T.vhs[:], T.land2[:, 32:192], T.lans2[:, 32:192], False, True)
+    kf = pickq(T.fin[:], T.land2[:], T.ofin[:], ab, k_ofin, k_z2)
+    kfs = picks(T.fins[:], T.lans2[:], T.ofin[:], ab, k_ofin, k_z2s)
+    for a in others:
+        c0 = 2560 + 64 * slot(a, rank)
+        ky = cp(T.ys[:, CB * a:CB * a + CB], T.ps[:, c0:c0 + CB], ty)
     dma("s", "dout", T.oc[:], c8(T.fin[:]), kf)
     for k in range(4):
         dma("s" if k < 2 else "a", "dout", T.osc[4 * k:4 * k + 4, :], T.fins[32 * k:32 * k + 4, :], kfs)

@@ -4,56 +4,25 @@ N, TOK, CAP, CB, DF = 4, 192, 80, 32, 80
 NX = N * CAP
 NH = NX // 2
 XC = 336
-HB = 352
-EPS, BIG, LOW = 1e-30, 1e29, -9e29
-RTB = [0, 1, 2, 3, 5, 4, 7, 6, 5, 4, 6, 7, 4, 5]
-RTS = [4, 6, 10]
-
-SCRATCH = {
-    "rtt": ("sbuf", [128, 512], "bfloat16"), "rtq": ("sbuf", [128, 128], "float8_e4m3fn_x4"), "rts": ("sbuf", [128, 128], "uint8"),
-    "rpq": ("sbuf", [128, 448], "float8_e4m3fn_x4"), "rps": ("sbuf", [128, 448], "uint8"), "rto": ("sbuf", [128, 28], "uint16"),
-    "xt": ("sbuf", [128, 776], "bfloat16"), "xq": ("sbuf", [128, 194], "float8_e4m3fn_x4"), "xs": ("sbuf", [128, 194], "uint8"),
-    "wt": ("sbuf", [128, 2048], "bfloat16"), "wq": ("sbuf", [128, 512], "float8_e4m3fn_x4"), "wsc": ("sbuf", [128, 512], "uint8"),
-    "r2t": ("sbuf", [128, 512], "bfloat16"), "r2q": ("sbuf", [128, 128], "float8_e4m3fn_x4"), "r2s": ("sbuf", [128, 128], "uint8"),
-    "r2p": ("sbuf", [128, 512], "float8_e4m3fn_x4"), "r2ps": ("sbuf", [128, 512], "uint8"), "r2o": ("sbuf", [128, 32], "uint16"),
-    "vxt": ("sbuf", [128, 512], "bfloat16"), "vxq": ("sbuf", [128, 128], "float8_e4m3fn_x4"), "vxs": ("sbuf", [128, 128], "uint8"),
-    "vht": ("sbuf", [128, 512], "bfloat16"), "vhq": ("sbuf", [128, 128], "float8_e4m3fn_x4"), "vhs": ("sbuf", [128, 128], "uint8"),
-    "hb": ("sbuf", [128, 4 * (NX + 2)], "bfloat16"),
-    "sl1": ("sbuf", [128, 240], "float8_e4m3fn_x4"), "ss1": ("sbuf", [128, 240], "uint8"),
-    "land1": ("sbuf", [128, XC], "float8_e4m3fn_x4"), "lans1": ("sbuf", [128, XC], "uint8"),
-    "msgo": ("sbuf", [128, 32], "bfloat16"), "msgi": ("sbuf", [128, 32], "bfloat16"),
-    "cnte": ("sbuf", [128, 8], "bfloat16"), "cntq": ("sbuf", [128, 8], "bfloat16"),
-    "xw": ("sbuf", [128, 704], "float8_e4m3fn_x4"), "xws": ("sbuf", [128, 704], "uint8"),
-    "sl2": ("sbuf", [128, 192], "float8_e4m3fn_x4"), "ss2": ("sbuf", [128, 192], "uint8"),
-    "land2": ("sbuf", [128, 208], "float8_e4m3fn_x4"), "lans2": ("sbuf", [128, 208], "uint8"),
-    "fin": ("sbuf", [128, 128], "float8_e4m3fn_x4"), "fins": ("sbuf", [128, 128], "uint8"),
-    "lwho": ("sbuf", [128, 32], "float32"), "whot": ("sbuf", [128, 32], "float32"),
-    "z1": ("sbuf", [128, 192], "float32"), "z2": ("sbuf", [128, 192], "float32"), "z3": ("sbuf", [128, 192], "float32"),
-    "mk": ("sbuf", [128, 192], "bfloat16"), "cum": ("sbuf", [128, 192], "bfloat16"), "zb": ("sbuf", [128, 320], "bfloat16"), "zf": ("sbuf", [128, 32], "float32"),
-    "jka": ("sbuf", [128, 1152], "bfloat16"), "jkd": ("sbuf", [128, 512], "bfloat16"),
-    "cnt1": ("sbuf", [128, 8], "float32"), "cntm": ("sbuf", [128, 4], "float32"), "off1": ("sbuf", [128, 24], "uint16"), "ozero": ("sbuf", [128, 4], "uint16"),
-    "inv": ("sbuf", [128, 320], "float32"), "em": ("sbuf", [128, 320], "float32"),
-    "s1": ("sbuf", [128, 320], "bfloat16"), "s2": ("sbuf", [128, 320], "bfloat16"), "c2": ("sbuf", [128, 320], "bfloat16"), "uw": ("sbuf", [128, 320], "bfloat16"),
-    "gd": ("sbuf", [128, 320], "bfloat16"), "nq": ("sbuf", [128, 320], "bfloat16"), "sg": ("sbuf", [128, 320], "bfloat16"),
-    "nf": ("sbuf", [128, 320], "bfloat16"), "t1": ("sbuf", [128, 320], "bfloat16"), "t2": ("sbuf", [128, 320], "bfloat16"),
-    "mk2": ("sbuf", [128, 320], "bfloat16"), "cum2": ("sbuf", [128, 320], "bfloat16"),
-    "jk2": ("sbuf", [128, 960], "bfloat16"), "jkb": ("sbuf", [128, 960], "bfloat16"), "jke": ("sbuf", [128, 640], "bfloat16"), "jkc": ("sbuf", [128, 640], "bfloat16"),
-    "en": ("sbuf", [128, 4], "float32"), "lt": ("sbuf", [128, 4], "float32"), "pen": ("sbuf", [128, 4], "float32"),
-    "bc": ("sbuf", [128, 192], "float32"), "bt": ("sbuf", [128, 192], "float32"), "qm": ("sbuf", [128, 2], "float32"),
-    "g4": ("sbuf", [128, 2], "float32"), "tl": ("sbuf", [128, 2], "float32"), "khb": ("sbuf", [128, 2], "float32"), "ac": ("sbuf", [128, 2], "float32"),
-    "cnt2": ("sbuf", [128, 4], "float32"), "off2": ("sbuf", [128, 12], "uint16"),
-    "nb": ("sbuf", [128, 320], "bfloat16"), "num": ("sbuf", [128, XC], "float32"), "wg": ("sbuf", [128, 96], "float32"), "wtr": ("sbuf", [128, 96], "float32"),
-    "ys": ("sbuf", [128, 128], "float32"),
-    "th1": ("sbuf", [128, 1], "float32"), "eb1": ("sbuf", [128, 1], "float32"), "th2": ("sbuf", [128, 1], "float32"), "eb2": ("sbuf", [128, 1], "float32"),
-    "pI": ("sbuf", [128, 16], "int32"), "rI": ("sbuf", [128, 16], "int32"), "qI": ("sbuf", [128, 16], "int32"),
-    "b16": ("sbuf", [128, 8], "int32"), "b32": ("sbuf", [128, 8], "int32"),
-    "cs": ("sbuf", [128, 8], "float32"), "csp": ("sbuf", [128, 8], "float32"), "csn": ("sbuf", [128, 8], "float32"), "cm": ("sbuf", [128, 8], "float32"), "cmn": ("sbuf", [128, 8], "float32"),
-    "i80": ("sbuf", [128, 80], "float32"), "ofin": ("sbuf", [128, 8], "uint16"),
-    "ps": ("psum", [128, 4096], "float32"),
-}
-SEMAPHORES = ["v", "a", "t", "gq", "dx", "drt", "dw", "dr2", "dvx", "dvh", "dxw", "dnb", "dout", "ls",
-              "arr0", "arr1", "arr2", "arr3", "am", "ae", "arrb", "aw"]
-EARLY = 2
+TINY, BIG, LOW, K = 1e-33, 1e29, -9e29, 2.0 ** 80
+PI = [1, 0, 2, 3]
+E4, NRT, NR2 = 4, 4, 5
+Q8, U8, BF, F32 = "float8_e4m3fn_x4", "uint8", "bfloat16", "float32"
+SCRATCH = {"ps": ("psum", [128, 4096], F32)}
+for _d, _l in (
+        (Q8, dict(rtq=128, r2q=128, rpq=320, r2p=352, xq=194, wq=512, vxq=128, vhq=128, hq=XC, sl1=240, land1=XC, sl2=192, land2=208, fin=128)),
+        (U8, dict(rts=128, r2s=128, rps=320, r2ps=352, xs=194, wsc=512, vxs=128, vhs=128, hs=XC, ss1=240, lans1=XC, ss2=192, lans2=208, fins=128)),
+        (BF, dict(rtt=512, r2t=512, xt=776, wt=2048, vxt=512, vht=512, hb=4 * (NX + 2), mo=24, msgi=32, cnte=8, z1=192, mk=192, cum=192,
+                  jka=384, jkd=576, jkf=576, s1=NX, s2=NX, c2=NX, uw=NX, gd=NX, nq=NX, sg=NX, nf=NX, t1=NX, t2=NX, mk2=NX, cum2=NX,
+                  jk2=960, jkb=640, jke=640, jkc=640, nb=NX)),
+        (F32, dict(offf=24, diag=24, ib=2, lwho=32, whot=32, z2=192, z3=192, cnt1=8, inv=NX, em=NX, en=4, lt=4, ck=32, bc=96, bt=96, gm=96,
+                   tl=1, sa=1, sb=1, fit=1, cnt2=2, num=XC, wg=96, wtr=96, ys=128, th1=1, eb1=1, th2=1, eb2=1, p2=1, pa=1, rf=1,
+                   b16=8, csp=8, csn=8, i80=80)),
+        ("int32", dict(ti=44, pI=1, rI=1)), ("uint16", dict(to=44, off1=24, off2=6, ofin=8))):
+    for _n, _w in _l.items():
+        SCRATCH[_n] = ("sbuf", [128, _w], _d)
+SEMAPHORES = ["v", "a", "t", "gq", "dx", "drt", "dw", "dr2", "dvx", "dvh", "dnb", "dout", "ls",
+              "arr0", "arr1", "arr2", "arr3", "am", "an", "ae", "arrb", "aw"]
 
 
 def rank_program(g, core, T, topo):
@@ -65,6 +34,8 @@ def rank_program(g, core, T, topo):
     others = [(rank + 1 + k) % N for k in range(N - 1)]
     near = rank ^ 1
     order = sorted(others, key=lambda b: (b != near, topo.same_plane(topo.chip(cores[b]), me_chip)))
+    far = sorted(order[1:])
+    srt = sorted(others)
     slot = lambda a, b: sorted(r for r in range(N) if r != b).index(a)
     eng = {"v": g.vector, "a": g.scalar, "t": g.tensor, "s": g.sync, "g": g}
     semof = {"v": "v", "a": "a", "t": "t", "g": "gq"}
@@ -104,12 +75,12 @@ def rank_program(g, core, T, topo):
     ts = lambda out, x, s1, s2, o0, o1, *d: op("v", lambda e: e.tensor_scalar(out, x, s1, s2, o0) if o1 is None else e.tensor_scalar(out, x, s1, s2, o0, o1), *d)
     tt = lambda out, x, y, o, *d: op("v", lambda e: e.tensor_tensor(out, x, y, o), *d)
     cp = lambda out, x, *d: op("v", lambda e: e.tensor_copy(out, x), *d)
-    red = lambda out, x, o, *d: op("v", lambda e: e.tensor_reduce(out, x, AxisListType.X, o), *d)
-    scan = lambda out, x, y, i, o, *d: op("v", lambda e: e.tensor_tensor_scan(out, x, y, i, OP.add, o), *d)
-    elem = lambda out, x, y, o, *d: op("v", lambda e: e.tensor_tensor_scan(out, x, y, -64.0, OP.max, o), *d)
+    scan = lambda out, x, y, i, o0, o1, *d: op("v", lambda e: e.tensor_tensor_scan(out, x, y, i, o0, o1), *d)
+    elem = lambda out, x, y, o, *d: scan(out, x, y, -64.0, OP.max, o, *d)
+    run = lambda out, x, p, n, i, *d: scan(out, x, T.rtt[0:p, 32:32 + n], i, OP.add, OP.add, *d)
     quant = lambda q, s, x, *d: op("v", lambda e: e.quantize_mx(q, s, x), *d)
     act = lambda out, x, f, b, s, *d: op("a", lambda e: e.activation(out, x, f, bias=b, scale=s), *d)
-    acc = lambda out, x, f, b, o, *d: op("a", lambda e: e.activation(out, x, f, bias=b, scale=1.0, accum_out=o), *d)
+    acc = lambda out, x, f, b, s, o, *d: op("a", lambda e: e.activation(out, x, f, bias=b, scale=s, accum_out=o), *d)
     pickq = lambda out, win, off, *d: op("v", lambda e: e.tensor_copy(out.bitcast(u32), win.bitcast(u32).indirect(off)), *d)
     picks = lambda out, win, off, *d: op("a", lambda e: e.activation(out, win.indirect(off), AF.Copy), *d)
     quad = lambda q: slice(32 * q, 32 * q + 32)
@@ -122,135 +93,121 @@ def rank_program(g, core, T, topo):
     d_x = dma("s", "dx", T.xt[:, 0:768], T.x[:])
     d_w = dma("s", "dw", T.wt[:], T.w[:], d_x)
     d_r2 = dma("s", "dr2", T.r2t[:, 0:20], T.r2[:, 0:20])
-    d_vx = dma("s", "dvx", T.vxt[:], T.vx[:])
-    d_vh = dma("s", "dvh", T.vht[:], T.vh[:])
 
-    gi = lambda out, pat, cmul: op("g", lambda e: e.iota(out, pat, 0, cmul))
-    gi(T.pI[:], [[0, 16]], 1)
-    gi(T.b16[:], [[16, 8]], 0)
-    k_g = gi(T.b32[:], [[32, 8]], 0)
-    k_80 = op("g", lambda e: e.iota(T.i80[:], [[1, 80]], 0, 0, allow_small_or_imprecise_dtypes=True))
-    ms(T.rtt[:, 32:512], 0.0)
-    c = 0
-    while c < len(RTB):
-        k_rto = ms(T.rto[:, 2 * c:2 * c + 2], RTB[c])
-        c += 1
+    gi = lambda out, pat, base, cmul: op("g", lambda e: e.iota(out, pat, base, cmul))
+    gf = lambda out, pat, base, cmul, *d: op("g", lambda e: e.iota(out, pat, base, cmul, allow_small_or_imprecise_dtypes=True), *d)
+
+    def table(c, vals):
+        j = 0
+        while j < len(vals):
+            n = 2
+            while j + n < len(vals) and vals[j + n] - vals[j + n - 1] == vals[j + 1] - vals[j]:
+                n += 1
+            n = min(n, len(vals) - j)
+            k = gi(T.ti[:, c + 2 * j:c + 2 * j + 2 * n], [[vals[j + 1] - vals[j] if n > 1 else 0, n], [0, 2]], vals[j], 0)
+            j += n
+        return k
+
+    k_p2 = gf(T.p2[:], [[0, 1]], -127, 2)
+    k_pI = gi(T.pI[:], [[0, 1]], 0, 1)
+    k_t1 = table(0, PI + [NRT + PI[(1 + j) % N] for j in range(6)])
+    k_16 = gf(T.b16[:], [[16, 8]], 0, 0)
+    k = gf(T.diag[:], [[0, 4], [-3200, 6]], 200, 200)
+    k_t2 = table(20, srt + [NR2 + srt[(1 + j) % 3] for j in range(4)] + [E4] * 4 + [TOK])
+    k_dg = gf(T.diag[:, 5:24:6], [[0, 4]], 1000, 0, k)
+    k_80 = gf(T.i80[:], [[1, 80]], 0, 0)
+    k_z0 = ms(T.rtt[:, 32:512], 0.0)
     k_x0 = ms(T.xt[:, 768:776], 0.0)
+    k = ts(T.rI[:], T.pI[:], 15, None, OP.bitwise_and, None, k_pI)
+    k_ck = ms(T.ck[:], (DF - 0.5) * K)
+    k_rf = ts(T.rf[:], T.rI[:], -1.0, -0.5, OP.mult, OP.add, k)
+    k_lw = ms(T.lwho[:], -1.0)
+    ms(T.r2t[:, 40:512], 0.0)
+    k = act(T.pa[:], T.p2[:], AF.Abs, 0.0, 1.0, k_p2)
+    k_th = act(T.th1[:], T.p2[:], AF.Copy, 0.0, TINY)
+    k_eb = act(T.eb1[:], T.pa[:], AF.Copy, 64 * TINY, -TINY, k)
 
     k = ts(T.rtt[:, 16:32], T.rtt[:, 0:16], -1.0, None, OP.mult, None, d_rt)
-    k_rq = quant(T.rtq[:], T.rts[:], T.rtt[:], k)
-    kp1 = pickq(T.rpq[:, 0:256], T.rtq[:], T.rto[:, 0:16], k_rq)
-    ks1 = picks(T.rps[:, 0:256], T.rts[:], T.rto[:, 0:16], k_rq, k_rto)
+    k_rq = quant(T.rtq[:], T.rts[:], T.rtt[:], k, k_z0)
+    k_o1 = cp(T.to[:, 0:20], T.ti[:, 0:20], k_t1)
+    kp1 = pickq(T.rpq[:, 0:256], T.rtq[:], T.to[:, 0:16], k_rq, k_o1)
+    ks1 = picks(T.rps[:, 0:256], T.rts[:], T.to[:, 0:16], k_rq, k_o1)
     k_xq = quant(T.xq[:], T.xs[:], T.xt[:], d_x, k_x0)
-    kp2 = pickq(T.rpq[:, 256:448], T.rtq[:], T.rto[:, 16:28])
-    ks2 = picks(T.rps[:, 256:448], T.rts[:], T.rto[:, 16:28])
-    ms(T.eb1[0:32, :], 0.0)
-    ms(T.eb1[32:64, :], -EPS)
-    ms(T.eb1[64:96, :], EPS)
-    k_th = ms(T.eb1[96:128, :], 0.0)
+    kp2 = pickq(T.rpq[:, 256:320], T.rtq[:], T.to[:, 16:20])
+    ks2 = picks(T.rps[:, 256:320], T.rts[:], T.to[:, 16:20])
     dm = []
     for j in range(3):
         mm(bank(j, 192), T.rpq[:, 0:128], T.rps[:, 0:128], T.xq[:, 0:192], T.xs[:, 0:192], True, False, kp1, ks1, k_xq)
-        a = 32 * RTS[j]
+        a = 128 + 32 * j
         dj = (kp2, ks2) if j else ()
         dm.append(mm(bank(j, 192), T.rpq[:, a:a + 128], T.rps[:, a:a + 128], T.xq[:, 0:192], T.xs[:, 0:192], False, True, *dj))
-    k_z1 = act(T.z1[:], bank(0, 192), AF.Identity, T.eb1[:], 1.0, dm[0], k_th)
-    ms(T.th1[0:64, :], -EPS / 2)
-    ms(T.th1[64:128, :], EPS / 2)
-    kr = ts(T.rI[:], T.pI[:], 15, None, OP.bitwise_and, None, k_g)
-    kq = ts(T.qI[:], T.pI[:], 31, None, OP.bitwise_and, None)
-    ms(T.zb[:], 0.0)
-    k1 = tt(T.cs[:], T.rI[:, 0:8], T.b16[:], OP.add, kr)
-    k_jk = ms(T.jkd[:, 192:193], -192.0)
-    k_jk = ms(T.jkd[:, 448:449], -192.0)
-    ts(T.csp[:], T.cs[:], 0.5, None, OP.add, None, k1)
-    k_cs = ts(T.csn[:], T.cs[:], -1.0, -0.5, OP.mult, OP.add)
+    k_z1 = act(T.z1[:], bank(0, 192), AF.Sign, T.eb1[:], 1.0, dm[0], k_eb)
+    k = act(T.csn[:], T.b16[:], AF.Identity, T.rf[:], -1.0, k_16, k_rf)
+    act(T.eb2[:], T.p2[:], AF.Copy, 0.0, -TINY)
+    k_cs = act(T.csp[:], T.csn[:], AF.Copy, 0.0, -1.0, k)
+    k_e2 = act(T.th2[:], T.p2[:], AF.Copy, -64 * TINY, -TINY)
     k = tt(T.z2[:], bank(1, 192), T.z1[:], OP.min, dm[1], k_z1)
-    k_lw = ms(T.lwho[:], -1.0)
     k_d1 = tt(T.z3[:], bank(2, 192), T.z2[:], OP.min, dm[2], k)
-    k2 = tt(T.cm[:], T.qI[:, 0:8], T.b32[:], OP.add, kq)
-    k = ts(T.mk[:], T.z3[:], T.th1[:], None, OP.is_gt, None, k_d1)
-    k_mo = ms(T.msgo[:], 0.0)
-    k_cum = scan(T.cum[:], T.mk[:], T.zb[:, 0:192], 0.0, OP.add, k)
+    k_o2 = cp(T.to[:, 20:44], T.ti[:, 20:44], k_t2)
+    k = ts(T.mk[:], T.z3[:], T.th1[:], None, OP.is_gt, None, k_d1, k_th)
+    k_cum = run(T.cum[:], T.mk[:], 128, TOK, 0.0, k)
     send(near, T.cnte[:, 0:1], T.cum[:, 191:192], "ae", k_cum)
-    k_cm = ts(T.cmn[:], T.cm[:], -1.0, -0.5, OP.mult, OP.add, k2)
-    k_a = [acc(T.jka[:, 192 * c:192 * c + 192], T.cum[:], AF.Sign, T.csn[:, c:c + 1], T.cnt1[:, c:c + 1], k_cum, k_cs) for c in range(3)]
-    k3 = ts(T.jkd[:, 0:192], T.cum[:], T.csp[:, 3:4], 2.0, OP.is_gt, OP.mult, k_cum)
-    k4 = ts(T.jkd[:, 256:448], T.cum[:], T.csp[:, 4:5], 2.0, OP.is_gt, OP.mult)
-    ts(T.cnt1[:, 5:6], T.cum[:, 191:192], -2.0, 192.0, OP.mult, OP.add)
-    red(T.cnt1[:, 3:4], T.jkd[:, 0:193], OP.add, k3, k_jk)
-    k_c = red(T.cnt1[:, 4:5], T.jkd[:, 256:449], OP.add, k4)
-    k_mi = ms(T.msgi[:, 8 * rank:8 * rank + 8], 0.0)
-    pk, psc, k_off = {}, {}, {}
+    for c in range(2):
+        acc(T.jka[:, 192 * c:192 * c + 192], T.cum[:], AF.Sign, T.csn[:, c:c + 1], 1.0, T.cnt1[:, c:c + 1], k_cum, k_cs)
+    k_a = act(T.cnt1[:, 5:6], T.cum[:, 191:192], AF.Copy, 192.0, -2.0)
+    seg = lambda c: slice(192 * (c - 2) + 16 * c, 192 * (c - 1))
+    kk = [ts(T.jkd[:, seg(c)], T.cum[:, 16 * c:192], T.csp[:, c:c + 1], 2.0, OP.is_gt, OP.mult, k_cum, k_cs) for c in (2, 3, 4)]
+    for c in (2, 3, 4):
+        k = run(T.jkf[:, seg(c)], T.jkd[:, seg(c)], 128, TOK - 16 * c, -192.0, kk[c - 2])
+    k_c = cp(T.cnt1[:, 2:5], T.jkf[:, 191:576:192], k)
+    pk, psc = {}, {}
     seq = order + [rank]
-
-    def offs1(b):
-        for q in range(N):
-            k_off[b] = ts(T.off1[quad(q), 6 * b:6 * b + 6], T.cnt1[quad(b), 0:6], -0.5, 96.0, OP.mult, OP.add, k_c, k_a[-1])
-
-    offs1(seq[0])
+    col1 = {b: 6 * i for i, b in enumerate(seq)}
+    off1 = lambda q, b: ts(T.off1[quad(q), col1[b]:col1[b] + 6], T.cnt1[quad(PI[b]), 0:6], -0.5, 96.0, OP.mult, OP.add, k_c, k_a)
+    todo = [(q, b) for b in seq for q in range(N)]
+    k_of = [off1(*todo[j]) for j in range(6)]
     for i, b in enumerate(seq):
         o, so = (T.sl1[:, 80 * i:80 * i + 80], T.ss1[:, 80 * i:80 * i + 80]) if b != rank else \
                 (T.land1[:, 80 * b:80 * b + 80], T.lans1[:, 80 * b:80 * b + 80])
-        pk[b] = pickq(o, T.xq[:, 0:194], T.off1[:, 6 * b:6 * b + 5], k_off[b])
-        psc[b] = picks(so, T.xs[:, 0:194], T.off1[:, 6 * b:6 * b + 5], k_off[b])
+        pk[b] = pickq(o, T.xq[:, 0:194], T.off1[:, 6 * i:6 * i + 5], k_of[4 * i + 3])
+        psc[b] = picks(so, T.xs[:, 0:194], T.off1[:, 6 * i:6 * i + 5], k_of[4 * i + 3])
         if b != rank:
-            send(b, c8(T.land1[:, 80 * rank:80 * rank + 80]), c8(T.sl1[:, 80 * i:80 * i + 80]), "arr%d" % rank, pk[b], k_lw)
-            send(b, T.lans1[:, 80 * rank:80 * rank + 80], T.ss1[:, 80 * i:80 * i + 80], "arr%d" % rank, psc[b])
-            offs1(seq[i + 1])
-    k_m = [acc(T.jka[:, 576 + 192 * c:768 + 192 * c], T.cum[:], AF.Sign, T.cmn[:, c:c + 1], T.cntm[:, c:c + 1], k_cm) for c in range(3)]
-    m_v, m_a = {}, {}
-    for b in seq:
-        m, o = (T.msgo, 8 * b) if b != rank else (T.msgi, 8 * rank)
-        m_v[b] = cp(m[:, o + 1:o + 2], T.off1[:, 6 * b + 5:6 * b + 6], k_off[b], k_mo) if b != near else k_mo
-        for c in range(3):
-            m_a[b] = act(m[quad(c), o:o + 1], T.cntm[quad(b), c:c + 1], AF.Copy, 96.0, -0.5, k_m[2], k_mo, k_mi)
-        if b != rank:
-            wd = 1 if b == near else 2
-            send(b, T.msgi[:, 8 * rank:8 * rank + wd], T.msgo[:, o:o + wd], "am", m_v[b], m_a[b])
+            send(b, c8(T.land1[:, 80 * rank:80 * rank + 80]), c8(o), "arr%d" % rank, pk[b], k_lw)
+            send(b, T.lans1[:, 80 * rank:80 * rank + 80], so, "arr%d" % rank, psc[b])
+        k_of += [off1(*x) for x in todo[4 * i + 6:4 * i + 10]]
+        if i == 2:
+            k_ng = ts(T.r2t[:, 20:40], T.r2t[:, 0:20], -1.0, None, OP.mult, None, d_r2)
+            k = cp(T.offf[:], T.off1[:], k_of[-1])
+    ozero = T.to[:, 42:43]
+    k_z = pickq(T.land1[:, NX:XC], T.xq[:, 0:194], ozero, k_o2)
+    k_mo = scan(T.mo[:], T.diag[:], T.offf[:], 0.0, OP.max, OP.min, k, k_dg)
+    for b in order[1:]:
+        send(b, T.msgi[:, 8 * rank:8 * rank + 2], T.mo[:, col1[b] + 4:col1[b] + 6], "am", k_mo)
+    send(near, T.msgi[:, 8 * rank:8 * rank + 1], T.mo[:, 4:5], "an")
 
-    k_oz = ms(T.ozero[:], TOK)
     k_wq = quant(T.wq[:], T.wsc[:], T.wt[:], d_w)
-    k_z = pickq(T.land1[:, NX:XC], T.xq[:, 0:194], T.ozero[:, 0:1], k_xq, k_oz)
-    k_zs = picks(T.lans1[:, NX:XC], T.xs[:, 0:194], T.ozero[:, 0:1], k_z)
-    ms(T.r2t[:, 40:512], 0.0)
-    k = ts(T.r2t[:, 20:40], T.r2t[:, 0:20], -1.0, None, OP.mult, None, d_r2)
-    srt = sorted(others)
-    one = {srt[0]: srt[1], srt[1]: srt[0], srt[2]: srt[0], rank: 0}
-    two = {srt[0]: srt[2], srt[1]: srt[2], srt[2]: srt[1], rank: 0}
-    blocks = [0, 1, 2, 3] + [5 + one[q] for q in range(N)] + [5 + two[q] for q in range(N)]
-    for c in range(12):
-        ms(T.r2o[:, 2 * c:2 * c + 2], blocks[c])
-    k_o = ms(T.r2o[:, 24:32], 4)
-    k_r2q = quant(T.r2q[:], T.r2s[:], T.r2t[:], k)
-    k_z2 = pickq(T.land2[:, 192:208], T.xq[:, 0:194], T.ozero[:, 0:1], k_xq)
-    k_z2s = picks(T.lans2[:, 192:208], T.xs[:, 0:194], T.ozero[:, 0:1], k_z2)
-    k_r2p = pickq(T.r2p[:], T.r2q[:], T.r2o[:], k_o, k_r2q)
-    k_r2s = picks(T.r2ps[:], T.r2s[:], T.r2o[:], k_o, k_r2q)
+    k_r2q = quant(T.r2q[:], T.r2s[:], T.r2t[:], k_ng)
+    k_zs = picks(T.lans1[:, NX:XC], T.xs[:, 0:194], ozero, k_o2)
+    k_r2p = pickq(T.r2p[:], T.r2q[:], T.to[:, 20:42], k_r2q)
+    k_r2s = picks(T.r2ps[:], T.r2s[:], T.to[:, 20:42], k_r2q)
+    am, an = ("am", arrivals(far, 1)), ("an", arrivals([near], 1))
     for q in range(N):
-        ms(T.eb2[quad(q), :], EPS / 2 if one[q] > q else -EPS / 2)
-        k_t2 = ms(T.th2[quad(q), :], EPS / 2 if two[q] > q else -EPS / 2)
-    k_num = ms(T.num[:], -1.0)
-    for q in range(N):
-        k_cq = cp(T.cntq[quad(q), 0:1], T.cnte[quad(rank), 0:1], ("ae", arrivals([near], 1)))
-    am = ("am", arrivals(others, 1))
-
-    def absent(s, cn, *dep):
-        return ts(T.inv[:, 80 * s:80 * s + 80], T.i80[:], cn, BIG, OP.is_ge, OP.mult, k_80, *dep)
-
-    absent(rank, T.msgi[:, 8 * rank + 1:8 * rank + 2], m_v[rank])
-    ki0 = absent(near, T.cntq[:, 0:1], k_cq)
+        act(T.ib[quad(q), 0:1], T.cnte[quad(PI[rank]), 0:1], AF.Copy, 0.5 * K, -K, ("ae", arrivals([near], 1)))
+    k = act(T.ib[:, 1:2], T.mo[:, 23:24], AF.Copy, 0.5 * K, -K, k_mo)
+    k_num = act(T.num[:], T.xt[:, 0:XC], AF.Copy, -1.0, 0.0)
+    act(T.inv[:, 80 * near:80 * near + 80], T.i80[:], AF.Relu, T.ib[:, 0:1], K, k, k_80)
+    ki0 = act(T.inv[:, 80 * rank:80 * rank + 80], T.i80[:], AF.Relu, T.ib[:, 1:2], K)
 
     arr = lambda s: ("arr%d" % s, arrivals([s], 2))
     home = (pk[rank], psc[rank])
     halves = [(0, NH, [0, 1]), (NH, NX + 2, [2, 3])]
     if rank >= 2:
         halves.reverse()
-    H = lambda a, b: (T.xw[:, HB + a:HB + b], T.xws[:, HB + a:HB + b])
-    P = lambda k: (T.r2p[:, 128 * k:128 * k + 128], T.r2ps[:, 128 * k:128 * k + 128])
+    H = lambda a, b: (T.hq[:, a:b], T.hs[:, a:b])
+    P = lambda k: (T.r2p[:, 32 * k:32 * k + 128], T.r2ps[:, 32 * k:32 * k + 128])
     f0, g0 = halves[0][0], halves[1][0]
     F, G = slice(f0, f0 + NH), slice(g0, g0 + NH)
-    blk = [0, 128, 192] if f0 == 0 else [192, 0, 64]
+    blk = [0, 128, 192] if f0 == 0 else [192, 64, 0]
 
     def products(h):
         c0, c1, who = halves[h]
@@ -264,113 +221,113 @@ def rank_program(g, core, T, topo):
         k1 = ts(hv(1), bank(4 * h + 1, c1 - c0), 0.0, 0.0625, OP.max, OP.mult, W[1])
         k2 = act(hv(2), bank(4 * h + 2, c1 - c0), AF.Relu, 0.0, 0.0625, W[2])
         k3 = ts(hv(3), bank(4 * h + 3, c1 - c0), 0.0, 0.0625, OP.max, OP.mult, W[3])
-        return quant(T.xw[:, HB + c0:HB + c1], T.xws[:, HB + c0:HB + c1], T.hb[:, 4 * c0:4 * c1], k0, k1, k2, k3)
+        return quant(T.hq[:, c0:c1], T.hs[:, c0:c1], T.hb[:, 4 * c0:4 * c1], k0, k1, k2, k3)
 
     def diff(k, j, c0, *d):
         mm(bank(k, NH), *P(0), *H(c0, c0 + NH), True, False, *d)
         return mm(bank(k, NH), *P(j), *H(c0, c0 + NH), False, True)
 
+    e4 = lambda k: T.ps[:, 512 * k + E4:512 * k + E4 + 1]
     W0 = products(0)
     kq0 = tile(0, W0)
     W1 = products(1)
-    k_vx = quant(T.vxq[:], T.vxs[:], T.vxt[:], d_vx)
-    k_vh = quant(T.vhq[:], T.vhs[:], T.vht[:], d_vh)
-    kq1 = tile(1, W1)
-    alla = [arr(s) for s in range(N) if s != rank]
-    dma("s", "dxw", c8(T.xw[:, 0:XC]), c8(T.land1[:]), *alla, *home, k_z, k_zs)
-    d_xw = dma("s", "dxw", T.xws[:, 0:XC], T.lans1[:])
-    for s in range(N):
-        d_nb = dma("s", "dnb", T.nb[0:1, 80 * s:80 * s + 80], T.msgi[0:80, 8 * s:8 * s + 1], am, m_v[rank], m_a[rank])
-
-    e4 = lambda k: T.ps[:, 512 * k + 4:512 * k + 5]
-    ea = mm(bank(0, NH), *P(3), *H(f0, f0 + NH), True, True, kq0, k_r2p, k_r2s, k_r2q)
+    ea = mm(bank(0, NH), *P(7), *H(f0, f0 + NH), True, True, kq0, k_r2p, k_r2s)
     e0 = mm(bank(1, 128), *H(blk[0], blk[0] + 128), T.r2q[:], T.r2s[:], True, True)
+    f1a = diff(2, 3, f0)
+    f2a = diff(3, 4, f0)
+    kq1 = tile(1, W1)
     ken0 = act(T.en[:, 0:1], e4(1), AF.Copy, 0.0, 1.0, e0)
-    if EARLY > 1:
-        f1a = diff(2, 1, f0)
-    eb = mm(bank(4, NH), *P(3), *H(g0, g0 + NH), True, True, kq1)
+    k_ef = tt(T.em[:, F], bank(0, NH), T.inv[:, F], OP.add, ea, ki0)
+    for s in range(N):
+        src = T.msgi[0:80, 8 * s:8 * s + 1] if s != rank else T.mo[0:80, 22:23]
+        d_nb = dma("s", "dnb", T.nb[0:1, 80 * s:80 * s + 80], src, am, an, k_mo)
+    d_vx = dma("s", "dvx", T.vxt[:], T.vx[:])
+    d_vh = dma("s", "dvh", T.vht[:], T.vh[:])
+
+    eb = mm(bank(4, NH), *P(7), *H(g0, g0 + NH), True, True, kq1)
     e2 = mm(bank(6, 128), *H(blk[2], blk[2] + 128), T.r2q[:], T.r2s[:], True, True)
     e1 = mm(bank(5, 128), *H(blk[1], blk[1] + 128), T.r2q[:], T.r2s[:], True, True)
-    if EARLY <= 1:
-        f1a = diff(2, 1, f0)
-    f2a = diff(3, 2, f0)
-    f1b = diff(7, 1, g0)
-    f2b = diff(1, 2, g0, ken0)
+    f1b = diff(7, 3, g0)
+    f2b = diff(1, 4, g0, ken0)
+    act(T.s1[:, F], bank(2, NH), AF.Sign, T.eb2[:], 1.0, f1a, k_e2)
+    k_sf = act(T.s2[:, F], bank(3, NH), AF.Sign, T.th2[:], 1.0, f2a)
     ken2 = act(T.en[:, 2:3], e4(6), AF.Copy, 0.0, 1.0, e2)
-    ken1 = act(T.en[:, 1:2], e4(5), AF.Copy, 0.0, 1.0, e1)
-    tt(T.em[:, F], bank(0, NH), T.inv[:, F], OP.add, ea, ki0)
-    for s in others:
-        if s != near:
-            ki = absent(s, T.msgi[:, 8 * s + 1:8 * s + 2], am)
+    for s in far:
+        ki = ts(T.inv[:, 80 * s:80 * s + 80], T.i80[:], T.msgi[:, 8 * s + 1:8 * s + 2], BIG, OP.is_ge, OP.mult, am, k_80)
     k_em = tt(T.em[:, G], bank(4, NH), T.inv[:, G], OP.add, eb, ki)
-    ms(T.zf[:], 0.0)
-    kc0 = ts(T.jk2[:, 0:320], T.em[:], T.en[:, 0:1], None, OP.is_lt, None, k_em, ken0)
-    kc1 = ts(T.jk2[:, 320:640], T.em[:], T.en[:, 1:2], None, OP.is_lt, None, ken1)
+    ts(T.jk2[:, 320:480], T.em[:, F], T.en[:, 0:1], K, OP.is_lt, OP.mult, k_ef, ken0)
+    kc0 = ts(T.jk2[:, 480:640], T.em[:, G], T.en[:, 0:1], K, OP.is_lt, OP.mult, k_em)
+    kc1 = ts(T.jk2[:, 0:NX], T.em[:], e4(5), K, OP.is_lt, OP.mult, e1)
     k = act(T.jk2[:, 640:960], T.em[:], AF.Sign, T.en[:, 2:3], -1.0, k_em, ken2)
-    kl2 = acc(T.jkb[:, 320:640], T.jk2[:, 640:960], AF.Relu, 0.0, T.lt[:, 2:3], k)
-    scan(T.jkc[:, 0:320], T.jk2[:, 0:320], T.zb[:], 0.0, OP.add, kc0)
-    k = scan(T.jkc[:, 320:640], T.jk2[:, 320:640], T.zb[:], 0.0, OP.add, kc1)
-    ms(T.khb[:, 0:1], 0.0)
-    cp(T.lt[:, 0:2], T.jkc[:, 319:640:320], k)
-    ts(T.pen[:, 0:2], T.jkc[:, 319:640:320], DF - 0.5, LOW, OP.is_ge, OP.mult)
-    kp = ts(T.pen[:, 2:3], T.lt[:, 2:3], DF - 0.5, LOW, OP.is_ge, OP.mult, kl2)
-    ms(T.khb[:, 1:2], -2.0 * HB)
-    act(T.s1[:, F], bank(2, NH), AF.Sign, T.eb2[:], 1.0, f1a, k_t2)
-    act(T.s2[:, F], bank(3, NH), AF.Sign, T.th2[:], 1.0, f2a)
+    k_cf = act(T.c2[:, F], T.s2[:, F], AF.Copy, 4.0, -1.0, k_sf)
+    kl2 = acc(T.jkb[:, 0:320], T.jk2[:, 640:960], AF.Relu, 0.0, K, T.lt[:, 2:3], k)
+    run(T.jkc[:, 320:640], T.jk2[:, 320:640], 128, NX, 0.0, kc0)
+    k = run(T.jkc[:, 0:320], T.jk2[:, 0:320], 128, NX, 0.0, kc1)
+    elem(T.uw[:, F], T.s1[:, F], T.c2[:, F], OP.subtract, k_cf)
+    kp = cp(T.lt[:, 0:2], T.jkc[:, 319:640:320], k)
     act(T.s1[:, G], bank(7, NH), AF.Sign, T.eb2[:], 1.0, f1b)
     k = act(T.s2[:, G], bank(1, NH), AF.Sign, T.th2[:], 1.0, f2b)
-    k_cc = act(T.c2[:], T.s2[:], AF.Copy, 4.0, -1.0, k)
-    for k in range(3):
-        ts(T.bc[:, 32 * k:32 * k + 32], T.zf[:], T.en[:, k:k + 1], T.pen[:, k:k + 1], OP.add, OP.add, kp)
-        kc = ts(T.bc[:, 96 + 32 * k:128 + 32 * k], T.zf[:], T.lt[:, k:k + 1], T.pen[:, k:k + 1], OP.add, OP.add)
-    kc = op("v", lambda e: e.transpose(T.bt[:], T.bc[:]), kc)
-    ms(T.ys[:, CB * rank:CB * rank + CB], 0.0)
-    red(T.qm[:, 0:1], T.bt[:, 0:96], OP.max, kc)
-    kc = red(T.qm[:, 1:2], T.bt[:, 96:192], OP.max)
-    ms(T.ofin[:, 2 * rank:2 * rank + 2], 192)
-    tt(T.g4[0:64, :], T.qm[0:64, :], T.qm[64:128, :], OP.max, kc)
-    kc = tt(T.g4[64:128, :], T.qm[64:128, :], T.qm[0:64, :], OP.max)
-    for q in range(N):
-        k = tt(T.tl[quad(q), :], T.g4[quad(q), :], T.g4[quad(q ^ 1), :], OP.max, kc)
-    k_uw = elem(T.uw[:], T.s1[:], T.c2[:], OP.subtract, k_cc)
-    k_sg = act(T.sg[:], T.em[:], AF.Sign, T.tl[:, 0:1], -1.0, k)
-    for s in range(N):
-        k_n = act(T.num[0:1, 80 * s:80 * s + 80], T.nb[0:1, 80 * s:80 * s + 80], AF.Copy, float(TOK * s), 1.0, d_nb, k_num)
-    k_gd = ts(T.gd[:], T.em[:], T.tl[:, 0:1], None, OP.is_equal, None, k)
-    k_t1 = elem(T.t1[:], T.sg[:], T.uw[:], OP.add, k_sg, k_uw)
-    k_nq = scan(T.nq[:], T.gd[:], T.zb[:], T.tl[:, 1:2], OP.add, k_gd)
-    k = ts(T.nf[:], T.nq[:], DF + 0.5, 6.0, OP.is_gt, OP.add, k_nq)
-    k = elem(T.t2[:], T.t1[:], T.nf[:], OP.subtract, k, k_t1)
-    k = ts(T.mk2[:], T.t2[:], -8.5, None, OP.is_gt, None, k)
-    k_c2 = scan(T.cum2[:], T.mk2[:], T.zb[:], 0.0, OP.add, k)
-    ka = acc(T.jkb[:, 640:960], T.cum2[:], AF.Sign, T.csn[:, 0:1], T.ac[:, 0:1], k_c2)
-    k = ts(T.jke[:, 0:320], T.cum2[:], T.csp[:, 1:2], 2.0, OP.is_gt, OP.mult, k_c2)
-    k = scan(T.jke[:, 320:640], T.jke[:, 0:320], T.zb[:], -320.0, OP.add, k)
-    ts(T.cnt2[:, 0:4:2], T.khb[:], T.ac[:, 0:1], None, OP.add, None, ka)
-    kc = ts(T.cnt2[:, 1:4:2], T.khb[:], T.jke[:, 639:640], None, OP.add, None, k)
+    k_cc = act(T.c2[:, G], T.s2[:, G], AF.Copy, 4.0, -1.0, k)
+    ts(T.bc[:, 64:96], T.ck[:], T.lt[:, 2:3], T.en[:, 2:3], OP.subtract, OP.min, kl2, k_ck)
+    ts(T.bc[:, 0:32], T.ck[:], T.lt[:, 0:1], e4(5), OP.subtract, OP.min, kp)
+    k = ts(T.bc[:, 32:64], T.ck[:], T.lt[:, 1:2], T.en[:, 0:1], OP.subtract, OP.min)
+    k = op("v", lambda e: e.transpose(T.bt[:], T.bc[:]), k)
+    k = scan(T.gm[0:64, :], T.bt[0:64, :], T.bt[64:128, :], LOW, OP.max, OP.max, k)
+    for q in range(3):
+        k_tl = tt(T.tl[quad(q), :], T.gm[0:32, 95:96], T.gm[32:64, 95:96], OP.max, k)
+    k_uw = elem(T.uw[:, G], T.s1[:, G], T.c2[:, G], OP.subtract, k_cc)
+    Q = slice(0, 96)
+    k_sg = acc(T.sg[Q, :], T.em[Q, :], AF.Sign, T.tl[Q, :], -1.0, T.sa[Q, :], k_tl)
+    k_sb = act(T.sb[Q, :], T.sa[Q, :], AF.Copy, DF + 0.5 - 1.5 * NH, -0.5, k_sg)
+    k = ts(T.gd[Q, :], T.em[Q, :], T.tl[Q, :], None, OP.is_equal, None, k_tl)
+    k_nq = run(T.nq[Q, :], T.gd[Q, :], 96, NX, -1.0 * NH, k)
+    k_t1 = elem(T.t1[Q, :], T.sg[Q, :], T.uw[Q, :], OP.add, k_sg, k_uw)
+    k = ts(T.fit[Q, :], T.nq[Q, 319:320], 0.5, T.sb[Q, :], OP.mult, OP.add, k_nq, k_sb)
+    k = ts(T.nf[Q, :], T.nq[Q, :], T.fit[Q, :], 6.0, OP.is_gt, OP.add, k)
+    k = elem(T.t2[Q, :], T.t1[Q, :], T.nf[Q, :], OP.subtract, k, k_t1)
+    k = ts(T.mk2[Q, :], T.t2[Q, :], -8.5, None, OP.is_gt, None, k)
+    k_c2 = run(T.cum2[Q, :], T.mk2[Q, :], 96, NX, 0.0, k)
+    ka = acc(T.jkb[Q, 320:640], T.cum2[Q, :], AF.Sign, T.csn[Q, 0:1], 1.0, T.cnt2[Q, 0:1], k_c2)
+    k = ts(T.jke[Q, 16:320], T.cum2[Q, 16:320], T.csp[Q, 1:2], 2.0, OP.is_gt, OP.mult, k_c2)
+    k = run(T.jke[Q, 336:640], T.jke[Q, 16:320], 96, NX - 16, -1.0 * NX, k)
+    kc = cp(T.cnt2[Q, 1:2], T.jke[Q, 639:640], k)
+    off2 = lambda q, i: ts(T.off2[quad(q), 2 * i:2 * i + 2], T.cnt2[quad(srt.index(order[i])), :], -0.5, NX / 2.0, OP.mult, OP.add, kc, ka)
+    todo = [(q, i) for i in range(3) for q in range(N)]
+    k_of = [off2(*todo[j]) for j in range(6)]
     for i, b in enumerate(order):
-        for q in range(N):
-            ko = ts(T.off2[quad(q), 4 * i:4 * i + 4], T.cnt2[quad(b), 0:4], -0.5, NX / 2.0, OP.mult, OP.add, kc)
-        o = slice(64 * i, 64 * i + 64)
-        kk = pickq(T.sl2[:, o], T.xw[:], T.off2[:, 4 * i:4 * i + 4], ko, d_xw)
-        ks = picks(T.ss2[:, o], T.xws[:], T.off2[:, 4 * i:4 * i + 4], ko, d_xw)
-        kw = op("a", lambda e: e.activation(T.wg[:, 32 * i:32 * i + 32], T.num[:].indirect(T.off2[:, 4 * i:4 * i + 2]), AF.Copy), k_n)
+        o, lst, ko = 64 * i, T.off2[:, 2 * i:2 * i + 2], k_of[4 * i + 3]
+        pickq(T.sl2[:, o:o + 32], T.land1[:], lst, ko)
+        kk = pickq(T.sl2[:, o + 32:o + 64], T.hq[:, 0:NX + 2], lst)
+        picks(T.ss2[:, o:o + 32], T.lans1[:], lst, ko)
+        ks = picks(T.ss2[:, o + 32:o + 64], T.hs[:, 0:NX + 2], lst)
         d = slice(64 * slot(rank, b), 64 * slot(rank, b) + 64)
-        send(b, c8(T.land2[:, d]), c8(T.sl2[:, o]), "arrb", kk)
-        send(b, T.lans2[:, d], T.ss2[:, o], "arrb", ks)
+        send(b, c8(T.land2[:, d]), c8(T.sl2[:, o:o + 64]), "arrb", kk)
+        send(b, T.lans2[:, d], T.ss2[:, o:o + 64], "arrb", ks)
+        k_of += [off2(*x) for x in todo[4 * i + 6:4 * i + 10]]
+        if i < 2:
+            for s in (2 * i, 2 * i + 1):
+                k_n = act(T.num[0:1, 80 * s:80 * s + 80], T.nb[0:1, 80 * s:80 * s + 80], AF.Copy, float(TOK * s), 1.0, d_nb, k_num)
+    kw = op("a", lambda e: e.activation(T.wg[:], T.num[:].indirect(T.off2[:]), AF.Copy), k_n)
     kw = op("v", lambda e: e.transpose(T.wtr[:], T.wg[:]), kw)
     for i, b in enumerate(order):
         send(b, T.lwho[:, rank:rank + 1], T.wtr[:, 32 * i:32 * i + 1], "aw", kw)
+
+    k_vx = quant(T.vxq[:], T.vxs[:], T.vxt[:], d_vx)
+    k_vh = quant(T.vhq[:], T.vhs[:], T.vht[:], d_vh)
+    k_z2 = pickq(T.land2[:, 192:208], T.xq[:, 0:194], ozero)
+    k_z2s = picks(T.lans2[:, 192:208], T.xs[:, 0:194], ozero)
+    ms(T.ys[:, CB * rank:CB * rank + CB], 0.0)
+    ms(T.ofin[:, 2 * rank:2 * rank + 2], 192)
     for a in others:
-        k_ofin = ts(T.ofin[:, 2 * a:2 * a + 2], T.cs[:, 0:2], 64.0 * slot(a, rank) + CB, None, OP.add, None)
+        k_ofin = ts(T.ofin[:, 2 * a:2 * a + 2], T.csp[:, 0:2], 64.0 * slot(a, rank) + CB - 0.5, None, OP.add, None)
 
     ab = ("arrb", arrivals(others, 2))
-    mm(bank(5, 160), T.vxq[:], T.vxs[:], T.land2[:, 0:160], T.lans2[:, 0:160], True, False, ab, k_vx, k_vh, ken1)
-    ty = mm(bank(5, 160), T.vhq[:], T.vhs[:], T.land2[:, 32:192], T.lans2[:, 32:192], False, True)
+    mm(bank(0, 160), T.vxq[:], T.vxs[:], T.land2[:, 0:160], T.lans2[:, 0:160], True, False, ab, k_vx, k_vh)
+    ty = mm(bank(0, 160), T.vhq[:], T.vhs[:], T.land2[:, 32:192], T.lans2[:, 32:192], False, True)
     kf = pickq(T.fin[:], T.land2[:], T.ofin[:], ab, k_ofin, k_z2)
     kfs = picks(T.fins[:], T.lans2[:], T.ofin[:], ab, k_ofin, k_z2s)
     for a in others:
-        c0 = 2560 + 64 * slot(a, rank)
+        c0 = 64 * slot(a, rank)
         ky = cp(T.ys[:, CB * a:CB * a + CB], T.ps[:, c0:c0 + CB], ty)
     dma("s", "dout", T.oc[:], c8(T.fin[:]), kf)
     for k in range(4):

@@ -4,21 +4,20 @@ N, TOK, CAP, CB, DF = 4, 192, 80, 32, 80
 NX = N * CAP
 NH = NX // 2
 XC = 336
-TINY, BIG, LOW, K = 1e-33, 1e29, -9e29, 2.0 ** 80
+TINY, BIG, K = 1e-33, 1e29, 2.0 ** 80
 PI = [1, 0, 2, 3]
-E4, NRT, NR2 = 4, 4, 5
+E4, NRT = 4, 4
 Q8, U8, BF, F32 = "float8_e4m3fn_x4", "uint8", "bfloat16", "float32"
-SCRATCH = {"ps": ("psum", [128, 4096], F32)}
+SCRATCH = {"ps": ("psum", [128, 4096], F32), "mk3": ("sbuf", [128, 10, 32], BF)}
 for _d, _l in (
-        (Q8, dict(rtq=128, r2q=128, rpq=320, r2p=352, xq=194, wq=512, vxq=128, vhq=128, hq=XC, sl1=240, land1=XC, sl2=192, land2=208, fin=128)),
-        (U8, dict(rts=128, r2s=128, rps=320, r2ps=352, xs=194, wsc=512, vxs=128, vhs=128, hs=XC, ss1=240, lans1=XC, ss2=192, lans2=208, fins=128)),
-        (BF, dict(rtt=512, r2t=512, xt=776, wt=2048, vxt=512, vht=512, hb=4 * (NX + 2), mo=24, msgi=32, cnte=8, z1=192, mk=192, cum=192,
-                  jka=384, jkd=576, jkf=576, s1=NX, s2=NX, c2=NX, uw=NX, gd=NX, nq=NX, sg=NX, nf=NX, t1=NX, t2=NX, mk2=NX, cum2=NX,
-                  jk2=960, jkb=640, jke=640, jkc=640, nb=NX)),
-        (F32, dict(offf=24, diag=24, ib=2, lwho=32, whot=32, z2=192, z3=192, cnt1=8, inv=NX, em=NX, en=4, lt=4, ck=32, bc=96, bt=96, gm=96,
-                   tl=1, sa=1, sb=1, fit=1, cnt2=2, num=XC, wg=96, wtr=96, ys=128, th1=1, eb1=1, th2=1, eb2=1, p2=1, pa=1, rf=1,
-                   b16=8, csp=8, csn=8, i80=80)),
-        ("int32", dict(ti=44, pI=1, rI=1)), ("uint16", dict(to=44, off1=24, off2=6, ofin=8))):
+        (Q8, dict(rtq=128, r2q=128, rpq=320, r2p=128, xq=194, wq=512, vxq=128, vhq=128, hq=XC, sl1=240, land1=XC, sl2=192, land2=208, fin=128)),
+        (U8, dict(rts=128, r2s=128, rps=320, r2ps=128, xs=194, wsc=512, vxs=128, vhs=128, hs=XC, ss1=240, lans1=XC, ss2=192, lans2=208, fins=128)),
+        (BF, dict(rtt=512, r2t=512, xt=776, wt=2048, vxt=512, vht=512, hb=4 * (NX + 2), mo=24, msgi=32, z1=192, mk=192, cum=192,
+                  jka=576, jkd=576, jkf=576, mk2=NX, cum2=NX, jk2=384, jkb=896, jke=640, jkc=384, nb=NX, tri=NX, trj=NX, sd=576, rd=576, bc=96, bt=96)),
+        (F32, dict(offf=24, diag=24, ib=4, cnte=4, cno=1, lwho=32, whot=32, z2=192, z3=192, cnt1=8, inv=NX, em=NX, lt=4, ck=96,
+                   es=24, cz=6, czi=6, zz=6, zr=6, pres=6, ka=3, km=3, kc=3, ku=3, kv=3, key=3, h25=1, kid=1,
+                   cnt2=2, num=XC, wg=96, wtr=96, ys=128, th1=1, tn1=1, eb1=1, p2=1, pa=1, rf=1, b16=8, csp=8, csn=8, i80=80)),
+        ("int32", dict(ti=30, pI=1, rI=1)), ("uint16", dict(to=30, off1=24, off2=6, ofin=8))):
     for _n, _w in _l.items():
         SCRATCH[_n] = ("sbuf", [128, _w], _d)
 SEMAPHORES = ["v", "a", "t", "gq", "dx", "drt", "dw", "dr2", "dvx", "dvh", "dnb", "dout", "ls",
@@ -92,7 +91,7 @@ def rank_program(g, core, T, topo):
     d_rt = dma("a", "drt", T.rtt[:, 0:16], T.rt[:, 0:16])
     d_x = dma("s", "dx", T.xt[:, 0:768], T.x[:])
     d_w = dma("s", "dw", T.wt[:], T.w[:], d_x)
-    d_r2 = dma("s", "dr2", T.r2t[:, 0:20], T.r2[:, 0:20])
+    d_r2 = dma("s", "dr2", T.r2t[:, 0:24], T.r2[:, 0:24])
 
     gi = lambda out, pat, base, cmul: op("g", lambda e: e.iota(out, pat, base, cmul))
     gf = lambda out, pat, base, cmul, *d: op("g", lambda e: e.iota(out, pat, base, cmul, allow_small_or_imprecise_dtypes=True), *d)
@@ -113,18 +112,25 @@ def rank_program(g, core, T, topo):
     k_t1 = table(0, PI + [NRT + PI[(1 + j) % N] for j in range(6)])
     k_16 = gf(T.b16[:], [[16, 8]], 0, 0)
     k = gf(T.diag[:], [[0, 4], [-3200, 6]], 200, 200)
-    k_t2 = table(20, srt + [NR2 + srt[(1 + j) % 3] for j in range(4)] + [E4] * 4 + [TOK])
+    k_t2 = table(20, [E4] * 4 + [TOK])
+    k1 = gf(T.czi[:], [[16, 3], [-CAP, 2]], 0, 1)
     k_dg = gf(T.diag[:, 5:24:6], [[0, 4]], 1000, 0, k)
     k_80 = gf(T.i80[:], [[1, 80]], 0, 0)
+    gf(T.zr[:], [[0, 3], [-30001, 2]], 1, 0)
+    op("g", lambda e: e.affine_select(T.cz[:], T.czi[:], [[-16, 3], [200, 2]], OP.is_ge, -1000.0, CAP - 1, -1), k1)
     k_z0 = ms(T.rtt[:, 32:512], 0.0)
     k_x0 = ms(T.xt[:, 768:776], 0.0)
     k = ts(T.rI[:], T.pI[:], 15, None, OP.bitwise_and, None, k_pI)
-    k_ck = ms(T.ck[:], (DF - 0.5) * K)
+    k_tj = ms(T.trj[:], -2.0)
     k_rf = ts(T.rf[:], T.rI[:], -1.0, -0.5, OP.mult, OP.add, k)
+    ms(T.ck[:, 32:64], 2.0 * DF - 1 - NX)
+    ms(T.h25[:], 2.5)
     k_lw = ms(T.lwho[:], -1.0)
-    ms(T.r2t[:, 40:512], 0.0)
+    k_ng = ms(T.r2t[:, 24:512], 0.0)
+    k_cz = op("g", lambda e: e.affine_select(T.tri[:], T.trj[:], [[-1, NX]], OP.is_gt, -3.0, 96, 1), k_tj)
     k = act(T.pa[:], T.p2[:], AF.Abs, 0.0, 1.0, k_p2)
     k_th = act(T.th1[:], T.p2[:], AF.Copy, 0.0, TINY)
+    act(T.tn1[:], T.p2[:], AF.Copy, 0.0, -TINY)
     k_eb = act(T.eb1[:], T.pa[:], AF.Copy, 64 * TINY, -TINY, k)
 
     k = ts(T.rtt[:, 16:32], T.rtt[:, 0:16], -1.0, None, OP.mult, None, d_rt)
@@ -143,15 +149,17 @@ def rank_program(g, core, T, topo):
         dm.append(mm(bank(j, 192), T.rpq[:, a:a + 128], T.rps[:, a:a + 128], T.xq[:, 0:192], T.xs[:, 0:192], False, True, *dj))
     k_z1 = act(T.z1[:], bank(0, 192), AF.Sign, T.eb1[:], 1.0, dm[0], k_eb)
     k = act(T.csn[:], T.b16[:], AF.Identity, T.rf[:], -1.0, k_16, k_rf)
-    act(T.eb2[:], T.p2[:], AF.Copy, 0.0, -TINY)
     k_cs = act(T.csp[:], T.csn[:], AF.Copy, 0.0, -1.0, k)
-    k_e2 = act(T.th2[:], T.p2[:], AF.Copy, -64 * TINY, -TINY)
-    k = tt(T.z2[:], bank(1, 192), T.z1[:], OP.min, dm[1], k_z1)
-    k_d1 = tt(T.z3[:], bank(2, 192), T.z2[:], OP.min, dm[2], k)
-    k_o2 = cp(T.to[:, 20:44], T.ti[:, 20:44], k_t2)
-    k = ts(T.mk[:], T.z3[:], T.th1[:], None, OP.is_gt, None, k_d1, k_th)
-    k_cum = run(T.cum[:], T.mk[:], 128, TOK, 0.0, k)
-    send(near, T.cnte[:, 0:1], T.cum[:, 191:192], "ae", k_cum)
+    two = [slice(0, 96), slice(96, 192)]
+    kk = [tt(T.z2[:, h], T.ps[:, 512 + h.start:512 + h.stop], T.z1[:, h], OP.min, dm[1], k_z1) for h in two]
+    kk = [tt(T.z3[:, h], T.ps[:, 1024 + h.start:1024 + h.stop], T.z2[:, h], OP.min, dm[2], k) for h, k in zip(two, kk)]
+    k_d1 = kk[1]
+    k = acc(T.jka[:, 384:576], T.z3[:], AF.Sign, T.tn1[:], 1.0, T.cno[:], k_d1)
+    send(near, T.cnte[:, 0:1], T.cno[:], "ae", k)
+    kk = [ts(T.mk[:, h], T.z3[:, h], T.th1[:], None, OP.is_gt, None, k, k_th) for h, k in zip(two, kk)]
+    k = run(T.cum[:, 0:96], T.mk[:, 0:96], 128, 96, 0.0, kk[0])
+    k_o2 = cp(T.to[:, 20:30], T.ti[:, 20:30], k_t2)
+    k_cum = run(T.cum[:, 96:192], T.mk[:, 96:192], 128, 96, T.cum[:, 95:96], k, kk[1])
     for c in range(2):
         acc(T.jka[:, 192 * c:192 * c + 192], T.cum[:], AF.Sign, T.csn[:, c:c + 1], 1.0, T.cnt1[:, c:c + 1], k_cum, k_cs)
     k_a = act(T.cnt1[:, 5:6], T.cum[:, 191:192], AF.Copy, 192.0, -2.0)
@@ -176,9 +184,9 @@ def rank_program(g, core, T, topo):
             send(b, T.lans1[:, 80 * rank:80 * rank + 80], so, "arr%d" % rank, psc[b])
         k_of += [off1(*x) for x in todo[4 * i + 6:4 * i + 10]]
         if i == 2:
-            k_ng = ts(T.r2t[:, 20:40], T.r2t[:, 0:20], -1.0, None, OP.mult, None, d_r2)
+            k_r2q = quant(T.r2q[:], T.r2s[:], T.r2t[:], d_r2, k_ng)
             k = cp(T.offf[:], T.off1[:], k_of[-1])
-    ozero = T.to[:, 42:43]
+    ozero = T.to[:, 28:29]
     k_z = pickq(T.land1[:, NX:XC], T.xq[:, 0:194], ozero, k_o2)
     k_mo = scan(T.mo[:], T.diag[:], T.offf[:], 0.0, OP.max, OP.min, k, k_dg)
     for b in order[1:]:
@@ -186,17 +194,20 @@ def rank_program(g, core, T, topo):
     send(near, T.msgi[:, 8 * rank:8 * rank + 1], T.mo[:, 4:5], "an")
 
     k_wq = quant(T.wq[:], T.wsc[:], T.wt[:], d_w)
-    k_r2q = quant(T.r2q[:], T.r2s[:], T.r2t[:], k_ng)
+    k_r2p = pickq(T.r2p[:], T.r2q[:], T.to[:, 20:28], k_r2q)
     k_zs = picks(T.lans1[:, NX:XC], T.xs[:, 0:194], ozero, k_o2)
-    k_r2p = pickq(T.r2p[:], T.r2q[:], T.to[:, 20:42], k_r2q)
-    k_r2s = picks(T.r2ps[:], T.r2s[:], T.to[:, 20:42], k_r2q)
+    k_r2s = picks(T.r2ps[:], T.r2s[:], T.to[:, 20:28], k_r2q)
     am, an = ("am", arrivals(far, 1)), ("an", arrivals([near], 1))
-    for q in range(N):
-        act(T.ib[quad(q), 0:1], T.cnte[quad(PI[rank]), 0:1], AF.Copy, 0.5 * K, -K, ("ae", arrivals([near], 1)))
-    k = act(T.ib[:, 1:2], T.mo[:, 23:24], AF.Copy, 0.5 * K, -K, k_mo)
+    zc = lambda s: slice(max(2 * s - 1, 0), min(2 * s + 1, 6))
     k_num = act(T.num[:], T.xt[:, 0:XC], AF.Copy, -1.0, 0.0)
-    act(T.inv[:, 80 * near:80 * near + 80], T.i80[:], AF.Relu, T.ib[:, 0:1], K, k, k_80)
-    ki0 = act(T.inv[:, 80 * rank:80 * rank + 80], T.i80[:], AF.Relu, T.ib[:, 1:2], K)
+    for i in range(3):
+        act(T.kid[quad(i), :], T.p2[quad(i), :], AF.Copy, i + 1.0, 0.0)
+    for q in range(N):
+        act(T.ib[quad(q), near:near + 1], T.cnte[quad(PI[rank]), 0:1], AF.Copy, (0.5 - TOK / 2) * K, -0.5 * K, ("ae", arrivals([near], 1)))
+    k = act(T.ib[:, rank:rank + 1], T.mo[:, 23:24], AF.Copy, 0.5 * K, -K, k_mo)
+    for s in (near, rank):
+        act(T.zz[:, zc(s)], T.cz[:, zc(s)], AF.Relu, T.ib[:, s:s + 1], K, k, k_cz)
+        ki0 = act(T.inv[:, 80 * s:80 * s + 80], T.i80[:], AF.Relu, T.ib[:, s:s + 1], K)
 
     arr = lambda s: ("arr%d" % s, arrivals([s], 2))
     home = (pk[rank], psc[rank])
@@ -204,10 +215,9 @@ def rank_program(g, core, T, topo):
     if rank >= 2:
         halves.reverse()
     H = lambda a, b: (T.hq[:, a:b], T.hs[:, a:b])
-    P = lambda k: (T.r2p[:, 32 * k:32 * k + 128], T.r2ps[:, 32 * k:32 * k + 128])
     f0, g0 = halves[0][0], halves[1][0]
     F, G = slice(f0, f0 + NH), slice(g0, g0 + NH)
-    blk = [0, 128, 192] if f0 == 0 else [192, 64, 0]
+    kE, kO = (0, 2) if f0 == 0 else (2, 0)
 
     def products(h):
         c0, c1, who = halves[h]
@@ -223,20 +233,16 @@ def rank_program(g, core, T, topo):
         k3 = ts(hv(3), bank(4 * h + 3, c1 - c0), 0.0, 0.0625, OP.max, OP.mult, W[3])
         return quant(T.hq[:, c0:c1], T.hs[:, c0:c1], T.hb[:, 4 * c0:4 * c1], k0, k1, k2, k3)
 
-    def diff(k, j, c0, *d):
-        mm(bank(k, NH), *P(0), *H(c0, c0 + NH), True, False, *d)
-        return mm(bank(k, NH), *P(j), *H(c0, c0 + NH), False, True)
-
-    e4 = lambda k: T.ps[:, 512 * k + E4:512 * k + E4 + 1]
+    eblock = lambda b, k, *d: mm(bank(b, 128), *H(96 * k, 96 * k + 128), T.r2q[:], T.r2s[:], True, True, *d)
+    keep = lambda b, k, *d: act(T.es[:, 8 * k:8 * k + 5], bank(b, 5), AF.Copy, 0.0, 1.0, *d)
+    en = lambda k: T.es[:, 8 * k + E4:8 * k + E4 + 1]
     W0 = products(0)
     kq0 = tile(0, W0)
     W1 = products(1)
-    ea = mm(bank(0, NH), *P(7), *H(f0, f0 + NH), True, True, kq0, k_r2p, k_r2s)
-    e0 = mm(bank(1, 128), *H(blk[0], blk[0] + 128), T.r2q[:], T.r2s[:], True, True)
-    f1a = diff(2, 3, f0)
-    f2a = diff(3, 4, f0)
+    ea = mm(bank(0, NH), T.r2p[:], T.r2ps[:], *H(f0, f0 + NH), True, True, kq0, k_r2p, k_r2s)
+    eE = eblock(1, kE)
     kq1 = tile(1, W1)
-    ken0 = act(T.en[:, 0:1], e4(1), AF.Copy, 0.0, 1.0, e0)
+    k_sE = keep(1, kE, eE)
     k_ef = tt(T.em[:, F], bank(0, NH), T.inv[:, F], OP.add, ea, ki0)
     for s in range(N):
         src = T.msgi[0:80, 8 * s:8 * s + 1] if s != rank else T.mo[0:80, 22:23]
@@ -244,52 +250,73 @@ def rank_program(g, core, T, topo):
     d_vx = dma("s", "dvx", T.vxt[:], T.vx[:])
     d_vh = dma("s", "dvh", T.vht[:], T.vh[:])
 
-    eb = mm(bank(4, NH), *P(7), *H(g0, g0 + NH), True, True, kq1)
-    e2 = mm(bank(6, 128), *H(blk[2], blk[2] + 128), T.r2q[:], T.r2s[:], True, True)
-    e1 = mm(bank(5, 128), *H(blk[1], blk[1] + 128), T.r2q[:], T.r2s[:], True, True)
-    f1b = diff(7, 3, g0)
-    f2b = diff(1, 4, g0, ken0)
-    act(T.s1[:, F], bank(2, NH), AF.Sign, T.eb2[:], 1.0, f1a, k_e2)
-    k_sf = act(T.s2[:, F], bank(3, NH), AF.Sign, T.th2[:], 1.0, f2a)
-    ken2 = act(T.en[:, 2:3], e4(6), AF.Copy, 0.0, 1.0, e2)
+    eM = eblock(5, 1, kq1)
+    eb = mm(bank(4, NH), T.r2p[:], T.r2ps[:], *H(g0, g0 + NH), True, True)
+    eO = eblock(6, kO)
+    dg = lambda k: slice(96 * k, 96 * k + 128)
+    o_ = {kE: 0, kO: 192}
+    sign = lambda a, m, k, *d: act(T.sd[:, a:a + m.stop - m.start], T.em[:, m], AF.Sign, en(k), -1.0, *d)
+    k = act(T.ib[:, far[0]:far[0] + 2], T.msgi[:, 8 * far[0] + 1:8 * far[0] + 10:8], AF.Copy, 0.5 * K, -K, am)
+    k_gE = sign(0, dg(kE), kE, k_sE, k_ef)
+    k_sM = keep(5, 1, eM)
+    for s in far:
+        k_zz = act(T.zz[:, zc(s)], T.cz[:, zc(s)], AF.Relu, T.ib[:, s:s + 1], K, k)
+    k_sO = keep(6, kO, eO)
     for s in far:
         ki = ts(T.inv[:, 80 * s:80 * s + 80], T.i80[:], T.msgi[:, 8 * s + 1:8 * s + 2], BIG, OP.is_ge, OP.mult, am, k_80)
     k_em = tt(T.em[:, G], bank(4, NH), T.inv[:, G], OP.add, eb, ki)
-    ts(T.jk2[:, 320:480], T.em[:, F], T.en[:, 0:1], K, OP.is_lt, OP.mult, k_ef, ken0)
-    kc0 = ts(T.jk2[:, 480:640], T.em[:, G], T.en[:, 0:1], K, OP.is_lt, OP.mult, k_em)
-    kc1 = ts(T.jk2[:, 0:NX], T.em[:], e4(5), K, OP.is_lt, OP.mult, e1)
-    k = act(T.jk2[:, 640:960], T.em[:], AF.Sign, T.en[:, 2:3], -1.0, k_em, ken2)
-    k_cf = act(T.c2[:, F], T.s2[:, F], AF.Copy, 4.0, -1.0, k_sf)
-    kl2 = acc(T.jkb[:, 0:320], T.jk2[:, 640:960], AF.Relu, 0.0, K, T.lt[:, 2:3], k)
-    run(T.jkc[:, 320:640], T.jk2[:, 320:640], 128, NX, 0.0, kc0)
-    k = run(T.jkc[:, 0:320], T.jk2[:, 0:320], 128, NX, 0.0, kc1)
-    elem(T.uw[:, F], T.s1[:, F], T.c2[:, F], OP.subtract, k_cf)
-    kp = cp(T.lt[:, 0:2], T.jkc[:, 319:640:320], k)
-    act(T.s1[:, G], bank(7, NH), AF.Sign, T.eb2[:], 1.0, f1b)
-    k = act(T.s2[:, G], bank(1, NH), AF.Sign, T.th2[:], 1.0, f2b)
-    k_cc = act(T.c2[:, G], T.s2[:, G], AF.Copy, 4.0, -1.0, k)
-    ts(T.bc[:, 64:96], T.ck[:], T.lt[:, 2:3], T.en[:, 2:3], OP.subtract, OP.min, kl2, k_ck)
-    ts(T.bc[:, 0:32], T.ck[:], T.lt[:, 0:1], e4(5), OP.subtract, OP.min, kp)
-    k = ts(T.bc[:, 32:64], T.ck[:], T.lt[:, 1:2], T.en[:, 0:1], OP.subtract, OP.min)
+    k_gF = sign(256 + f0, F, 1, k_sM)
+    k_gG = sign(256 + g0, G, 1, k_em)
+    k_gO = sign(128, dg(kO), kO, k_sO)
+
+    def rest(k, *d):
+        a, b, o = (128, NX, OP.is_lt) if k == 0 else (0, 192, OP.is_le)
+        return ts(T.jk2[:, o_[k]:o_[k] + 192], T.em[:, a:b], en(k), -2.0, o, OP.mult, *d)
+
+    mix = lambda a, b, c, *d: elem(T.rd[:, a:b], T.sd[:, a:b], T.tri[:, c:c + b - a], OP.add, *d)
+    count = lambda a, b, k, *d: acc(T.jkb[:, a:b], T.rd[:, a:b], AF.Sign, T.h25[:], 1.0, T.lt[:, k:k + 1], *d)
+    room = lambda k, *d: run(T.jkc[:, o_[k]:o_[k] + 192], T.jk2[:, o_[k]:o_[k] + 192], 128, 192, 2.0 * DF - 1 - 128, *d)
+    wide = lambda k, *d: ts(T.ck[:, 32 * k:32 * k + 32], T.rtt[:, 32:64], T.jkc[:, o_[k] + 191:o_[k] + 192], None, OP.add, None, *d)
+    col = lambda i: T.es[:, srt[i]:24:8]
+    k_mE = mix(0, 128, 96, k_gE, k_cz)
+    k_pr = scan(T.pres[:], T.zr[:], T.zz[:], 0.0, OP.max, OP.subtract, k_zz)
+    k1 = rest(kE, k_em)
+    mix(256 + f0, 256 + f0 + NH, f0, k_gF)
+    tt(T.ka[:], col(1), col(0), OP.is_gt, k_sO)
+    k_mM = mix(256 + g0, 256 + g0 + NH, g0, k_gG)
+    k2 = tt(T.km[:], col(1), col(0), OP.max)
+    k_mO = mix(128, 256, 96, k_gO)
+    count(0, 128, kE, k_mE)
+    count(256, 576, 1, k_mM)
+    kl = count(128, 256, kO, k_mO)
+    k3 = rest(kO)
+    k2 = tt(T.kc[:], col(2), T.km[:], OP.is_gt, k2)
+    k1 = room(kE, k1)
+    k = room(kO, k3)
+    tt(T.ku[:], T.ka[:], T.kc[:], OP.max, k2)
+    k2 = tt(T.kv[:], T.kc[:], T.pres[:, 1:6:2], OP.add, k_pr)
+    wide(kE, k1)
+    k2 = tt(T.key[:], T.ku[:], T.kv[:], OP.add, k2)
+    k1 = wide(kO, k)
+    hand = lambda k, *d: ts(T.bc[:, 32 * k:32 * k + 32], T.ck[:, 32 * k:32 * k + 32], T.lt[:, k:k + 1], T.key[:, k:k + 1], OP.is_gt, OP.mult, *d)
+    hand(kE, k2, kl)
+    hand(1)
+    k = hand(kO, k1)
     k = op("v", lambda e: e.transpose(T.bt[:], T.bc[:]), k)
-    k = scan(T.gm[0:64, :], T.bt[0:64, :], T.bt[64:128, :], LOW, OP.max, OP.max, k)
-    for q in range(3):
-        k_tl = tt(T.tl[quad(q), :], T.gm[0:32, 95:96], T.gm[32:64, 95:96], OP.max, k)
-    k_uw = elem(T.uw[:, G], T.s1[:, G], T.c2[:, G], OP.subtract, k_cc)
+    for q in range(N):
+        for i in range(3):
+            o = T.mk3[quad(i), q:9:3, :] if q < 3 else T.mk3[quad(i), 9, :]
+            x = T.bt[quad(q), :] if q < 3 else T.bt[quad(q), 64:96]
+            if i == 2 or (q, i) == (3, 1):
+                k2 = act(o, x, AF.Copy, 0.0, 1.0, k)
+            else:
+                k1 = cp(o, x, k)
     Q = slice(0, 96)
-    k_sg = acc(T.sg[Q, :], T.em[Q, :], AF.Sign, T.tl[Q, :], -1.0, T.sa[Q, :], k_tl)
-    k_sb = act(T.sb[Q, :], T.sa[Q, :], AF.Copy, DF + 0.5 - 1.5 * NH, -0.5, k_sg)
-    k = ts(T.gd[Q, :], T.em[Q, :], T.tl[Q, :], None, OP.is_equal, None, k_tl)
-    k_nq = run(T.nq[Q, :], T.gd[Q, :], 96, NX, -1.0 * NH, k)
-    k_t1 = elem(T.t1[Q, :], T.sg[Q, :], T.uw[Q, :], OP.add, k_sg, k_uw)
-    k = ts(T.fit[Q, :], T.nq[Q, 319:320], 0.5, T.sb[Q, :], OP.mult, OP.add, k_nq, k_sb)
-    k = ts(T.nf[Q, :], T.nq[Q, :], T.fit[Q, :], 6.0, OP.is_gt, OP.add, k)
-    k = elem(T.t2[Q, :], T.t1[Q, :], T.nf[Q, :], OP.subtract, k, k_t1)
-    k = ts(T.mk2[Q, :], T.t2[Q, :], -8.5, None, OP.is_gt, None, k)
+    k = ts(T.mk2[Q, :], T.mk3[Q, :, :], T.kid[Q, :], None, OP.is_equal, None, k1, k2)
     k_c2 = run(T.cum2[Q, :], T.mk2[Q, :], 96, NX, 0.0, k)
-    ka = acc(T.jkb[Q, 320:640], T.cum2[Q, :], AF.Sign, T.csn[Q, 0:1], 1.0, T.cnt2[Q, 0:1], k_c2)
-    k = ts(T.jke[Q, 16:320], T.cum2[Q, 16:320], T.csp[Q, 1:2], 2.0, OP.is_gt, OP.mult, k_c2)
-    k = run(T.jke[Q, 336:640], T.jke[Q, 16:320], 96, NX - 16, -1.0 * NX, k)
+    ka = acc(T.jkb[Q, 576:896], T.cum2[Q, :], AF.Sign, T.csn[Q, 0:1], 1.0, T.cnt2[Q, 0:1], k_c2)
+    k = ts(T.jke[Q, 16:NX], T.cum2[Q, 16:NX], T.csp[Q, 1:2], 2.0, OP.is_gt, OP.mult, k_c2)
+    k = run(T.jke[Q, 336:640], T.jke[Q, 16:NX], 96, NX - 16, -1.0 * NX, k)
     kc = cp(T.cnt2[Q, 1:2], T.jke[Q, 639:640], k)
     off2 = lambda q, i: ts(T.off2[quad(q), 2 * i:2 * i + 2], T.cnt2[quad(srt.index(order[i])), :], -0.5, NX / 2.0, OP.mult, OP.add, kc, ka)
     todo = [(q, i) for i in range(3) for q in range(N)]

@@ -4,24 +4,24 @@ N, TOK, CAP, CB, DF = 4, 192, 80, 32, 80
 NX = N * CAP
 NH = NX // 2
 XC = 336
-TINY, BIG, K = 1e-33, 1e29, 2.0 ** 80
+TINY, K = 1e-33, 2.0 ** 80
 PI = [1, 0, 2, 3]
-E4, NRT = 4, 4
+E4 = 4
 Q8, U8, BF, F32 = "float8_e4m3fn_x4", "uint8", "bfloat16", "float32"
 SCRATCH = {"ps": ("psum", [128, 4096], F32), "mk3": ("sbuf", [128, 10, 32], BF)}
 for _d, _l in (
-        (Q8, dict(rtq=128, r2q=128, rpq=320, r2p=128, xq=194, wq=512, vxq=128, vhq=128, hq=XC, sl1=240, land1=XC, sl2=192, land2=208, fin=128)),
-        (U8, dict(rts=128, r2s=128, rps=320, r2ps=128, xs=194, wsc=512, vxs=128, vhs=128, hs=XC, ss1=240, lans1=XC, ss2=192, lans2=208, fins=128)),
-        (BF, dict(rtt=512, r2t=512, xt=776, wt=2048, vxt=512, vht=512, hb=4 * (NX + 2), mo=24, msgi=32, z1=192, mk=192, cum=192,
-                  jka=576, jkd=576, jkf=576, mk2=NX, cum2=NX, jk2=384, jkb=896, jke=640, jkc=384, nb=NX, tri=NX, trj=NX, sd=576, rd=576, bc=96, bt=96)),
+        (Q8, dict(rtq=128, rnq=128, r2q=128, rpq=320, r2p=128, xq=194, wq=512, vxq=128, vhq=128, hq=XC, sl1=240, land1=XC, sl2=192, land2=288, fin=128)),
+        (U8, dict(rts=128, rns=128, r2s=128, rps=320, r2ps=128, xs=194, wsc=512, vxs=128, vhs=128, hs=XC, ss1=240, lans1=XC, ss2=192, lans2=288, fins=128)),
+        (BF, dict(rtt=512, rnt=512, r2t=512, xt=776, wt=2048, vxt=512, vht=512, hb=4 * (NX + 2), mo=24, msgi=32, z1=192, mk=192, cum=192,
+                  jka=576, jkd=576, jkf=576, mk2=NX, cum2=NX, jk2=384, jkb=896, jke=640, jkc=384, nb=NX, tri=NX, sd=576, rd=576, bc=96)),
         (F32, dict(offf=24, diag=24, ib=4, cnte=4, cno=1, lwho=32, whot=32, z2=192, z3=192, cnt1=8, inv=NX, em=NX, lt=4, ck=96,
-                   es=24, cz=6, czi=6, zz=6, zr=6, pres=6, ka=3, km=3, kc=3, ku=3, kv=3, key=3, h25=1, kid=1,
+                   es=24, cz=6, czi=6, zz=6, zr=6, pres=6, ka=3, km=3, kc=3, ku=3, kv=3, key=3, h25=1, kid=1, p96=4,
                    cnt2=2, num=XC, wg=96, wtr=96, ys=128, th1=1, tn1=1, eb1=1, p2=1, pa=1, rf=1, b16=8, csp=8, csn=8, i80=80)),
-        ("int32", dict(ti=30, pI=1, rI=1)), ("uint16", dict(to=30, off1=24, off2=6, ofin=8))):
+        ("int32", dict(ti=34, pI=1, rI=1)), ("uint16", dict(to=34, off1=24, off2=6, ofin=8))):
     for _n, _w in _l.items():
         SCRATCH[_n] = ("sbuf", [128, _w], _d)
 SEMAPHORES = ["v", "a", "t", "gq", "dx", "drt", "dw", "dr2", "dvx", "dvh", "dnb", "dout", "ls",
-              "arr0", "arr1", "arr2", "arr3", "am", "an", "ae", "arrb", "aw"]
+              "arr0", "arr1", "arr2", "arr3", "am", "an", "ae", "ab0", "ab1", "ab2", "aw"]
 
 
 def rank_program(g, core, T, topo):
@@ -35,7 +35,6 @@ def rank_program(g, core, T, topo):
     order = sorted(others, key=lambda b: (b != near, topo.same_plane(topo.chip(cores[b]), me_chip)))
     far = sorted(order[1:])
     srt = sorted(others)
-    slot = lambda a, b: sorted(r for r in range(N) if r != b).index(a)
     eng = {"v": g.vector, "a": g.scalar, "t": g.tensor, "s": g.sync, "g": g}
     semof = {"v": "v", "a": "a", "t": "t", "g": "gq"}
     tot, seen = {}, {q: {} for q in eng}
@@ -77,6 +76,7 @@ def rank_program(g, core, T, topo):
     scan = lambda out, x, y, i, o0, o1, *d: op("v", lambda e: e.tensor_tensor_scan(out, x, y, i, o0, o1), *d)
     elem = lambda out, x, y, o, *d: scan(out, x, y, -64.0, OP.max, o, *d)
     run = lambda out, x, p, n, i, *d: scan(out, x, T.rtt[0:p, 32:32 + n], i, OP.add, OP.add, *d)
+    turn = lambda out, x, *d: op("v", lambda e: e.transpose(out, x), *d)
     quant = lambda q, s, x, *d: op("v", lambda e: e.quantize_mx(q, s, x), *d)
     act = lambda out, x, f, b, s, *d: op("a", lambda e: e.activation(out, x, f, bias=b, scale=s), *d)
     acc = lambda out, x, f, b, s, o, *d: op("a", lambda e: e.activation(out, x, f, bias=b, scale=s, accum_out=o), *d)
@@ -109,56 +109,60 @@ def rank_program(g, core, T, topo):
 
     k_p2 = gf(T.p2[:], [[0, 1]], -127, 2)
     k_pI = gi(T.pI[:], [[0, 1]], 0, 1)
-    k_t1 = table(0, PI + [NRT + PI[(1 + j) % N] for j in range(6)])
+    k_t1 = table(0, PI + [PI[(1 + j) % N] for j in range(6)])
     k_16 = gf(T.b16[:], [[16, 8]], 0, 0)
     k = gf(T.diag[:], [[0, 4], [-3200, 6]], 200, 200)
-    k_t2 = table(20, [E4] * 4 + [TOK])
+    k_t2 = table(20, [E4] * 4 + [TOK] * 3)
     k1 = gf(T.czi[:], [[16, 3], [-CAP, 2]], 0, 1)
     k_dg = gf(T.diag[:, 5:24:6], [[0, 4]], 1000, 0, k)
+    gf(T.p96[:], [[-CAP, N]], 96, 1)
     k_80 = gf(T.i80[:], [[1, 80]], 0, 0)
     gf(T.zr[:], [[0, 3], [-30001, 2]], 1, 0)
-    op("g", lambda e: e.affine_select(T.cz[:], T.czi[:], [[-16, 3], [200, 2]], OP.is_ge, -1000.0, CAP - 1, -1), k1)
-    k_z0 = ms(T.rtt[:, 32:512], 0.0)
+    k_cz = op("g", lambda e: e.affine_select(T.cz[:], T.czi[:], [[-16, 3], [200, 2]], OP.is_ge, -1000.0, CAP - 1, -1), k1)
+    k_z0 = ms(T.rtt[:, 16:512], 0.0)
     k_x0 = ms(T.xt[:, 768:776], 0.0)
     k = ts(T.rI[:], T.pI[:], 15, None, OP.bitwise_and, None, k_pI)
-    k_tj = ms(T.trj[:], -2.0)
+    k_zn = ms(T.rnt[:, 16:512], 0.0)
     k_rf = ts(T.rf[:], T.rI[:], -1.0, -0.5, OP.mult, OP.add, k)
     ms(T.ck[:, 32:64], 2.0 * DF - 1 - NX)
     ms(T.h25[:], 2.5)
     k_lw = ms(T.lwho[:], -1.0)
-    k_ng = ms(T.r2t[:, 24:512], 0.0)
-    k_cz = op("g", lambda e: e.affine_select(T.tri[:], T.trj[:], [[-1, NX]], OP.is_gt, -3.0, 96, 1), k_tj)
     k = act(T.pa[:], T.p2[:], AF.Abs, 0.0, 1.0, k_p2)
     k_th = act(T.th1[:], T.p2[:], AF.Copy, 0.0, TINY)
     act(T.tn1[:], T.p2[:], AF.Copy, 0.0, -TINY)
     k_eb = act(T.eb1[:], T.pa[:], AF.Copy, 64 * TINY, -TINY, k)
 
-    k = ts(T.rtt[:, 16:32], T.rtt[:, 0:16], -1.0, None, OP.mult, None, d_rt)
-    k_rq = quant(T.rtq[:], T.rts[:], T.rtt[:], k, k_z0)
+    k = act(T.rnt[:, 0:16], T.rtt[:, 0:16], AF.Copy, 0.0, -1.0, d_rt)
+    k_rq = quant(T.rtq[:], T.rts[:], T.rtt[:], d_rt, k_z0)
     k_o1 = cp(T.to[:, 0:20], T.ti[:, 0:20], k_t1)
-    kp1 = pickq(T.rpq[:, 0:256], T.rtq[:], T.to[:, 0:16], k_rq, k_o1)
-    ks1 = picks(T.rps[:, 0:256], T.rts[:], T.to[:, 0:16], k_rq, k_o1)
+    k_nq = quant(T.rnq[:], T.rns[:], T.rnt[:], k, k_zn)
+    kp0 = pickq(T.rpq[:, 0:128], T.rtq[:], T.to[:, 0:8], k_rq, k_o1)
+    ks0 = picks(T.rps[:, 0:128], T.rts[:], T.to[:, 0:8], k_rq, k_o1)
     k_xq = quant(T.xq[:], T.xs[:], T.xt[:], d_x, k_x0)
-    kp2 = pickq(T.rpq[:, 256:320], T.rtq[:], T.to[:, 16:20])
-    ks2 = picks(T.rps[:, 256:320], T.rts[:], T.to[:, 16:20])
-    dm = []
-    for j in range(3):
-        mm(bank(j, 192), T.rpq[:, 0:128], T.rps[:, 0:128], T.xq[:, 0:192], T.xs[:, 0:192], True, False, kp1, ks1, k_xq)
-        a = 128 + 32 * j
-        dj = (kp2, ks2) if j else ()
-        dm.append(mm(bank(j, 192), T.rpq[:, a:a + 128], T.rps[:, a:a + 128], T.xq[:, 0:192], T.xs[:, 0:192], False, True, *dj))
-    k_z1 = act(T.z1[:], bank(0, 192), AF.Sign, T.eb1[:], 1.0, dm[0], k_eb)
+    kp1 = pickq(T.rpq[:, 128:256], T.rnq[:], T.to[:, 8:16], k_nq)
+    ks1 = picks(T.rps[:, 128:256], T.rns[:], T.to[:, 8:16], k_nq)
+    kp2 = pickq(T.rpq[:, 256:320], T.rnq[:], T.to[:, 16:20])
+    ks2 = picks(T.rps[:, 256:320], T.rns[:], T.to[:, 16:20])
+    k_ng = ms(T.r2t[:, 24:512], 0.0)
+    score = lambda j, a, first, *d: mm(bank(j, 192), T.rpq[:, a:a + 128], T.rps[:, a:a + 128], T.xq[:, 0:192], T.xs[:, 0:192], first, not first, *d)
+    score(0, 0, True, kp0, ks0, k_xq)
+    score(1, 0, True)
+    dm = [score(0, 128, False, kp1, ks1)]
+    score(2, 0, True)
+    dm += [score(1, 160, False, kp2, ks2), score(2, 192, False)]
+    two = [slice(0, 96), slice(96, 192)]
+    kz = [act(T.z1[:, h], T.ps[:, h], AF.Sign, T.eb1[:], 1.0, dm[0], k_eb) for h in two]
+    k_z1 = kz[1]
     k = act(T.csn[:], T.b16[:], AF.Identity, T.rf[:], -1.0, k_16, k_rf)
     k_cs = act(T.csp[:], T.csn[:], AF.Copy, 0.0, -1.0, k)
-    two = [slice(0, 96), slice(96, 192)]
-    kk = [tt(T.z2[:, h], T.ps[:, 512 + h.start:512 + h.stop], T.z1[:, h], OP.min, dm[1], k_z1) for h in two]
+    kk = [tt(T.z2[:, h], T.ps[:, 512 + h.start:512 + h.stop], T.z1[:, h], OP.min, dm[1], k) for h, k in zip(two, kz)]
     kk = [tt(T.z3[:, h], T.ps[:, 1024 + h.start:1024 + h.stop], T.z2[:, h], OP.min, dm[2], k) for h, k in zip(two, kk)]
     k_d1 = kk[1]
     k = acc(T.jka[:, 384:576], T.z3[:], AF.Sign, T.tn1[:], 1.0, T.cno[:], k_d1)
     send(near, T.cnte[:, 0:1], T.cno[:], "ae", k)
     kk = [ts(T.mk[:, h], T.z3[:, h], T.th1[:], None, OP.is_gt, None, k, k_th) for h, k in zip(two, kk)]
     k = run(T.cum[:, 0:96], T.mk[:, 0:96], 128, 96, 0.0, kk[0])
-    k_o2 = cp(T.to[:, 20:30], T.ti[:, 20:30], k_t2)
+    k_o2 = cp(T.to[:, 20:34], T.ti[:, 20:34], k_t2)
     k_cum = run(T.cum[:, 96:192], T.mk[:, 96:192], 128, 96, T.cum[:, 95:96], k, kk[1])
     for c in range(2):
         acc(T.jka[:, 192 * c:192 * c + 192], T.cum[:], AF.Sign, T.csn[:, c:c + 1], 1.0, T.cnt1[:, c:c + 1], k_cum, k_cs)
@@ -197,11 +201,12 @@ def rank_program(g, core, T, topo):
     k_r2p = pickq(T.r2p[:], T.r2q[:], T.to[:, 20:28], k_r2q)
     k_zs = picks(T.lans1[:, NX:XC], T.xs[:, 0:194], ozero, k_o2)
     k_r2s = picks(T.r2ps[:], T.r2s[:], T.to[:, 20:28], k_r2q)
+    for s in range(N):
+        ts(T.tri[:, 80 * s:80 * s + 80], T.i80[:], T.p96[:, s:s + 1], -3.0, OP.is_lt, OP.add, k_80)
     am, an = ("am", arrivals(far, 1)), ("an", arrivals([near], 1))
     zc = lambda s: slice(max(2 * s - 1, 0), min(2 * s + 1, 6))
     k_num = act(T.num[:], T.xt[:, 0:XC], AF.Copy, -1.0, 0.0)
-    for i in range(3):
-        act(T.kid[quad(i), :], T.p2[quad(i), :], AF.Copy, i + 1.0, 0.0)
+    act(T.kid[:], T.p2[:], AF.Copy, -2.0, 0.0)
     for q in range(N):
         act(T.ib[quad(q), near:near + 1], T.cnte[quad(PI[rank]), 0:1], AF.Copy, (0.5 - TOK / 2) * K, -0.5 * K, ("ae", arrivals([near], 1)))
     k = act(T.ib[:, rank:rank + 1], T.mo[:, 23:24], AF.Copy, 0.5 * K, -K, k_mo)
@@ -242,7 +247,6 @@ def rank_program(g, core, T, topo):
     ea = mm(bank(0, NH), T.r2p[:], T.r2ps[:], *H(f0, f0 + NH), True, True, kq0, k_r2p, k_r2s)
     eE = eblock(1, kE)
     kq1 = tile(1, W1)
-    k_sE = keep(1, kE, eE)
     k_ef = tt(T.em[:, F], bank(0, NH), T.inv[:, F], OP.add, ea, ki0)
     for s in range(N):
         src = T.msgi[0:80, 8 * s:8 * s + 1] if s != rank else T.mo[0:80, 22:23]
@@ -250,20 +254,22 @@ def rank_program(g, core, T, topo):
     d_vx = dma("s", "dvx", T.vxt[:], T.vx[:])
     d_vh = dma("s", "dvh", T.vht[:], T.vh[:])
 
-    eM = eblock(5, 1, kq1)
-    eb = mm(bank(4, NH), T.r2p[:], T.r2ps[:], *H(g0, g0 + NH), True, True)
+    eb = mm(bank(4, NH), T.r2p[:], T.r2ps[:], *H(g0, g0 + NH), True, True, kq1)
+    eM = eblock(5, 1)
     eO = eblock(6, kO)
     dg = lambda k: slice(96 * k, 96 * k + 128)
     o_ = {kE: 0, kO: 192}
     sign = lambda a, m, k, *d: act(T.sd[:, a:a + m.stop - m.start], T.em[:, m], AF.Sign, en(k), -1.0, *d)
     k = act(T.ib[:, far[0]:far[0] + 2], T.msgi[:, 8 * far[0] + 1:8 * far[0] + 10:8], AF.Copy, 0.5 * K, -K, am)
-    k_gE = sign(0, dg(kE), kE, k_sE, k_ef)
-    k_sM = keep(5, 1, eM)
+    k_sE = keep(1, kE, eE)
     for s in far:
         k_zz = act(T.zz[:, zc(s)], T.cz[:, zc(s)], AF.Relu, T.ib[:, s:s + 1], K, k)
-    k_sO = keep(6, kO, eO)
     for s in far:
-        ki = ts(T.inv[:, 80 * s:80 * s + 80], T.i80[:], T.msgi[:, 8 * s + 1:8 * s + 2], BIG, OP.is_ge, OP.mult, am, k_80)
+        ki = act(T.inv[:, 80 * s:80 * s + 80], T.i80[:], AF.Relu, T.ib[:, s:s + 1], K)
+    k_gE = sign(0, dg(kE), kE, k_sE, k_ef)
+    k_sM = keep(5, 1, eM)
+    k_sO = keep(6, kO, eO)
+    k_pr = scan(T.pres[:], T.zr[:], T.zz[:], 0.0, OP.max, OP.subtract, k_zz)
     k_em = tt(T.em[:, G], bank(4, NH), T.inv[:, G], OP.add, eb, ki)
     k_gF = sign(256 + f0, F, 1, k_sM)
     k_gG = sign(256 + g0, G, 1, k_em)
@@ -276,48 +282,44 @@ def rank_program(g, core, T, topo):
     mix = lambda a, b, c, *d: elem(T.rd[:, a:b], T.sd[:, a:b], T.tri[:, c:c + b - a], OP.add, *d)
     count = lambda a, b, k, *d: acc(T.jkb[:, a:b], T.rd[:, a:b], AF.Sign, T.h25[:], 1.0, T.lt[:, k:k + 1], *d)
     room = lambda k, *d: run(T.jkc[:, o_[k]:o_[k] + 192], T.jk2[:, o_[k]:o_[k] + 192], 128, 192, 2.0 * DF - 1 - 128, *d)
-    wide = lambda k, *d: ts(T.ck[:, 32 * k:32 * k + 32], T.rtt[:, 32:64], T.jkc[:, o_[k] + 191:o_[k] + 192], None, OP.add, None, *d)
+    wide = lambda k, *d: act(T.ck[:, 32 * k:32 * k + 32], T.rtt[:, 32:64], AF.Identity, T.jkc[:, o_[k] + 191:o_[k] + 192], 1.0, *d)
     col = lambda i: T.es[:, srt[i]:24:8]
-    k_mE = mix(0, 128, 96, k_gE, k_cz)
-    k_pr = scan(T.pres[:], T.zr[:], T.zz[:], 0.0, OP.max, OP.subtract, k_zz)
+    k_mE = mix(0, 128, 96, k_gE)
     k1 = rest(kE, k_em)
+    k3 = rest(kO, k_sO)
     mix(256 + f0, 256 + f0 + NH, f0, k_gF)
-    tt(T.ka[:], col(1), col(0), OP.is_gt, k_sO)
     k_mM = mix(256 + g0, 256 + g0 + NH, g0, k_gG)
+    tt(T.ka[:], col(1), col(0), OP.is_gt)
     k2 = tt(T.km[:], col(1), col(0), OP.max)
     k_mO = mix(128, 256, 96, k_gO)
     count(0, 128, kE, k_mE)
     count(256, 576, 1, k_mM)
-    kl = count(128, 256, kO, k_mO)
-    k3 = rest(kO)
+    count(128, 256, kO, k_mO)
     k2 = tt(T.kc[:], col(2), T.km[:], OP.is_gt, k2)
     k1 = room(kE, k1)
-    k = room(kO, k3)
     tt(T.ku[:], T.ka[:], T.kc[:], OP.max, k2)
     k2 = tt(T.kv[:], T.kc[:], T.pres[:, 1:6:2], OP.add, k_pr)
-    wide(kE, k1)
-    k2 = tt(T.key[:], T.ku[:], T.kv[:], OP.add, k2)
+    k = room(kO, k3)
+    kl = wide(kE, k1)
     k1 = wide(kO, k)
+    k2 = tt(T.key[:], T.ku[:], T.kv[:], OP.add, k2)
     hand = lambda k, *d: ts(T.bc[:, 32 * k:32 * k + 32], T.ck[:, 32 * k:32 * k + 32], T.lt[:, k:k + 1], T.key[:, k:k + 1], OP.is_gt, OP.mult, *d)
-    hand(kE, k2, kl)
-    hand(1)
+    hand(1, k2, kl)
+    hand(kE)
     k = hand(kO, k1)
-    k = op("v", lambda e: e.transpose(T.bt[:], T.bc[:]), k)
     for q in range(N):
-        for i in range(3):
-            o = T.mk3[quad(i), q:9:3, :] if q < 3 else T.mk3[quad(i), 9, :]
-            x = T.bt[quad(q), :] if q < 3 else T.bt[quad(q), 64:96]
-            if i == 2 or (q, i) == (3, 1):
-                k2 = act(o, x, AF.Copy, 0.0, 1.0, k)
-            else:
-                k1 = cp(o, x, k)
+        k1 = turn(T.mk3[0:32, q:9:3, :], T.bc[quad(q), :], k) if q < 3 else turn(T.mk3[0:32, 9, :], T.bc[quad(q), 64:96])
+    k2 = act(T.mk2[quad(2), :], T.mk3[0:32, :, :], AF.Relu, T.kid[0:32, :], 1.0, k1)
+    for i in range(2):
+        k = ts(T.mk2[quad(i), :], T.mk3[0:32, :, :], i + 1.0, None, OP.is_equal, None, k1)
     Q = slice(0, 96)
-    k = ts(T.mk2[Q, :], T.mk3[Q, :, :], T.kid[Q, :], None, OP.is_equal, None, k1, k2)
-    k_c2 = run(T.cum2[Q, :], T.mk2[Q, :], 96, NX, 0.0, k)
+    k_c2 = run(T.cum2[Q, :], T.mk2[Q, :], 96, NX, 0.0, k, k2)
     ka = acc(T.jkb[Q, 576:896], T.cum2[Q, :], AF.Sign, T.csn[Q, 0:1], 1.0, T.cnt2[Q, 0:1], k_c2)
-    k = ts(T.jke[Q, 16:NX], T.cum2[Q, 16:NX], T.csp[Q, 1:2], 2.0, OP.is_gt, OP.mult, k_c2)
-    k = run(T.jke[Q, 336:640], T.jke[Q, 16:NX], 96, NX - 16, -1.0 * NX, k)
-    kc = cp(T.cnt2[Q, 1:2], T.jke[Q, 639:640], k)
+    k0 = ts(T.jke[Q, 16:168], T.cum2[Q, 16:168], T.csp[Q, 1:2], 2.0, OP.is_gt, OP.mult, k_c2)
+    k1 = ts(T.jke[Q, 168:NX], T.cum2[Q, 168:NX], T.csp[Q, 1:2], 2.0, OP.is_gt, OP.mult)
+    run(T.jke[Q, 336:488], T.jke[Q, 16:168], 96, 152, -1.0 * NX, k0)
+    k = run(T.jke[Q, 488:640], T.jke[Q, 168:NX], 96, 152, 0.0, k1)
+    kc = tt(T.cnt2[Q, 1:2], T.jke[Q, 487:488], T.jke[Q, 639:640], OP.add, k)
     off2 = lambda q, i: ts(T.off2[quad(q), 2 * i:2 * i + 2], T.cnt2[quad(srt.index(order[i])), :], -0.5, NX / 2.0, OP.mult, OP.add, kc, ka)
     todo = [(q, i) for i in range(3) for q in range(N)]
     k_of = [off2(*todo[j]) for j in range(6)]
@@ -327,39 +329,39 @@ def rank_program(g, core, T, topo):
         kk = pickq(T.sl2[:, o + 32:o + 64], T.hq[:, 0:NX + 2], lst)
         picks(T.ss2[:, o:o + 32], T.lans1[:], lst, ko)
         ks = picks(T.ss2[:, o + 32:o + 64], T.hs[:, 0:NX + 2], lst)
-        d = slice(64 * slot(rank, b), 64 * slot(rank, b) + 64)
-        send(b, c8(T.land2[:, d]), c8(T.sl2[:, o:o + 64]), "arrb", kk)
-        send(b, T.lans2[:, d], T.ss2[:, o:o + 64], "arrb", ks)
+        d = slice(96 + o, 160 + o)
+        send(b, c8(T.land2[:, d]), c8(T.sl2[:, o:o + 64]), "ab%d" % i, kk)
+        send(b, T.lans2[:, d], T.ss2[:, o:o + 64], "ab%d" % i, ks)
         k_of += [off2(*x) for x in todo[4 * i + 6:4 * i + 10]]
         if i < 2:
             for s in (2 * i, 2 * i + 1):
                 k_n = act(T.num[0:1, 80 * s:80 * s + 80], T.nb[0:1, 80 * s:80 * s + 80], AF.Copy, float(TOK * s), 1.0, d_nb, k_num)
     kw = op("a", lambda e: e.activation(T.wg[:], T.num[:].indirect(T.off2[:]), AF.Copy), k_n)
-    kw = op("v", lambda e: e.transpose(T.wtr[:], T.wg[:]), kw)
+    kw = turn(T.wtr[:], T.wg[:], kw)
     for i, b in enumerate(order):
         send(b, T.lwho[:, rank:rank + 1], T.wtr[:, 32 * i:32 * i + 1], "aw", kw)
 
+    k_z2 = pickq(T.land2[:, 0:96], T.xq[:, 0:194], T.to[:, 28:34])
+    k_z2s = picks(T.lans2[:, 0:96], T.xs[:, 0:194], T.to[:, 28:34])
     k_vx = quant(T.vxq[:], T.vxs[:], T.vxt[:], d_vx)
     k_vh = quant(T.vhq[:], T.vhs[:], T.vht[:], d_vh)
-    k_z2 = pickq(T.land2[:, 192:208], T.xq[:, 0:194], ozero)
-    k_z2s = picks(T.lans2[:, 192:208], T.xs[:, 0:194], ozero)
+    for j in range(3):
+        k_ofin = ts(T.ofin[:, 2 * j:2 * j + 2], T.csp[:, 0:2], 128.0 + 64 * j - 0.5, None, OP.add, None)
     ms(T.ys[:, CB * rank:CB * rank + CB], 0.0)
-    ms(T.ofin[:, 2 * rank:2 * rank + 2], 192)
-    for a in others:
-        k_ofin = ts(T.ofin[:, 2 * a:2 * a + 2], T.csp[:, 0:2], 64.0 * slot(a, rank) + CB - 0.5, None, OP.add, None)
+    pickq(T.fin[:, CB * rank:CB * rank + CB], T.xq[:, 0:194], T.to[:, 28:30])
+    picks(T.fins[:, CB * rank:CB * rank + CB], T.xs[:, 0:194], T.to[:, 28:30])
 
-    ab = ("arrb", arrivals(others, 2))
-    mm(bank(0, 160), T.vxq[:], T.vxs[:], T.land2[:, 0:160], T.lans2[:, 0:160], True, False, ab, k_vx, k_vh)
-    ty = mm(bank(0, 160), T.vhq[:], T.vhs[:], T.land2[:, 32:192], T.lans2[:, 32:192], False, True)
-    kf = pickq(T.fin[:], T.land2[:], T.ofin[:], ab, k_ofin, k_z2)
-    kfs = picks(T.fins[:], T.lans2[:], T.ofin[:], ab, k_ofin, k_z2s)
-    for a in others:
-        c0 = 64 * slot(a, rank)
-        ky = cp(T.ys[:, CB * a:CB * a + CB], T.ps[:, c0:c0 + CB], ty)
+    for j, a in enumerate(order):
+        ab, o, pl = ("ab%d" % j, arrivals([a], 2)), 64 * j, slice(CB * a, CB * a + CB)
+        mm(bank(j, 128), T.vxq[:], T.vxs[:], T.land2[:, o:o + 128], T.lans2[:, o:o + 128], True, False, ab, k_vx, k_vh, k_z2s)
+        ty = mm(bank(j, 128), T.vhq[:], T.vhs[:], T.land2[:, o + 32:o + 160], T.lans2[:, o + 32:o + 160], False, True)
+        kfs = picks(T.fins[:, pl], T.lans2[:, 0:o + 160], T.ofin[:, 2 * j:2 * j + 2], ab, k_ofin, k_z2s)
+        kf = pickq(T.fin[:, pl], T.land2[:, 0:o + 160], T.ofin[:, 2 * j:2 * j + 2], ab, k_ofin)
+        ky = cp(T.ys[:, pl], T.ps[:, 512 * j + 96:512 * j + 128], ty)
     dma("s", "dout", T.oc[:], c8(T.fin[:]), kf)
     for k in range(4):
         dma("s" if k < 2 else "a", "dout", T.osc[4 * k:4 * k + 4, :], T.fins[32 * k:32 * k + 4, :], kfs)
     dma("a", "dout", T.y[:], T.ys[:], ky)
-    kw = op("v", lambda e: e.transpose(T.whot[:], T.lwho[:]), ("aw", arrivals(others, 1)), k_lw)
+    kw = turn(T.whot[:], T.lwho[:], ("aw", arrivals(others, 1)), k_lw)
     dma("s", "dout", T.who[:], T.whot[0:4, :], kw)
     wait("g", [(s, n) for s, n in tot.items()])

from concourse.mybir import dt, AluOpType as OP, AxisListType, ActivationFunctionType as AF

N, TOK, CAP, CB, DF = 4, 192, 80, 32, 80
NX = N * CAP
NH = NX // 2
XC = 336
TINY, K = 1e-33, 2.0 ** 80
PI = [1, 0, 2, 3]
E4 = 4
Q8, U8, BF, F32 = "float8_e4m3fn_x4", "uint8", "bfloat16", "float32"
SCRATCH = {"ps": ("psum", [128, 4096], F32), "mk3": ("sbuf", [128, 10, 32], BF)}
for _d, _l in (
        (Q8, dict(rtq=128, rnq=128, r2q=128, rpq=320, r2p=128, xq=194, wq=512, vxq=128, vhq=128, hq=XC, sl1=240, land1=XC, sl2=192, land2=288, fin=128)),
        (U8, dict(rts=128, rns=128, r2s=128, rps=320, r2ps=128, xs=194, wsc=512, vxs=128, vhs=128, hs=XC, ss1=240, lans1=XC, ss2=192, lans2=288, fins=128)),
        (BF, dict(rtt=512, rnt=512, r2t=512, xt=776, wt=2048, vxt=512, vht=512, hb=4 * (NX + 2), mo=24, msgi=32, z1=192, mk=192, cum=192,
                  jka=576, jkd=576, jkf=576, mk2=NX, cum2=NX, jk2=384, jkb=896, jke=640, jkc=384, nb=NX, tri=NX, sd=576, rd=576, bc=96)),
        (F32, dict(offf=24, diag=24, ib=4, cnte=4, cno=1, lwho=32, whot=32, z2=192, z3=192, cnt1=8, inv=NX, em=NX, lt=4, ck=96,
                   es=24, cz=6, czi=6, zz=6, zr=6, pres=6, ka=3, km=3, kc=3, ku=3, kv=3, key=3, h25=1, kid=1, p96=4,
                   cnt2=2, num=XC, wg=96, wtr=96, ys=128, th1=1, tn1=1, eb1=1, p2=1, pa=1, rf=1, b16=8, csp=8, csn=8, i80=80)),
        ("int32", dict(ti=34, pI=1, rI=1)), ("uint16", dict(to=34, off1=24, off2=6, ofin=8))):
    for _n, _w in _l.items():
        SCRATCH[_n] = ("sbuf", [128, _w], _d)
SEMAPHORES = ["v", "a", "t", "gq", "dx", "drt", "dw", "dr2", "dvx", "dvh", "dnb", "dout", "ls",
              "arr0", "arr1", "arr2", "arr3", "am", "an", "ae", "ab0", "ab1", "ab2", "aw"]


def rank_program(g, core, T, topo):
    rank = T.rank_of(core)
    if rank is None:
        return
    cores = list(T.cores)
    me_chip = topo.chip(core)
    others = [(rank + 1 + k) % N for k in range(N - 1)]
    near = rank ^ 1
    order = sorted(others, key=lambda b: (b != near, topo.same_plane(topo.chip(cores[b]), me_chip)))
    far = sorted(order[1:])
    srt = sorted(others)
    eng = {"v": g.vector, "a": g.scalar, "t": g.tensor, "s": g.sync, "g": g}
    semof = {"v": "v", "a": "a", "t": "t", "g": "gq"}
    tot, seen = {}, {q: {} for q in eng}

    def wait(q, deps):
        for s, n in deps:
            if seen[q].get(s, 0) < n:
                eng[q].wait_ge(T.sem[s], n)
                seen[q][s] = n

    def op(q, fn, *deps):
        wait(q, deps)
        s = semof[q]
        fn(eng[q]).then_inc(T.sem[s], 1)
        tot[s] = tot.get(s, 0) + 1
        return (s, tot[s])

    def dma(q, s, out, src, *deps):
        wait(q, deps)
        eng[q].dma_start(out, src).then_inc(T.sem[s], 16)
        tot[s] = tot.get(s, 0) + 16
        return (s, tot[s])

    def send(b, out, src, sem, *deps):
        wait("g", deps)
        rid, pid, _ = topo.addr(cores[b])
        g.remote_dma(out, src, T.sem[sem], T.sem.ls, pid, rid, topo.mask(core, cores[b]))
        tot["ls"] = tot.get("ls", 0) + len(topo.engines(core, cores[b]))

    def arrivals(srcs, per):
        return per * sum(len(topo.engines(cores[s], core)) for s in srcs)

    u8, u32 = dt.uint8, dt.uint32
    c8 = lambda v: v.bitcast(u8)
    ms = lambda ap, val, *d: op("v", lambda e: e.memset(ap, val), *d)
    ts = lambda out, x, s1, s2, o0, o1, *d: op("v", lambda e: e.tensor_scalar(out, x, s1, s2, o0) if o1 is None else e.tensor_scalar(out, x, s1, s2, o0, o1), *d)
    tt = lambda out, x, y, o, *d: op("v", lambda e: e.tensor_tensor(out, x, y, o), *d)
    cp = lambda out, x, *d: op("v", lambda e: e.tensor_copy(out, x), *d)
    scan = lambda out, x, y, i, o0, o1, *d: op("v", lambda e: e.tensor_tensor_scan(out, x, y, i, o0, o1), *d)
    elem = lambda out, x, y, o, *d: scan(out, x, y, -64.0, OP.max, o, *d)
    run = lambda out, x, p, n, i, *d: scan(out, x, T.rtt[0:p, 32:32 + n], i, OP.add, OP.add, *d)
    turn = lambda out, x, *d: op("v", lambda e: e.transpose(out, x), *d)
    quant = lambda q, s, x, *d: op("v", lambda e: e.quantize_mx(q, s, x), *d)
    act = lambda out, x, f, b, s, *d: op("a", lambda e: e.activation(out, x, f, bias=b, scale=s), *d)
    acc = lambda out, x, f, b, s, o, *d: op("a", lambda e: e.activation(out, x, f, bias=b, scale=s, accum_out=o), *d)
    pickq = lambda out, win, off, *d: op("v", lambda e: e.tensor_copy(out.bitcast(u32), win.bitcast(u32).indirect(off)), *d)
    picks = lambda out, win, off, *d: op("a", lambda e: e.activation(out, win.indirect(off), AF.Copy), *d)
    quad = lambda q: slice(32 * q, 32 * q + 32)
    bank = lambda k, n: T.ps[:, 512 * k:512 * k + n]

    def mm(out, w, ws, x, xs, start, stop, *d):
        return op("t", lambda e: e.matmul_mx(out, w, ws, x, xs, start, stop), *d)

    d_rt = dma("a", "drt", T.rtt[:, 0:16], T.rt[:, 0:16])
    d_x = dma("s", "dx", T.xt[:, 0:768], T.x[:])
    d_w = dma("s", "dw", T.wt[:], T.w[:], d_x)
    d_r2 = dma("s", "dr2", T.r2t[:, 0:24], T.r2[:, 0:24])

    gi = lambda out, pat, base, cmul: op("g", lambda e: e.iota(out, pat, base, cmul))
    gf = lambda out, pat, base, cmul, *d: op("g", lambda e: e.iota(out, pat, base, cmul, allow_small_or_imprecise_dtypes=True), *d)

    def table(c, vals):
        j = 0
        while j < len(vals):
            n = 2
            while j + n < len(vals) and vals[j + n] - vals[j + n - 1] == vals[j + 1] - vals[j]:
                n += 1
            n = min(n, len(vals) - j)
            k = gi(T.ti[:, c + 2 * j:c + 2 * j + 2 * n], [[vals[j + 1] - vals[j] if n > 1 else 0, n], [0, 2]], vals[j], 0)
            j += n
        return k

    k_p2 = gf(T.p2[:], [[0, 1]], -127, 2)
    k_pI = gi(T.pI[:], [[0, 1]], 0, 1)
    k_t1 = table(0, PI + [PI[(1 + j) % N] for j in range(6)])
    k_16 = gf(T.b16[:], [[16, 8]], 0, 0)
    k = gf(T.diag[:], [[0, 4], [-3200, 6]], 200, 200)
    k_t2 = table(20, [E4] * 4 + [TOK] * 3)
    k1 = gf(T.czi[:], [[16, 3], [-CAP, 2]], 0, 1)
    k_dg = gf(T.diag[:, 5:24:6], [[0, 4]], 1000, 0, k)
    gf(T.p96[:], [[-CAP, N]], 96, 1)
    k_80 = gf(T.i80[:], [[1, 80]], 0, 0)
    gf(T.zr[:], [[0, 3], [-30001, 2]], 1, 0)
    k_cz = op("g", lambda e: e.affine_select(T.cz[:], T.czi[:], [[-16, 3], [200, 2]], OP.is_ge, -1000.0, CAP - 1, -1), k1)
    k_z0 = ms(T.rtt[:, 16:512], 0.0)
    k_x0 = ms(T.xt[:, 768:776], 0.0)
    k = ts(T.rI[:], T.pI[:], 15, None, OP.bitwise_and, None, k_pI)
    k_zn = ms(T.rnt[:, 16:512], 0.0)
    k_rf = ts(T.rf[:], T.rI[:], -1.0, -0.5, OP.mult, OP.add, k)
    ms(T.ck[:, 32:64], 2.0 * DF - 1 - NX)
    ms(T.h25[:], 2.5)
    k_lw = ms(T.lwho[:], -1.0)
    k = act(T.pa[:], T.p2[:], AF.Abs, 0.0, 1.0, k_p2)
    k_th = act(T.th1[:], T.p2[:], AF.Copy, 0.0, TINY)
    act(T.tn1[:], T.p2[:], AF.Copy, 0.0, -TINY)
    k_eb = act(T.eb1[:], T.pa[:], AF.Copy, 64 * TINY, -TINY, k)

    k = act(T.rnt[:, 0:16], T.rtt[:, 0:16], AF.Copy, 0.0, -1.0, d_rt)
    k_rq = quant(T.rtq[:], T.rts[:], T.rtt[:], d_rt, k_z0)
    k_o1 = cp(T.to[:, 0:20], T.ti[:, 0:20], k_t1)
    k_nq = quant(T.rnq[:], T.rns[:], T.rnt[:], k, k_zn)
    kp0 = pickq(T.rpq[:, 0:128], T.rtq[:], T.to[:, 0:8], k_rq, k_o1)
    ks0 = picks(T.rps[:, 0:128], T.rts[:], T.to[:, 0:8], k_rq, k_o1)
    k_xq = quant(T.xq[:], T.xs[:], T.xt[:], d_x, k_x0)
    kp1 = pickq(T.rpq[:, 128:256], T.rnq[:], T.to[:, 8:16], k_nq)
    ks1 = picks(T.rps[:, 128:256], T.rns[:], T.to[:, 8:16], k_nq)
    kp2 = pickq(T.rpq[:, 256:320], T.rnq[:], T.to[:, 16:20])
    ks2 = picks(T.rps[:, 256:320], T.rns[:], T.to[:, 16:20])
    k_ng = ms(T.r2t[:, 24:512], 0.0)
    score = lambda j, a, first, *d: mm(bank(j, 192), T.rpq[:, a:a + 128], T.rps[:, a:a + 128], T.xq[:, 0:192], T.xs[:, 0:192], first, not first, *d)
    score(0, 0, True, kp0, ks0, k_xq)
    score(1, 0, True)
    dm = [score(0, 128, False, kp1, ks1)]
    score(2, 0, True)
    dm += [score(1, 160, False, kp2, ks2), score(2, 192, False)]
    two = [slice(0, 96), slice(96, 192)]
    kz = [act(T.z1[:, h], T.ps[:, h], AF.Sign, T.eb1[:], 1.0, dm[0], k_eb) for h in two]
    k_z1 = kz[1]
    k = act(T.csn[:], T.b16[:], AF.Identity, T.rf[:], -1.0, k_16, k_rf)
    k_cs = act(T.csp[:], T.csn[:], AF.Copy, 0.0, -1.0, k)
    kk = [tt(T.z2[:, h], T.ps[:, 512 + h.start:512 + h.stop], T.z1[:, h], OP.min, dm[1], k) for h, k in zip(two, kz)]
    kk = [tt(T.z3[:, h], T.ps[:, 1024 + h.start:1024 + h.stop], T.z2[:, h], OP.min, dm[2], k) for h, k in zip(two, kk)]
    k_d1 = kk[1]
    k = acc(T.jka[:, 384:576], T.z3[:], AF.Sign, T.tn1[:], 1.0, T.cno[:], k_d1)
    send(near, T.cnte[:, 0:1], T.cno[:], "ae", k)
    kk = [ts(T.mk[:, h], T.z3[:, h], T.th1[:], None, OP.is_gt, None, k, k_th) for h, k in zip(two, kk)]
    k = run(T.cum[:, 0:96], T.mk[:, 0:96], 128, 96, 0.0, kk[0])
    k_o2 = cp(T.to[:, 20:34], T.ti[:, 20:34], k_t2)
    k_cum = run(T.cum[:, 96:192], T.mk[:, 96:192], 128, 96, T.cum[:, 95:96], k, kk[1])
    for c in range(2):
        acc(T.jka[:, 192 * c:192 * c + 192], T.cum[:], AF.Sign, T.csn[:, c:c + 1], 1.0, T.cnt1[:, c:c + 1], k_cum, k_cs)
    k_a = act(T.cnt1[:, 5:6], T.cum[:, 191:192], AF.Copy, 192.0, -2.0)
    seg = lambda c: slice(192 * (c - 2) + 16 * c, 192 * (c - 1))
    kk = [ts(T.jkd[:, seg(c)], T.cum[:, 16 * c:192], T.csp[:, c:c + 1], 2.0, OP.is_gt, OP.mult, k_cum, k_cs) for c in (2, 3, 4)]
    for c in (2, 3, 4):
        k = run(T.jkf[:, seg(c)], T.jkd[:, seg(c)], 128, TOK - 16 * c, -192.0, kk[c - 2])
    k_c = cp(T.cnt1[:, 2:5], T.jkf[:, 191:576:192], k)
    pk, psc = {}, {}
    seq = order + [rank]
    col1 = {b: 6 * i for i, b in enumerate(seq)}
    off1 = lambda q, b: ts(T.off1[quad(q), col1[b]:col1[b] + 6], T.cnt1[quad(PI[b]), 0:6], -0.5, 96.0, OP.mult, OP.add, k_c, k_a)
    todo = [(q, b) for b in seq for q in range(N)]
    k_of = [off1(*todo[j]) for j in range(6)]
    for i, b in enumerate(seq):
        o, so = (T.sl1[:, 80 * i:80 * i + 80], T.ss1[:, 80 * i:80 * i + 80]) if b != rank else \
                (T.land1[:, 80 * b:80 * b + 80], T.lans1[:, 80 * b:80 * b + 80])
        pk[b] = pickq(o, T.xq[:, 0:194], T.off1[:, 6 * i:6 * i + 5], k_of[4 * i + 3])
        psc[b] = picks(so, T.xs[:, 0:194], T.off1[:, 6 * i:6 * i + 5], k_of[4 * i + 3])
        if b != rank:
            send(b, c8(T.land1[:, 80 * rank:80 * rank + 80]), c8(o), "arr%d" % rank, pk[b], k_lw)
            send(b, T.lans1[:, 80 * rank:80 * rank + 80], so, "arr%d" % rank, psc[b])
        k_of += [off1(*x) for x in todo[4 * i + 6:4 * i + 10]]
        if i == 2:
            k_r2q = quant(T.r2q[:], T.r2s[:], T.r2t[:], d_r2, k_ng)
            k = cp(T.offf[:], T.off1[:], k_of[-1])
    ozero = T.to[:, 28:29]
    k_z = pickq(T.land1[:, NX:XC], T.xq[:, 0:194], ozero, k_o2)
    k_mo = scan(T.mo[:], T.diag[:], T.offf[:], 0.0, OP.max, OP.min, k, k_dg)
    for b in order[1:]:
        send(b, T.msgi[:, 8 * rank:8 * rank + 2], T.mo[:, col1[b] + 4:col1[b] + 6], "am", k_mo)
    send(near, T.msgi[:, 8 * rank:8 * rank + 1], T.mo[:, 4:5], "an")

    k_wq = quant(T.wq[:], T.wsc[:], T.wt[:], d_w)
    k_r2p = pickq(T.r2p[:], T.r2q[:], T.to[:, 20:28], k_r2q)
    k_zs = picks(T.lans1[:, NX:XC], T.xs[:, 0:194], ozero, k_o2)
    k_r2s = picks(T.r2ps[:], T.r2s[:], T.to[:, 20:28], k_r2q)
    for s in range(N):
        ts(T.tri[:, 80 * s:80 * s + 80], T.i80[:], T.p96[:, s:s + 1], -3.0, OP.is_lt, OP.add, k_80)
    am, an = ("am", arrivals(far, 1)), ("an", arrivals([near], 1))
    zc = lambda s: slice(max(2 * s - 1, 0), min(2 * s + 1, 6))
    k_num = act(T.num[:], T.xt[:, 0:XC], AF.Copy, -1.0, 0.0)
    act(T.kid[:], T.p2[:], AF.Copy, -2.0, 0.0)
    for q in range(N):
        act(T.ib[quad(q), near:near + 1], T.cnte[quad(PI[rank]), 0:1], AF.Copy, (0.5 - TOK / 2) * K, -0.5 * K, ("ae", arrivals([near], 1)))
    k = act(T.ib[:, rank:rank + 1], T.mo[:, 23:24], AF.Copy, 0.5 * K, -K, k_mo)
    for s in (near, rank):
        act(T.zz[:, zc(s)], T.cz[:, zc(s)], AF.Relu, T.ib[:, s:s + 1], K, k, k_cz)
        ki0 = act(T.inv[:, 80 * s:80 * s + 80], T.i80[:], AF.Relu, T.ib[:, s:s + 1], K)

    arr = lambda s: ("arr%d" % s, arrivals([s], 2))
    home = (pk[rank], psc[rank])
    halves = [(0, NH, [0, 1]), (NH, NX + 2, [2, 3])]
    if rank >= 2:
        halves.reverse()
    H = lambda a, b: (T.hq[:, a:b], T.hs[:, a:b])
    f0, g0 = halves[0][0], halves[1][0]
    F, G = slice(f0, f0 + NH), slice(g0, g0 + NH)
    kE, kO = (0, 2) if f0 == 0 else (2, 0)

    def products(h):
        c0, c1, who = halves[h]
        deps = [arr(s) for s in who if s != rank] + list(home) + [k_z, k_zs, k_wq, k_d1, k_z1]
        return [mm(bank(4 * h + i, c1 - c0), T.wq[:, 128 * i:128 * i + 128], T.wsc[:, 128 * i:128 * i + 128], T.land1[:, c0:c1], T.lans1[:, c0:c1], True, True, *deps) for i in range(4)]

    def tile(h, W):
        c0, c1, who = halves[h]
        hv = lambda i: T.hb[:, 4 * c0 + i:4 * c1:4]
        k0 = act(hv(0), bank(4 * h, c1 - c0), AF.Relu, 0.0, 0.0625, W[0])
        k1 = ts(hv(1), bank(4 * h + 1, c1 - c0), 0.0, 0.0625, OP.max, OP.mult, W[1])
        k2 = act(hv(2), bank(4 * h + 2, c1 - c0), AF.Relu, 0.0, 0.0625, W[2])
        k3 = ts(hv(3), bank(4 * h + 3, c1 - c0), 0.0, 0.0625, OP.max, OP.mult, W[3])
        return quant(T.hq[:, c0:c1], T.hs[:, c0:c1], T.hb[:, 4 * c0:4 * c1], k0, k1, k2, k3)

    eblock = lambda b, k, *d: mm(bank(b, 128), *H(96 * k, 96 * k + 128), T.r2q[:], T.r2s[:], True, True, *d)
    keep = lambda b, k, *d: act(T.es[:, 8 * k:8 * k + 5], bank(b, 5), AF.Copy, 0.0, 1.0, *d)
    en = lambda k: T.es[:, 8 * k + E4:8 * k + E4 + 1]
    W0 = products(0)
    kq0 = tile(0, W0)
    W1 = products(1)
    ea = mm(bank(0, NH), T.r2p[:], T.r2ps[:], *H(f0, f0 + NH), True, True, kq0, k_r2p, k_r2s)
    eE = eblock(1, kE)
    kq1 = tile(1, W1)
    k_ef = tt(T.em[:, F], bank(0, NH), T.inv[:, F], OP.add, ea, ki0)
    for s in range(N):
        src = T.msgi[0:80, 8 * s:8 * s + 1] if s != rank else T.mo[0:80, 22:23]
        d_nb = dma("s", "dnb", T.nb[0:1, 80 * s:80 * s + 80], src, am, an, k_mo)
    d_vx = dma("s", "dvx", T.vxt[:], T.vx[:])
    d_vh = dma("s", "dvh", T.vht[:], T.vh[:])

    eb = mm(bank(4, NH), T.r2p[:], T.r2ps[:], *H(g0, g0 + NH), True, True, kq1)
    eM = eblock(5, 1)
    eO = eblock(6, kO)
    dg = lambda k: slice(96 * k, 96 * k + 128)
    o_ = {kE: 0, kO: 192}
    sign = lambda a, m, k, *d: act(T.sd[:, a:a + m.stop - m.start], T.em[:, m], AF.Sign, en(k), -1.0, *d)
    k = act(T.ib[:, far[0]:far[0] + 2], T.msgi[:, 8 * far[0] + 1:8 * far[0] + 10:8], AF.Copy, 0.5 * K, -K, am)
    k_sE = keep(1, kE, eE)
    for s in far:
        k_zz = act(T.zz[:, zc(s)], T.cz[:, zc(s)], AF.Relu, T.ib[:, s:s + 1], K, k)
    for s in far:
        ki = act(T.inv[:, 80 * s:80 * s + 80], T.i80[:], AF.Relu, T.ib[:, s:s + 1], K)
    k_gE = sign(0, dg(kE), kE, k_sE, k_ef)
    k_sM = keep(5, 1, eM)
    k_sO = keep(6, kO, eO)
    k_pr = scan(T.pres[:], T.zr[:], T.zz[:], 0.0, OP.max, OP.subtract, k_zz)
    k_em = tt(T.em[:, G], bank(4, NH), T.inv[:, G], OP.add, eb, ki)
    k_gF = sign(256 + f0, F, 1, k_sM)
    k_gG = sign(256 + g0, G, 1, k_em)
    k_gO = sign(128, dg(kO), kO, k_sO)

    def rest(k, *d):
        a, b, o = (128, NX, OP.is_lt) if k == 0 else (0, 192, OP.is_le)
        return ts(T.jk2[:, o_[k]:o_[k] + 192], T.em[:, a:b], en(k), -2.0, o, OP.mult, *d)

    mix = lambda a, b, c, *d: elem(T.rd[:, a:b], T.sd[:, a:b], T.tri[:, c:c + b - a], OP.add, *d)
    count = lambda a, b, k, *d: acc(T.jkb[:, a:b], T.rd[:, a:b], AF.Sign, T.h25[:], 1.0, T.lt[:, k:k + 1], *d)
    room = lambda k, *d: run(T.jkc[:, o_[k]:o_[k] + 192], T.jk2[:, o_[k]:o_[k] + 192], 128, 192, 2.0 * DF - 1 - 128, *d)
    wide = lambda k, *d: act(T.ck[:, 32 * k:32 * k + 32], T.rtt[:, 32:64], AF.Identity, T.jkc[:, o_[k] + 191:o_[k] + 192], 1.0, *d)
    col = lambda i: T.es[:, srt[i]:24:8]
    k_mE = mix(0, 128, 96, k_gE)
    k1 = rest(kE, k_em)
    k3 = rest(kO, k_sO)
    mix(256 + f0, 256 + f0 + NH, f0, k_gF)
    k_mM = mix(256 + g0, 256 + g0 + NH, g0, k_gG)
    tt(T.ka[:], col(1), col(0), OP.is_gt)
    k2 = tt(T.km[:], col(1), col(0), OP.max)
    k_mO = mix(128, 256, 96, k_gO)
    count(0, 128, kE, k_mE)
    count(256, 576, 1, k_mM)
    count(128, 256, kO, k_mO)
    k2 = tt(T.kc[:], col(2), T.km[:], OP.is_gt, k2)
    k1 = room(kE, k1)
    tt(T.ku[:], T.ka[:], T.kc[:], OP.max, k2)
    k2 = tt(T.kv[:], T.kc[:], T.pres[:, 1:6:2], OP.add, k_pr)
    k = room(kO, k3)
    kl = wide(kE, k1)
    k1 = wide(kO, k)
    k2 = tt(T.key[:], T.ku[:], T.kv[:], OP.add, k2)
    hand = lambda k, *d: ts(T.bc[:, 32 * k:32 * k + 32], T.ck[:, 32 * k:32 * k + 32], T.lt[:, k:k + 1], T.key[:, k:k + 1], OP.is_gt, OP.mult, *d)
    hand(1, k2, kl)
    hand(kE)
    k = hand(kO, k1)
    for q in range(N):
        k1 = turn(T.mk3[0:32, q:9:3, :], T.bc[quad(q), :], k) if q < 3 else turn(T.mk3[0:32, 9, :], T.bc[quad(q), 64:96])
    k2 = act(T.mk2[quad(2), :], T.mk3[0:32, :, :], AF.Relu, T.kid[0:32, :], 1.0, k1)
    for i in range(2):
        k = ts(T.mk2[quad(i), :], T.mk3[0:32, :, :], i + 1.0, None, OP.is_equal, None, k1)
    Q = slice(0, 96)
    k_c2 = run(T.cum2[Q, :], T.mk2[Q, :], 96, NX, 0.0, k, k2)
    ka = acc(T.jkb[Q, 576:896], T.cum2[Q, :], AF.Sign, T.csn[Q, 0:1], 1.0, T.cnt2[Q, 0:1], k_c2)
    k0 = ts(T.jke[Q, 16:168], T.cum2[Q, 16:168], T.csp[Q, 1:2], 2.0, OP.is_gt, OP.mult, k_c2)
    k1 = ts(T.jke[Q, 168:NX], T.cum2[Q, 168:NX], T.csp[Q, 1:2], 2.0, OP.is_gt, OP.mult)
    run(T.jke[Q, 336:488], T.jke[Q, 16:168], 96, 152, -1.0 * NX, k0)
    k = run(T.jke[Q, 488:640], T.jke[Q, 168:NX], 96, 152, 0.0, k1)
    kc = tt(T.cnt2[Q, 1:2], T.jke[Q, 487:488], T.jke[Q, 639:640], OP.add, k)
    off2 = lambda q, i: ts(T.off2[quad(q), 2 * i:2 * i + 2], T.cnt2[quad(srt.index(order[i])), :], -0.5, NX / 2.0, OP.mult, OP.add, kc, ka)
    todo = [(q, i) for i in range(3) for q in range(N)]
    k_of = [off2(*todo[j]) for j in range(6)]
    for i, b in enumerate(order):
        o, lst, ko = 64 * i, T.off2[:, 2 * i:2 * i + 2], k_of[4 * i + 3]
        pickq(T.sl2[:, o:o + 32], T.land1[:], lst, ko)
        kk = pickq(T.sl2[:, o + 32:o + 64], T.hq[:, 0:NX + 2], lst)
        picks(T.ss2[:, o:o + 32], T.lans1[:], lst, ko)
        ks = picks(T.ss2[:, o + 32:o + 64], T.hs[:, 0:NX + 2], lst)
        d = slice(96 + o, 160 + o)
        send(b, c8(T.land2[:, d]), c8(T.sl2[:, o:o + 64]), "ab%d" % i, kk)
        send(b, T.lans2[:, d], T.ss2[:, o:o + 64], "ab%d" % i, ks)
        k_of += [off2(*x) for x in todo[4 * i + 6:4 * i + 10]]
        if i < 2:
            for s in (2 * i, 2 * i + 1):
                k_n = act(T.num[0:1, 80 * s:80 * s + 80], T.nb[0:1, 80 * s:80 * s + 80], AF.Copy, float(TOK * s), 1.0, d_nb, k_num)
    kw = op("a", lambda e: e.activation(T.wg[:], T.num[:].indirect(T.off2[:]), AF.Copy), k_n)
    kw = turn(T.wtr[:], T.wg[:], kw)
    for i, b in enumerate(order):
        send(b, T.lwho[:, rank:rank + 1], T.wtr[:, 32 * i:32 * i + 1], "aw", kw)

    k_z2 = pickq(T.land2[:, 0:96], T.xq[:, 0:194], T.to[:, 28:34])
    k_z2s = picks(T.lans2[:, 0:96], T.xs[:, 0:194], T.to[:, 28:34])
    k_vx = quant(T.vxq[:], T.vxs[:], T.vxt[:], d_vx)
    k_vh = quant(T.vhq[:], T.vhs[:], T.vht[:], d_vh)
    for j in range(3):
        k_ofin = ts(T.ofin[:, 2 * j:2 * j + 2], T.csp[:, 0:2], 128.0 + 64 * j - 0.5, None, OP.add, None)
    ms(T.ys[:, CB * rank:CB * rank + CB], 0.0)
    pickq(T.fin[:, CB * rank:CB * rank + CB], T.xq[:, 0:194], T.to[:, 28:30])
    picks(T.fins[:, CB * rank:CB * rank + CB], T.xs[:, 0:194], T.to[:, 28:30])

    for j, a in enumerate(order):
        ab, o, pl = ("ab%d" % j, arrivals([a], 2)), 64 * j, slice(CB * a, CB * a + CB)
        mm(bank(j, 128), T.vxq[:], T.vxs[:], T.land2[:, o:o + 128], T.lans2[:, o:o + 128], True, False, ab, k_vx, k_vh, k_z2s)
        ty = mm(bank(j, 128), T.vhq[:], T.vhs[:], T.land2[:, o + 32:o + 160], T.lans2[:, o + 32:o + 160], False, True)
        kfs = picks(T.fins[:, pl], T.lans2[:, 0:o + 160], T.ofin[:, 2 * j:2 * j + 2], ab, k_ofin, k_z2s)
        kf = pickq(T.fin[:, pl], T.land2[:, 0:o + 160], T.ofin[:, 2 * j:2 * j + 2], ab, k_ofin)
        ky = cp(T.ys[:, pl], T.ps[:, 512 * j + 96:512 * j + 128], ty)
    dma("s", "dout", T.oc[:], c8(T.fin[:]), kf)
    for k in range(4):
        dma("s" if k < 2 else "a", "dout", T.osc[4 * k:4 * k + 4, :], T.fins[32 * k:32 * k + 4, :], kfs)
    dma("a", "dout", T.y[:], T.ys[:], ky)
    kw = turn(T.whot[:], T.lwho[:], ("aw", arrivals(others, 1)), k_lw)
    dma("s", "dout", T.who[:], T.whot[0:4, :], kw)
    wait("g", [(s, n) for s, n in tot.items()])
